import numpy as np
import ml_dtypes


def mxq(x, axis, fmt="e4m3"):
    dtype, down = {"e4m3": (ml_dtypes.float8_e4m3fn, 7), "e5m2": (ml_dtypes.float8_e5m2, 14)}[fmt]
    v = np.moveaxis(np.asarray(x, np.float32).astype(ml_dtypes.bfloat16).astype(np.float64), axis, -1)
    blocks = v.reshape(v.shape[:-1] + (-1, 32))
    amax = np.abs(blocks).max(-1, keepdims=True)
    byte = np.maximum(np.where(amax > 0, np.frexp(amax)[1] - 1 + 127, 0) - down, 1)
    scale = np.exp2(byte - 127.0)
    codes = (blocks / scale).astype(np.float32).astype(dtype).astype(np.float64)
    return np.moveaxis((codes * scale).reshape(v.shape), -1, axis)


WIDE = False


def mx_kscale(k):
    if not WIDE:
        return np.ones(k)
    levels = np.array([10, -10, 5, -5, 0])
    if k % 512:
        return np.exp2(np.random.permutation(np.resize(levels, k // 32))).repeat(32)
    a = np.empty((k // 512, 16))
    for p in range(k // 512):
        a[p, :8] = np.random.permutation(np.resize(levels, 8))
        for g in range(8):
            far = levels[np.abs(levels - a[p, g]) >= 10]
            a[p, g + 8] = far[np.random.randint(len(far))]
    return np.exp2(a.ravel()).repeat(32)


def f64(x):
    return np.asarray(x).astype(np.float64)


def striped(idx):
    return np.tile(idx.reshape(-1, 16).T, (8, 1)).astype(np.uint16)


def unstriped(offs):
    return offs[:16].T.reshape(-1).astype(np.int64)


E2M1 = np.array([0.0, 0.5, 1.0, 1.5, 2.0, 3.0, 4.0, 6.0, -0.0, -0.5, -1.0, -1.5, -2.0, -3.0, -4.0, -6.0])


def pack_weight(w, fmt):
    k, n = w.shape
    w = f64(np.asarray(w, np.float32).astype(ml_dtypes.bfloat16)).reshape(k // 32, 32, n)
    amax = np.abs(w).max(1)
    if fmt == "e4m3":
        byte = np.frexp(amax)[1] - 1 + 127 - 7
    else:
        mant, ex = np.frexp(amax / 6.0)
        byte = np.where(mant > 0.5, ex, ex - 1) + 127
    byte = np.clip(np.where(amax > 0, byte, 1), 1, 254)
    scaled = (w * np.exp2(127.0 - byte)[:, None, :]).reshape(k, n).astype(np.float32)
    by_word = np.ascontiguousarray(scaled.reshape(k // 512, 128, 4, n).transpose(0, 1, 3, 2))
    if fmt == "e4m3":
        words = by_word.astype(ml_dtypes.float8_e4m3fn).view(np.uint8)
    else:
        c = by_word.astype(ml_dtypes.float4_e2m1fn).view(np.uint8) & 0xF
        words = (c[..., 0::2] | (c[..., 1::2] << 4)).reshape(k // 512, 128, 2 * n)
    return np.ascontiguousarray(words), np.ascontiguousarray(byte.astype(np.uint8).reshape(k // 512, 16, n))


def unpack_weight(words, scales, fmt):
    g, _, n = scales.shape
    words = np.ascontiguousarray(words).reshape(g, 128, n, -1)
    if fmt == "e4m3":
        vals = words.view(ml_dtypes.float8_e4m3fn).astype(np.float64)
    else:
        nib = np.empty((g, 128, n, 4), np.uint8)
        nib[..., 0::2] = words & 0xF
        nib[..., 1::2] = words >> 4
        vals = E2M1[nib]
    vals = vals * np.repeat(np.exp2(scales.astype(np.float64) - 127.0), 8, axis=1)[..., None]
    return vals.transpose(0, 1, 3, 2).reshape(g * 512, n)


def gelu(v):
    return 0.5 * v * (1.0 + np.tanh(np.sqrt(2.0 / np.pi) * (v + 0.044715 * v**3)))


def pack_table4(v):
    words, scales = pack_weight(v, "e2m1")
    g, t = words.shape[0] // 2, v.shape[1]
    words = words.reshape(g, 2, 128, t, 2).transpose(0, 2, 3, 1, 4)
    return np.concatenate([words.reshape(g, -1), scales.reshape(g, -1)], axis=1)


def unpack_table4(tab):
    g, t = tab.shape[0], tab.shape[1] // 544
    words = tab[:, :512 * t].reshape(g, 128, t, 2, 2).transpose(0, 3, 1, 2, 4).reshape(2 * g, 128, 2 * t)
    return unpack_weight(words, tab[:, 512 * t:].reshape(2 * g, 16, t), "e2m1")


K, T, S, H, N = 2048, 4096, 1024, 1024, 256


def setup_inputs():
    n = np.random.standard_normal
    s = mx_kscale(K)[:, None]
    u = mx_kscale(H)[:, None]
    tab = pack_table4(n((K, T)) * s)
    offs = striped(np.random.permutation(T)[:S])
    w1 = (n((K, H)) / np.sqrt(K) / s).astype(np.float32)
    centre = (0.7 * n(H)).astype(np.float32)
    gain = (np.exp(0.3 * n(H)) * u[:, 0]).astype(np.float32)
    w2_words, w2_scales = pack_weight(n((H, N)) / np.sqrt(H) / u, "e2m1")
    return {"tab": tab, "offs": offs, "w1": w1, "centre": centre, "gain": gain,
            "w2_words": w2_words, "w2_scales": w2_scales}


def reference(tab, offs, w1, centre, gain, w2_words, w2_scales):
    v = unpack_table4(tab)[:, unstriped(offs)]
    w1q = mxq(f64(w1), 0, "e4m3")
    p = w1q.T @ v
    d = p - f64(centre)[:, None]
    h = f64(gain)[:, None] * np.exp(-np.square(d))
    hq = mxq(h, 0, "e4m3")
    w2 = unpack_weight(w2_words, w2_scales, "e2m1")
    return w2.T @ hq

@@ -1,0 +1,229 @@
+from contextlib import ExitStack
+
+import concourse.mybir as mybir
+
+K, T, S, H, N = 2048, 4096, 1024, 1024, 256
+FLOPS = 2 * K * H * S + 2 * H * N * S
+
+F32 = mybir.dt.float32
+BF16 = mybir.dt.bfloat16
+I32 = mybir.dt.int32
+U32 = mybir.dt.uint32
+U16 = mybir.dt.uint16
+U8 = mybir.dt.uint8
+FP8X4 = mybir.dt.float8_e4m3fn_x4
+FP4X4 = mybir.dt.float4_e2m1fn_x4
+ACT = mybir.ActivationFunctionType
+MULT = mybir.AluOpType.mult
+
+P = 128
+PACK = 4
+PASS = P * PACK
+BANK = 512
+K_PASSES = K // PASS
+R_PASSES = H // PASS
+LAST_CHUNKS = (256, 128, 128)
+
+
+def tile_list_redshift_gaussian_bumps_kernel(tc, tab, offs, w1, centre, gain, w2_words, w2_scales, out):
+    nc = tc.nc
+    with ExitStack() as ctx:
+        keep = ctx.enter_context(tc.tile_pool(name="keep", bufs=1))
+        ring = ctx.enter_context(tc.tile_pool(name="ring", bufs=2))
+        psum = ctx.enter_context(tc.psum_pool(name="psum", bufs=8))
+
+        offsets = keep.tile([P, S // 16], U16, name="offsets")
+        tab_words = [keep.tile([P, T], U32, name="tab_words%d" % m) for m in range(2)]
+        tab_scales = keep.tile([P, T], U8, name="tab_scales")
+        w1_raw = {}
+        for b in range(R_PASSES):
+            for a in range(K_PASSES):
+                w1_raw[b, a] = keep.tile([P, PACK, PASS], F32, name="w1_raw%d%d" % (b, a))
+        centre_sb = keep.tile([P, R_PASSES, PACK], F32, name="centre_sb")
+        gain_sb = keep.tile([P, R_PASSES, PACK], F32, name="gain_sb")
+        w2w = keep.tile([P, R_PASSES, 2 * N], U8, name="w2w", align_bytes=64)
+        w2s = keep.tile([P, R_PASSES, N], U8, name="w2s", align_bytes=64)
+        v_scales = keep.tile([P, K_PASSES, S], U8, name="v_scales", align_bytes=64)
+        warm = keep.tile([P, 1], F32, name="warm")
+
+        def load_w1(b, a):
+            nc.sync.dma_start(
+                out=w1_raw[b, a][:],
+                in_=w1[a * PASS:(a + 1) * PASS, b * PASS:(b + 1) * PASS].rearrange("(p j) c -> p j c", j=PACK))
+
+        def load_words(m):
+            nc.sync.dma_start(
+                out=tab_words[m][:].bitcast(I32),
+                in_=tab[m, 0:PASS * T].rearrange("(p x) -> p x", p=P).bitcast(I32))
+
+        nc.vector.memset(tab_scales[64:128, :].bitcast(I32), 0)
+        nc.vector.memset(v_scales[:].rearrange("p a j -> p (a j)").bitcast(I32), 0)
+        nc.vector.memset(w2s[:].rearrange("p a c -> p (a c)").bitcast(I32), 0)
+        nc.vector.memset(warm[:], 0.0)
+        nc.scalar.activation(out=warm[:], in_=warm[:], func=ACT.Exp)
+
+        load_w1(0, 0)
+        nc.sync.dma_start(offsets[:], offs)
+        for m in range(2):
+            nc.sync.dma_start(
+                out=tab_scales[m:64:2, :].bitcast(I32),
+                in_=tab[m, PASS * T:].rearrange("(h q t) -> q h t", h=2, q=16).bitcast(I32))
+        load_words(0)
+        nc.sync.dma_start(out=centre_sb[:], in_=centre.rearrange("(b p t) -> p b t", p=P, t=PACK))
+        nc.sync.dma_start(out=gain_sb[:], in_=gain.rearrange("(b p t) -> p b t", p=P, t=PACK))
+        load_w1(0, 1)
+        load_words(1)
+        load_w1(0, 2)
+        load_w1(0, 3)
+        for a in range(K_PASSES):
+            load_w1(1, a)
+        nc.sync.dma_start(out=w2w[:].bitcast(I32), in_=w2_words.rearrange("a p c -> p a c").bitcast(I32))
+        for q in range(4):
+            nc.sync.dma_start(
+                out=w2s[32 * q:32 * q + 4, :, :].bitcast(I32),
+                in_=w2_scales[:, 4 * q:4 * q + 4, :].rearrange("a r c -> r a c").bitcast(I32))
+
+        picked_scales = keep.tile([P, S], U8, name="picked_scales")
+        nc.vector.tensor_copy(picked_scales[:], tab_scales[:].indirect(offsets[:]))
+        for q in range(4):
+            nc.gpsimd.dma_start(
+                out=v_scales[32 * q:32 * q + 4, :, :].bitcast(I32),
+                in_=picked_scales[16 * q:16 * q + 16, :].bitcast(I32))
+
+        v_words = {}
+
+        def pick_words(m):
+            picked = keep.tile([P, S], U32, name="picked%d" % m)
+            nc.vector.tensor_copy(picked[:], tab_words[m][:].indirect(offsets[:]))
+            parted = keep.tile([P, 2, S], U16, name="parted%d" % m, align_bytes=64)
+            nc.vector.tensor_copy(parted[:], picked[:].bitcast(U16).rearrange("p (j h) -> p h j", h=2))
+            v_words[m] = parted
+
+        w1_codes = {}
+        w1_scales = {}
+        w1_grouped = {}
+
+        def group_w1(b, a, cut):
+            grouped = ring.tile([P, PACK, P, PACK], BF16, name="w1_grouped", align_bytes=64, bufs=3)
+            dst = grouped[:].rearrange("p t m j -> p m j t")
+            src = w1_raw[b, a][:].rearrange("p j (m t) -> p m j t", t=PACK)
+            if cut > 0:
+                nc.scalar.copy(out=dst[:, 0:cut], in_=src[:, 0:cut])
+            if cut < P:
+                nc.vector.tensor_copy(out=dst[:, cut:P], in_=src[:, cut:P])
+            w1_grouped[b, a] = grouped
+
+        def quantise_w1(b, a):
+            codes = keep.tile([P, PASS], U32, name="w1_codes%d%d" % (b, a), align_bytes=64)
+            scales = keep.tile([P, PASS], U8, name="w1_scales%d%d" % (b, a), align_bytes=64)
+            nc.vector.quantize_mx(out=codes[:].bitcast(FP8X4), scales=scales[:],
+                                  in_=w1_grouped[b, a][:].rearrange("p t m j -> p (t m j)"))
+            w1_codes[b, a] = codes
+            w1_scales[b, a] = scales
+
+        banks = {}
+
+        def project(b, steps):
+            for a, half in steps:
+                m, h = divmod(a, 2)
+                cols = slice(half * BANK, (half + 1) * BANK)
+                for t in range(PACK):
+                    if a == 0:
+                        banks[b, half, t] = psum.tile([P, BANK], F32, name="bank")
+                    nc.tensor.matmul_mx(
+                        out=banks[b, half, t][:],
+                        lhsT=w1_codes[b, a][:, t * P:(t + 1) * P].bitcast(FP8X4),
+                        lhsT_scale=w1_scales[b, a][:, t * P:(t + 1) * P],
+                        rhs=v_words[m][:, h, cols].bitcast(FP4X4),
+                        rhs_scale=v_scales[:, 2 * h + m, cols],
+                        start=(a == 0), stop=(a == K_PASSES - 1))
+
+        squares = {}
+
+        def square(b, half):
+            sq = ring.tile([P, PACK, BANK], F32, name="sq")
+            for t in range(PACK):
+                nc.scalar.activation(out=sq[:, t, :], in_=banks[b, half, t][:], func=ACT.Square,
+                                     bias=centre_sb[:, b, t:t + 1], scale=-1.0)
+            squares[b, half] = sq
+
+        h_codes = {}
+        h_scales = {}
+
+        def bump(b, j0, width):
+            half, c0 = divmod(j0, BANK)
+            bell = ring.tile([P, PACK, width], F32, name="bell", bufs=3)
+            nc.scalar.activation(out=bell[:], in_=squares[b, half][:, :, c0:c0 + width], func=ACT.Exp, scale=-1.0)
+            hb = ring.tile([P, width, PACK], BF16, name="hb", align_bytes=64)
+            nc.vector.tensor_tensor(
+                out=hb[:].rearrange("p (c i) t -> p c t i", i=4),
+                in0=bell[:].rearrange("p t (c i) -> p c t i", i=4),
+                in1=gain_sb[:, b, :].unsqueeze(1).unsqueeze(3).to_broadcast([P, width // 4, PACK, 4]),
+                op=MULT)
+            codes = keep.tile([P, width], U32, name="h_codes%d_%d" % (b, j0), align_bytes=64)
+            scales = keep.tile([P, width], U8, name="h_scales%d_%d" % (b, j0), align_bytes=64)
+            nc.vector.quantize_mx(out=codes[:].bitcast(FP8X4), scales=scales[:],
+                                  in_=hb[:].rearrange("p j t -> p (j t)"))
+            for j in range(j0, j0 + width, P):
+                h_codes[b, j] = (codes, j - j0)
+                h_scales[b, j] = (scales, j - j0)
+
+        def read_out(dst, u, j0, width):
+            for b in range(R_PASSES):
+                codes, c0 = h_codes[b, j0]
+                scales, c0 = h_scales[b, j0]
+                nc.tensor.matmul_mx(
+                    out=dst,
+                    lhsT=w2w[:, b, 2 * P * u:2 * P * (u + 1)].bitcast(FP4X4),
+                    lhsT_scale=w2s[:, b, P * u:P * (u + 1)],
+                    rhs=codes[:, c0:c0 + width].bitcast(FP8X4),
+                    rhs_scale=scales[:, c0:c0 + width],
+                    start=(b == 0), stop=(b == R_PASSES - 1))
+
+        out_rows = out.rearrange("(u p) j -> p u j", p=P)
+
+        group_w1(0, 0, P)
+        quantise_w1(0, 0)
+        pick_words(0)
+        group_w1(0, 1, P)
+        quantise_w1(0, 1)
+        pick_words(1)
+        group_w1(0, 2, P)
+        group_w1(0, 3, 0)
+        quantise_w1(0, 2)
+        quantise_w1(0, 3)
+        project(0, [(0, 0), (0, 1), (1, 0), (1, 1), (2, 0), (3, 0), (2, 1), (3, 1)])
+        square(0, 0)
+        for a in range(K_PASSES):
+            group_w1(1, a, 0)
+            quantise_w1(1, a)
+        bump(0, 0, BANK)
+        square(0, 1)
+        bump(0, BANK, BANK)
+        project(1, [(a, half) for half in range(2) for a in range(K_PASSES)])
+        square(1, 0)
+        bump(1, 0, BANK)
+        first = []
+        for u in range(2):
+            acc = psum.tile([P, BANK], F32, name="bank")
+            read_out(acc[:], u, 0, BANK)
+            first.append(acc)
+        square(1, 1)
+        j0 = BANK
+        late = []
+        for width in LAST_CHUNKS:
+            bump(1, j0, width)
+            acc = psum.tile([P, BANK], F32, name="bank")
+            for u in range(2):
+                for c in range(0, width, P):
+                    read_out(acc[:, u * width + c:u * width + c + P], u, j0 + c, P)
+            late.append((acc, j0, width))
+            j0 += width
+        for u in range(2):
+            staged = keep.tile([P, BANK], F32, name="staged%d" % u)
+            nc.scalar.copy(out=staged[:], in_=first[u][:])
+            nc.sync.dma_start(out=out_rows[:, u, 0:BANK], in_=staged[:])
+        for acc, j0, width in late:
+            staged = keep.tile([P, 2, width], F32, name="staged_late%d" % j0)
+            nc.scalar.copy(out=staged[:].rearrange("p u j -> p (u j)"), in_=acc[:, 0:2 * width])
+            nc.sync.dma_start(out=out_rows[:, :, j0:j0 + width], in_=staged[:])

@@ -14,7 +14,7 @@ U8 = mybir.dt.uint8
 FP8X4 = mybir.dt.float8_e4m3fn_x4
 FP4X4 = mybir.dt.float4_e2m1fn_x4
 ACT = mybir.ActivationFunctionType
-MULT = mybir.AluOpType.mult
+ALU = mybir.AluOpType
 
 P = 128
 PACK = 4
@@ -22,7 +22,6 @@ PASS = P * PACK
 BANK = 512
 K_PASSES = K // PASS
 R_PASSES = H // PASS
-LAST_CHUNKS = (256, 128, 128)
 
 
 def tile_list_redshift_gaussian_bumps_kernel(tc, tab, offs, w1, centre, gain, w2_words, w2_scales, out):
@@ -33,62 +32,36 @@ def tile_list_redshift_gaussian_bumps_kernel(tc, tab, offs, w1, centre, gain, w2
         psum = ctx.enter_context(tc.psum_pool(name="psum", bufs=8))
 
         offsets = keep.tile([P, S // 16], U16, name="offsets")
-        tab_words = [keep.tile([P, T], U32, name="tab_words%d" % m) for m in range(2)]
-        tab_scales = keep.tile([P, T], U8, name="tab_scales")
-        w1_raw = {}
-        for b in range(R_PASSES):
-            for a in range(K_PASSES):
-                w1_raw[b, a] = keep.tile([P, PACK, PASS], F32, name="w1_raw%d%d" % (b, a))
+        tab_scales = keep.tile([P, T], U8, name="tab_scales", tag="area_b")
         centre_sb = keep.tile([P, R_PASSES, PACK], F32, name="centre_sb")
         gain_sb = keep.tile([P, R_PASSES, PACK], F32, name="gain_sb")
         w2w = keep.tile([P, R_PASSES, 2 * N], U8, name="w2w", align_bytes=64)
         w2s = keep.tile([P, R_PASSES, N], U8, name="w2s", align_bytes=64)
-        v_scales = keep.tile([P, K_PASSES, S], U8, name="v_scales", align_bytes=64)
+        v_scales = [keep.tile([P, 2, S], U8, name="v_scales%d" % m, align_bytes=64) for m in range(2)]
         warm = keep.tile([P, 1], F32, name="warm")
+        picked_scales = keep.tile([P, S], U8, name="picked_scales")
+        tab_words = {}
+        w1_raw = {}
 
-        def load_w1(b, a):
-            nc.sync.dma_start(
-                out=w1_raw[b, a][:],
-                in_=w1[a * PASS:(a + 1) * PASS, b * PASS:(b + 1) * PASS].rearrange("(p j) c -> p j c", j=PACK))
+        def load_w1(tag, pieces):
+            raw = keep.tile([P, len(pieces), PACK, PASS], F32, name="w1_raw", tag=tag)
+            for i, (b, a) in enumerate(pieces):
+                w1_raw[b, a] = raw[:, i]
+                nc.sync.dma_start(
+                    out=w1_raw[b, a],
+                    in_=w1[a * PASS:(a + 1) * PASS, b * PASS:(b + 1) * PASS].rearrange("(p j) c -> p j c", j=PACK))
 
-        def load_words(m):
+        def load_words(tag, m):
+            tab_words[m] = keep.tile([P, T], U32, name="tab_words", tag=tag)
             nc.sync.dma_start(
                 out=tab_words[m][:].bitcast(I32),
                 in_=tab[m, 0:PASS * T].rearrange("(p x) -> p x", p=P).bitcast(I32))
 
-        nc.vector.memset(tab_scales[64:128, :].bitcast(I32), 0)
-        nc.vector.memset(v_scales[:].rearrange("p a j -> p (a j)").bitcast(I32), 0)
-        nc.vector.memset(w2s[:].rearrange("p a c -> p (a c)").bitcast(I32), 0)
-        nc.vector.memset(warm[:], 0.0)
-        nc.scalar.activation(out=warm[:], in_=warm[:], func=ACT.Exp)
-
-        load_w1(0, 0)
-        nc.sync.dma_start(offsets[:], offs)
-        for m in range(2):
-            nc.sync.dma_start(
-                out=tab_scales[m:64:2, :].bitcast(I32),
-                in_=tab[m, PASS * T:].rearrange("(h q t) -> q h t", h=2, q=16).bitcast(I32))
-        load_words(0)
-        nc.sync.dma_start(out=centre_sb[:], in_=centre.rearrange("(b p t) -> p b t", p=P, t=PACK))
-        nc.sync.dma_start(out=gain_sb[:], in_=gain.rearrange("(b p t) -> p b t", p=P, t=PACK))
-        load_w1(0, 1)
-        load_words(1)
-        load_w1(0, 2)
-        load_w1(0, 3)
-        for a in range(K_PASSES):
-            load_w1(1, a)
-        nc.sync.dma_start(out=w2w[:].bitcast(I32), in_=w2_words.rearrange("a p c -> p a c").bitcast(I32))
-        for q in range(4):
-            nc.sync.dma_start(
-                out=w2s[32 * q:32 * q + 4, :, :].bitcast(I32),
-                in_=w2_scales[:, 4 * q:4 * q + 4, :].rearrange("a r c -> r a c").bitcast(I32))
-
-        picked_scales = keep.tile([P, S], U8, name="picked_scales")
-        nc.vector.tensor_copy(picked_scales[:], tab_scales[:].indirect(offsets[:]))
-        for q in range(4):
-            nc.gpsimd.dma_start(
-                out=v_scales[32 * q:32 * q + 4, :, :].bitcast(I32),
-                in_=picked_scales[16 * q:16 * q + 16, :].bitcast(I32))
+        def place_scales(m):
+            for q in range(4):
+                nc.sync.dma_start(
+                    out=v_scales[m][32 * q:32 * q + 4, :, :].bitcast(I32),
+                    in_=picked_scales[32 * m + 8 * q:32 * m + 8 * q + 8, :].bitcast(I32))
 
         v_words = {}
 
@@ -99,79 +72,85 @@ def tile_list_redshift_gaussian_bumps_kernel(tc, tab, offs, w1, centre, gain, w2
             nc.vector.tensor_copy(parted[:], picked[:].bitcast(U16).rearrange("p (j h) -> p h j", h=2))
             v_words[m] = parted
 
-        w1_codes = {}
-        w1_scales = {}
         w1_grouped = {}
+        w1_q = {}
 
-        def group_w1(b, a, cut):
-            grouped = ring.tile([P, PACK, P, PACK], BF16, name="w1_grouped", align_bytes=64, bufs=3)
+        def group_w1(b, a, t0, t1, on_scalar):
+            grouped = ring.tile([P, t1 - t0, P, PACK], BF16, name="w1_grouped", align_bytes=64, bufs=4)
             dst = grouped[:].rearrange("p t m j -> p m j t")
-            src = w1_raw[b, a][:].rearrange("p j (m t) -> p m j t", t=PACK)
-            if cut > 0:
-                nc.scalar.copy(out=dst[:, 0:cut], in_=src[:, 0:cut])
-            if cut < P:
-                nc.vector.tensor_copy(out=dst[:, cut:P], in_=src[:, cut:P])
-            w1_grouped[b, a] = grouped
+            src = w1_raw[b, a].rearrange("p j (m t) -> p j m t", t=PACK)[:, :, :, t0:t1].rearrange("p j m t -> p m j t")
+            if on_scalar:
+                nc.scalar.copy(out=dst, in_=src)
+            else:
+                nc.vector.tensor_copy(out=dst, in_=src)
+            w1_grouped[b, a, t0] = (grouped, t1)
 
-        def quantise_w1(b, a):
-            codes = keep.tile([P, PASS], U32, name="w1_codes%d%d" % (b, a), align_bytes=64)
-            scales = keep.tile([P, PASS], U8, name="w1_scales%d%d" % (b, a), align_bytes=64)
+        def quantise_w1(b, a, t0):
+            grouped, t1 = w1_grouped[b, a, t0]
+            codes = keep.tile([P, (t1 - t0) * P], U32, name="w1_codes%d%d%d" % (b, a, t0), align_bytes=64)
+            scales = keep.tile([P, (t1 - t0) * P], U8, name="w1_scales%d%d%d" % (b, a, t0), align_bytes=64)
             nc.vector.quantize_mx(out=codes[:].bitcast(FP8X4), scales=scales[:],
-                                  in_=w1_grouped[b, a][:].rearrange("p t m j -> p (t m j)"))
-            w1_codes[b, a] = codes
-            w1_scales[b, a] = scales
+                                  in_=grouped[:].rearrange("p t m j -> p (t m j)"))
+            for t in range(t0, t1):
+                cols = slice((t - t0) * P, (t - t0 + 1) * P)
+                w1_q[b, a, t] = (codes[:, cols], scales[:, cols])
 
         banks = {}
 
-        def project(b, steps):
-            for a, half in steps:
+        def project(b, half):
+            cols = slice(half * BANK, (half + 1) * BANK)
+            for a in range(K_PASSES):
                 m, h = divmod(a, 2)
-                cols = slice(half * BANK, (half + 1) * BANK)
                 for t in range(PACK):
                     if a == 0:
                         banks[b, half, t] = psum.tile([P, BANK], F32, name="bank")
+                    codes, scales = w1_q[b, a, t]
                     nc.tensor.matmul_mx(
                         out=banks[b, half, t][:],
-                        lhsT=w1_codes[b, a][:, t * P:(t + 1) * P].bitcast(FP8X4),
-                        lhsT_scale=w1_scales[b, a][:, t * P:(t + 1) * P],
-                        rhs=v_words[m][:, h, cols].bitcast(FP4X4),
-                        rhs_scale=v_scales[:, 2 * h + m, cols],
+                        lhsT=codes.bitcast(FP8X4), lhsT_scale=scales,
+                        rhs=v_words[m][:, h, cols].bitcast(FP4X4), rhs_scale=v_scales[m][:, h, cols],
                         start=(a == 0), stop=(a == K_PASSES - 1))
 
-        squares = {}
-
-        def square(b, half):
-            sq = ring.tile([P, PACK, BANK], F32, name="sq")
-            for t in range(PACK):
-                nc.scalar.activation(out=sq[:, t, :], in_=banks[b, half, t][:], func=ACT.Square,
-                                     bias=centre_sb[:, b, t:t + 1], scale=-1.0)
-            squares[b, half] = sq
-
-        h_codes = {}
-        h_scales = {}
-
-        def bump(b, j0, width):
+        def square(b, j0, width, on_vector):
             half, c0 = divmod(j0, BANK)
-            bell = ring.tile([P, PACK, width], F32, name="bell", bufs=3)
-            nc.scalar.activation(out=bell[:], in_=squares[b, half][:, :, c0:c0 + width], func=ACT.Exp, scale=-1.0)
+            sq = ring.tile([P, PACK, width], F32, name="sq", bufs=3)
+            for t in range(PACK):
+                src = banks[b, half, t][:, c0:c0 + width]
+                if t < on_vector:
+                    dist = ring.tile([P, width], F32, name="dist")
+                    nc.vector.tensor_scalar(out=dist[:], in0=src, scalar1=centre_sb[:, b, t:t + 1], scalar2=None,
+                                            op0=ALU.subtract)
+                    nc.vector.tensor_tensor(out=sq[:, t, :], in0=dist[:], in1=dist[:], op=ALU.mult)
+                else:
+                    nc.scalar.activation(out=sq[:, t, :], in_=src, func=ACT.Square,
+                                         bias=centre_sb[:, b, t:t + 1], scale=-1.0)
+            assert width % P == 0
+            return sq
+
+        h_q = {}
+
+        def bell(sq, c0, width):
+            e = ring.tile([P, PACK, width], F32, name="bell", bufs=4)
+            nc.scalar.activation(out=e[:], in_=sq[:, :, c0:c0 + width], func=ACT.Exp, scale=-1.0)
+            return e
+
+        def bump(e, c0, b, j0, width):
             hb = ring.tile([P, width, PACK], BF16, name="hb", align_bytes=64)
             nc.vector.tensor_tensor(
                 out=hb[:].rearrange("p (c i) t -> p c t i", i=4),
-                in0=bell[:].rearrange("p t (c i) -> p c t i", i=4),
+                in0=e[:, :, c0:c0 + width].rearrange("p t (c i) -> p c t i", i=4),
                 in1=gain_sb[:, b, :].unsqueeze(1).unsqueeze(3).to_broadcast([P, width // 4, PACK, 4]),
-                op=MULT)
+                op=ALU.mult)
             codes = keep.tile([P, width], U32, name="h_codes%d_%d" % (b, j0), align_bytes=64)
             scales = keep.tile([P, width], U8, name="h_scales%d_%d" % (b, j0), align_bytes=64)
             nc.vector.quantize_mx(out=codes[:].bitcast(FP8X4), scales=scales[:],
                                   in_=hb[:].rearrange("p j t -> p (j t)"))
             for j in range(j0, j0 + width, P):
-                h_codes[b, j] = (codes, j - j0)
-                h_scales[b, j] = (scales, j - j0)
+                h_q[b, j] = (codes, scales, j - j0)
 
         def read_out(dst, u, j0, width):
             for b in range(R_PASSES):
-                codes, c0 = h_codes[b, j0]
-                scales, c0 = h_scales[b, j0]
+                codes, scales, c0 = h_q[b, j0]
                 nc.tensor.matmul_mx(
                     out=dst,
                     lhsT=w2w[:, b, 2 * P * u:2 * P * (u + 1)].bitcast(FP4X4),
@@ -182,48 +161,99 @@ def tile_list_redshift_gaussian_bumps_kernel(tc, tab, offs, w1, centre, gain, w2
 
         out_rows = out.rearrange("(u p) j -> p u j", p=P)
 
-        group_w1(0, 0, P)
-        quantise_w1(0, 0)
-        pick_words(0)
-        group_w1(0, 1, P)
-        quantise_w1(0, 1)
-        pick_words(1)
-        group_w1(0, 2, P)
-        group_w1(0, 3, 0)
-        quantise_w1(0, 2)
-        quantise_w1(0, 3)
-        project(0, [(0, 0), (0, 1), (1, 0), (1, 1), (2, 0), (3, 0), (2, 1), (3, 1)])
-        square(0, 0)
-        for a in range(K_PASSES):
-            group_w1(1, a, 0)
-            quantise_w1(1, a)
-        bump(0, 0, BANK)
-        square(0, 1)
-        bump(0, BANK, BANK)
-        project(1, [(a, half) for half in range(2) for a in range(K_PASSES)])
-        square(1, 0)
-        bump(1, 0, BANK)
-        first = []
-        for u in range(2):
-            acc = psum.tile([P, BANK], F32, name="bank")
-            read_out(acc[:], u, 0, BANK)
-            first.append(acc)
-        square(1, 1)
-        j0 = BANK
-        late = []
-        for width in LAST_CHUNKS:
-            bump(1, j0, width)
+        def finish(j0, width, on_scalar):
             acc = psum.tile([P, BANK], F32, name="bank")
             for u in range(2):
                 for c in range(0, width, P):
                     read_out(acc[:, u * width + c:u * width + c + P], u, j0 + c, P)
-            late.append((acc, j0, width))
-            j0 += width
-        for u in range(2):
-            staged = keep.tile([P, BANK], F32, name="staged%d" % u)
-            nc.scalar.copy(out=staged[:], in_=first[u][:])
-            nc.sync.dma_start(out=out_rows[:, u, 0:BANK], in_=staged[:])
-        for acc, j0, width in late:
-            staged = keep.tile([P, 2, width], F32, name="staged_late%d" % j0)
-            nc.scalar.copy(out=staged[:].rearrange("p u j -> p (u j)"), in_=acc[:, 0:2 * width])
+            staged = keep.tile([P, 2, width], F32, name="staged%d" % j0)
+            if on_scalar:
+                nc.scalar.copy(out=staged[:].rearrange("p u j -> p (u j)"), in_=acc[:, 0:2 * width])
+            else:
+                nc.vector.tensor_copy(out=staged[:].rearrange("p u j -> p (u j)"), in_=acc[:, 0:2 * width])
             nc.sync.dma_start(out=out_rows[:, :, j0:j0 + width], in_=staged[:])
+
+        def finish_bank(u, j0, on_scalar):
+            acc = psum.tile([P, BANK], F32, name="bank")
+            read_out(acc[:], u, j0, BANK)
+            staged = keep.tile([P, BANK], F32, name="staged_bank%d_%d" % (u, j0))
+            if on_scalar:
+                nc.scalar.copy(out=staged[:], in_=acc[:])
+            else:
+                nc.vector.tensor_copy(out=staged[:], in_=acc[:])
+            nc.sync.dma_start(out=out_rows[:, u, j0:j0 + BANK], in_=staged[:])
+
+        nc.vector.memset(tab_scales[64:128, :].bitcast(I32), 0)
+        for m in range(2):
+            nc.vector.memset(v_scales[m][:].rearrange("p h j -> p (h j)").bitcast(I32), 0)
+        nc.vector.memset(w2s[:].rearrange("p a c -> p (a c)").bitcast(I32), 0)
+        nc.vector.memset(warm[:], 0.0)
+        nc.scalar.activation(out=warm[:], in_=warm[:], func=ACT.Exp)
+
+        nc.sync.dma_start(offsets[:], offs)
+        for m in range(2):
+            nc.sync.dma_start(
+                out=tab_scales[32 * m:32 * m + 32, :].bitcast(I32),
+                in_=tab[m, PASS * T:].rearrange("(h q t) -> q h t", h=2, q=16).bitcast(I32))
+        load_w1("area_c", [(0, 0)])
+        load_words("area_a", 0)
+        nc.gpsimd.dma_start(out=centre_sb[:], in_=centre.rearrange("(b p t) -> p b t", p=P, t=PACK))
+        nc.gpsimd.dma_start(out=gain_sb[:], in_=gain.rearrange("(b p t) -> p b t", p=P, t=PACK))
+        nc.gpsimd.dma_start(out=w2w[:].bitcast(I32), in_=w2_words.rearrange("a p c -> p a c").bitcast(I32))
+        for q in range(4):
+            nc.gpsimd.dma_start(
+                out=w2s[32 * q:32 * q + 4, :, :].bitcast(I32),
+                in_=w2_scales[:, 4 * q:4 * q + 4, :].rearrange("a r c -> r a c").bitcast(I32))
+
+        nc.vector.tensor_copy(picked_scales[:], tab_scales[:].indirect(offsets[:]))
+        place_scales(0)
+        load_words("area_b", 1)
+        place_scales(1)
+        group_w1(0, 0, 0, 4, True)
+        load_w1("area_c", [(0, 1), (0, 2)])
+        quantise_w1(0, 0, 0)
+        pick_words(0)
+        load_w1("area_a", [(0, 3), (1, 0)])
+        pick_words(1)
+        load_w1("area_b", [(1, 1), (1, 2)])
+        for a in range(1, K_PASSES):
+            group_w1(0, a, 2, 4, True)
+            group_w1(0, a, 0, 2, False)
+            quantise_w1(0, a, 0)
+            quantise_w1(0, a, 2)
+            if a == 2:
+                load_w1("area_c", [(1, 3)])
+        project(0, 0)
+        project(0, 1)
+        sq = square(0, 0, BANK, 0)
+        for a in range(K_PASSES - 1):
+            group_w1(1, a, 0, 4, False)
+            quantise_w1(1, a, 0)
+        for t0 in (0, 2):
+            group_w1(1, 3, t0, t0 + 2, False)
+            quantise_w1(1, 3, t0)
+        e00 = bell(sq, 0, BANK)
+        sq = square(0, BANK, BANK, 0)
+        e01 = bell(sq, 0, BANK)
+        project(1, 0)
+        project(1, 1)
+        for c in range(0, BANK, 256):
+            bump(e00, c, 0, c, 256)
+        bump(e01, 0, 0, BANK, BANK)
+        sq = square(1, 0, BANK, 0)
+        e = bell(sq, 0, BANK)
+        bump(e, 0, 1, 0, BANK)
+        sq = square(1, BANK, 256, 0)
+        e = bell(sq, 0, 256)
+        bump(e, 0, 1, BANK, 256)
+        sq = square(1, 768, 256, 0)
+        e2 = bell(sq, 0, 128)
+        e3 = bell(sq, 128, 128)
+        assert S == 2 * BANK
+        bump(e2, 0, 1, 768, 128)
+        bump(e3, 0, 1, 896, 128)
+        finish(0, 256, True)
+        finish(256, 256, True)
+        finish(512, 256, True)
+        finish(768, 128, True)
+        finish(896, 128, True)

@@ -32,11 +32,9 @@ def tile_list_redshift_gaussian_bumps_kernel(tc, tab, offs, w1, centre, gain, w2
         psum = ctx.enter_context(tc.psum_pool(name="psum", bufs=8))
 
         offsets = keep.tile([P, S // 16], U16, name="offsets")
-        tab_scales = keep.tile([P, T], U8, name="tab_scales", tag="area_b")
+        tab_scales = keep.tile([P, T], U8, name="tab_scales", tag="area_b", align_bytes=64)
         centre_sb = keep.tile([P, R_PASSES, PACK], F32, name="centre_sb")
         gain_sb = keep.tile([P, R_PASSES, PACK], F32, name="gain_sb")
-        w2w = keep.tile([P, R_PASSES, 2 * N], U8, name="w2w", align_bytes=64)
-        w2s = keep.tile([P, R_PASSES, N], U8, name="w2s", align_bytes=64)
         v_scales = [keep.tile([P, 2, S], U8, name="v_scales%d" % m, align_bytes=64) for m in range(2)]
         warm = keep.tile([P, 1], F32, name="warm")
         picked_scales = keep.tile([P, S], U8, name="picked_scales")
@@ -44,7 +42,7 @@ def tile_list_redshift_gaussian_bumps_kernel(tc, tab, offs, w1, centre, gain, w2
         w1_raw = {}
 
         def load_w1(tag, pieces):
-            raw = keep.tile([P, len(pieces), PACK, PASS], F32, name="w1_raw", tag=tag)
+            raw = keep.tile([P, len(pieces), PACK, PASS], F32, name="w1_raw", tag=tag, align_bytes=64)
             for i, (b, a) in enumerate(pieces):
                 w1_raw[b, a] = raw[:, i]
                 nc.sync.dma_start(
@@ -52,7 +50,7 @@ def tile_list_redshift_gaussian_bumps_kernel(tc, tab, offs, w1, centre, gain, w2
                     in_=w1[a * PASS:(a + 1) * PASS, b * PASS:(b + 1) * PASS].rearrange("(p j) c -> p j c", j=PACK))
 
         def load_words(tag, m):
-            tab_words[m] = keep.tile([P, T], U32, name="tab_words", tag=tag)
+            tab_words[m] = keep.tile([P, T], U32, name="tab_words", tag=tag, align_bytes=64)
             nc.sync.dma_start(
                 out=tab_words[m][:].bitcast(I32),
                 in_=tab[m, 0:PASS * T].rearrange("(p x) -> p x", p=P).bitcast(I32))
@@ -111,21 +109,13 @@ def tile_list_redshift_gaussian_bumps_kernel(tc, tab, offs, w1, centre, gain, w2
                         rhs=v_words[m][:, h, cols].bitcast(FP4X4), rhs_scale=v_scales[m][:, h, cols],
                         start=(a == 0), stop=(a == K_PASSES - 1))
 
-        def square(b, j0, width, on_vector):
+        def square(sq, b, j0, width):
             half, c0 = divmod(j0, BANK)
-            sq = ring.tile([P, PACK, width], F32, name="sq", bufs=3)
             for t in range(PACK):
                 src = banks[b, half, t][:, c0:c0 + width]
-                if t < on_vector:
-                    dist = ring.tile([P, width], F32, name="dist")
-                    nc.vector.tensor_scalar(out=dist[:], in0=src, scalar1=centre_sb[:, b, t:t + 1], scalar2=None,
-                                            op0=ALU.subtract)
-                    nc.vector.tensor_tensor(out=sq[:, t, :], in0=dist[:], in1=dist[:], op=ALU.mult)
-                else:
-                    nc.scalar.activation(out=sq[:, t, :], in_=src, func=ACT.Square,
-                                         bias=centre_sb[:, b, t:t + 1], scale=-1.0)
+                nc.scalar.activation(out=sq[:, t, c0:c0 + width], in_=src, func=ACT.Square,
+                                     bias=centre_sb[:, b, t:t + 1], scale=-1.0)
             assert width % P == 0
-            return sq
 
         h_q = {}
 
@@ -134,19 +124,32 @@ def tile_list_redshift_gaussian_bumps_kernel(tc, tab, offs, w1, centre, gain, w2
             nc.scalar.activation(out=e[:], in_=sq[:, :, c0:c0 + width], func=ACT.Exp, scale=-1.0)
             return e
 
-        def bump(e, c0, b, j0, width):
-            hb = ring.tile([P, width, PACK], BF16, name="hb", align_bytes=64)
-            nc.vector.tensor_tensor(
-                out=hb[:].rearrange("p (c i) t -> p c t i", i=4),
-                in0=e[:, :, c0:c0 + width].rearrange("p t (c i) -> p c t i", i=4),
-                in1=gain_sb[:, b, :].unsqueeze(1).unsqueeze(3).to_broadcast([P, width // 4, PACK, 4]),
-                op=ALU.mult)
-            codes = keep.tile([P, width], U32, name="h_codes%d_%d" % (b, j0), align_bytes=64)
-            scales = keep.tile([P, width], U8, name="h_scales%d_%d" % (b, j0), align_bytes=64)
-            nc.vector.quantize_mx(out=codes[:].bitcast(FP8X4), scales=scales[:],
-                                  in_=hb[:].rearrange("p j t -> p (j t)"))
-            for j in range(j0, j0 + width, P):
-                h_q[b, j] = (codes, scales, j - j0)
+        def bump(e, b, j0, width, parts, held=None):
+            step = width // parts
+            planes = []
+            woven = []
+            for c0 in range(0, width, step):
+                if held and c0 == 0:
+                    pl = keep.tile([P, PACK, step], BF16, name="planes_held", tag=held, align_bytes=64)
+                else:
+                    pl = ring.tile([P, PACK, step], BF16, name="planes", bufs=3)
+                for t in range(PACK):
+                    nc.vector.tensor_scalar(out=pl[:, t, :], in0=e[:, t, c0:c0 + step],
+                                            scalar1=gain_sb[:, b, t:t + 1], scalar2=None, op0=ALU.mult)
+                planes.append(pl)
+            for pl in planes:
+                hb = ring.tile([P, step, PACK], BF16, name="hb", align_bytes=64, bufs=3)
+                nc.vector.tensor_copy(out=hb[:].rearrange("p (c i) t -> p c t i", i=4),
+                                      in_=pl[:].rearrange("p t (c i) -> p c t i", i=4))
+                woven.append(hb)
+            for i, hb in enumerate(woven):
+                j1 = j0 + i * step
+                codes = keep.tile([P, step], U32, name="h_codes%d_%d" % (b, j1), align_bytes=64)
+                scales = keep.tile([P, step], U8, name="h_scales%d_%d" % (b, j1), align_bytes=64)
+                nc.vector.quantize_mx(out=codes[:].bitcast(FP8X4), scales=scales[:],
+                                      in_=hb[:].rearrange("p j t -> p (j t)"))
+                for j in range(j1, j1 + step, P):
+                    h_q[b, j] = (codes, scales, j - j1)
 
         def read_out(dst, u, j0, width):
             for b in range(R_PASSES):
@@ -161,32 +164,18 @@ def tile_list_redshift_gaussian_bumps_kernel(tc, tab, offs, w1, centre, gain, w2
 
         out_rows = out.rearrange("(u p) j -> p u j", p=P)
 
-        def finish(j0, width, on_scalar):
+        def finish(staged, j0, width):
             acc = psum.tile([P, BANK], F32, name="bank")
             for u in range(2):
                 for c in range(0, width, P):
                     read_out(acc[:, u * width + c:u * width + c + P], u, j0 + c, P)
-            staged = keep.tile([P, 2, width], F32, name="staged%d" % j0)
-            if on_scalar:
-                nc.scalar.copy(out=staged[:].rearrange("p u j -> p (u j)"), in_=acc[:, 0:2 * width])
-            else:
-                nc.vector.tensor_copy(out=staged[:].rearrange("p u j -> p (u j)"), in_=acc[:, 0:2 * width])
-            nc.sync.dma_start(out=out_rows[:, :, j0:j0 + width], in_=staged[:])
-
-        def finish_bank(u, j0, on_scalar):
-            acc = psum.tile([P, BANK], F32, name="bank")
-            read_out(acc[:], u, j0, BANK)
-            staged = keep.tile([P, BANK], F32, name="staged_bank%d_%d" % (u, j0))
-            if on_scalar:
-                nc.scalar.copy(out=staged[:], in_=acc[:])
-            else:
-                nc.vector.tensor_copy(out=staged[:], in_=acc[:])
-            nc.sync.dma_start(out=out_rows[:, u, j0:j0 + BANK], in_=staged[:])
+            rows = staged[:, 2 * j0:2 * (j0 + width)]
+            nc.scalar.copy(out=rows, in_=acc[:, 0:2 * width])
+            nc.sync.dma_start(out=out_rows[:, :, j0:j0 + width], in_=rows.rearrange("p (u j) -> p u j", u=2))
 
         nc.vector.memset(tab_scales[64:128, :].bitcast(I32), 0)
         for m in range(2):
             nc.vector.memset(v_scales[m][:].rearrange("p h j -> p (h j)").bitcast(I32), 0)
-        nc.vector.memset(w2s[:].rearrange("p a c -> p (a c)").bitcast(I32), 0)
         nc.vector.memset(warm[:], 0.0)
         nc.scalar.activation(out=warm[:], in_=warm[:], func=ACT.Exp)
 
@@ -197,13 +186,8 @@ def tile_list_redshift_gaussian_bumps_kernel(tc, tab, offs, w1, centre, gain, w2
                 in_=tab[m, PASS * T:].rearrange("(h q t) -> q h t", h=2, q=16).bitcast(I32))
         load_w1("area_c", [(0, 0)])
         load_words("area_a", 0)
-        nc.gpsimd.dma_start(out=centre_sb[:], in_=centre.rearrange("(b p t) -> p b t", p=P, t=PACK))
-        nc.gpsimd.dma_start(out=gain_sb[:], in_=gain.rearrange("(b p t) -> p b t", p=P, t=PACK))
-        nc.gpsimd.dma_start(out=w2w[:].bitcast(I32), in_=w2_words.rearrange("a p c -> p a c").bitcast(I32))
-        for q in range(4):
-            nc.gpsimd.dma_start(
-                out=w2s[32 * q:32 * q + 4, :, :].bitcast(I32),
-                in_=w2_scales[:, 4 * q:4 * q + 4, :].rearrange("a r c -> r a c").bitcast(I32))
+        nc.sync.dma_start(out=centre_sb[:], in_=centre.rearrange("(b p t) -> p b t", p=P, t=PACK))
+        nc.sync.dma_start(out=gain_sb[:], in_=gain.rearrange("(b p t) -> p b t", p=P, t=PACK))
 
         nc.vector.tensor_copy(picked_scales[:], tab_scales[:].indirect(offsets[:]))
         place_scales(0)
@@ -225,35 +209,46 @@ def tile_list_redshift_gaussian_bumps_kernel(tc, tab, offs, w1, centre, gain, w2
                 load_w1("area_c", [(1, 3)])
         project(0, 0)
         project(0, 1)
-        sq = square(0, 0, BANK, 0)
-        for a in range(K_PASSES - 1):
-            group_w1(1, a, 0, 4, False)
+        sq = ring.tile([P, PACK, BANK], F32, name="sq")
+        square(sq, 0, 0, BANK)
+        for a in range(K_PASSES):
+            group_w1(1, a, 0, 2, False)
+            group_w1(1, a, 2, 4, False)
             quantise_w1(1, a, 0)
-        for t0 in (0, 2):
-            group_w1(1, 3, t0, t0 + 2, False)
-            quantise_w1(1, 3, t0)
+            quantise_w1(1, a, 2)
+        w2w = keep.tile([P, R_PASSES, 2 * N], U8, name="w2w", tag="area_a", align_bytes=64)
+        nc.sync.dma_start(out=w2w[:].bitcast(I32), in_=w2_words.rearrange("a p c -> p a c").bitcast(I32))
+        w2s = keep.tile([P, R_PASSES, N], U8, name="w2s", tag="area_b", align_bytes=64)
+        nc.vector.memset(w2s[:].rearrange("p a c -> p (a c)").bitcast(I32), 0)
+        for q in range(4):
+            nc.sync.dma_start(
+                out=w2s[32 * q:32 * q + 4, :, :].bitcast(I32),
+                in_=w2_scales[:, 4 * q:4 * q + 4, :].rearrange("a r c -> r a c").bitcast(I32))
         e00 = bell(sq, 0, BANK)
-        sq = square(0, BANK, BANK, 0)
+        sq = ring.tile([P, PACK, BANK], F32, name="sq")
+        square(sq, 0, BANK, BANK)
         e01 = bell(sq, 0, BANK)
         project(1, 0)
         project(1, 1)
-        for c in range(0, BANK, 256):
-            bump(e00, c, 0, c, 256)
-        bump(e01, 0, 0, BANK, BANK)
-        sq = square(1, 0, BANK, 0)
+        bump(e00, 0, 0, BANK, 1, "area_c")
+        bump(e01, 0, BANK, BANK, 2)
+        sq = ring.tile([P, PACK, BANK], F32, name="sq")
+        square(sq, 1, 0, BANK)
         e = bell(sq, 0, BANK)
-        bump(e, 0, 1, 0, BANK)
-        sq = square(1, BANK, 256, 0)
+        bump(e, 1, 0, BANK, 2)
+        sq = keep.tile([P, PACK, BANK], F32, name="sq_last", tag="area_d")
+        square(sq, 1, BANK, 256)
         e = bell(sq, 0, 256)
-        bump(e, 0, 1, BANK, 256)
-        sq = square(1, 768, 256, 0)
-        e2 = bell(sq, 0, 128)
-        e3 = bell(sq, 128, 128)
+        bump(e, 1, BANK, 256, 2)
+        square(sq, 1, 768, 256)
+        e2 = bell(sq, 256, 128)
+        e3 = bell(sq, 384, 128)
         assert S == 2 * BANK
-        bump(e2, 0, 1, 768, 128)
-        bump(e3, 0, 1, 896, 128)
-        finish(0, 256, True)
-        finish(256, 256, True)
-        finish(512, 256, True)
-        finish(768, 128, True)
-        finish(896, 128, True)
+        bump(e2, 1, 768, 128, 1)
+        bump(e3, 1, 896, 128, 1)
+        staged = keep.tile([P, 2 * S], F32, name="staged", tag="area_d")
+        finish(staged, 0, 256)
+        finish(staged, 256, 256)
+        finish(staged, 512, 256)
+        finish(staged, 768, 128)
+        finish(staged, 896, 128)

@@ -20,8 +20,11 @@ P = 128
 PACK = 4
 PASS = P * PACK
 BANK = 512
+CHUNK = 256
+QUADRANTS = 4
 K_PASSES = K // PASS
-R_PASSES = H // PASS
+GROUPS = H // PASS
+ALIGN = 64
 
 
 def tile_list_redshift_gaussian_bumps_kernel(tc, tab, offs, w1, centre, gain, w2_words, w2_scales, out):
@@ -32,49 +35,48 @@ def tile_list_redshift_gaussian_bumps_kernel(tc, tab, offs, w1, centre, gain, w2
         psum = ctx.enter_context(tc.psum_pool(name="psum", bufs=8))
 
         offsets = keep.tile([P, S // 16], U16, name="offsets")
-        tab_scales = keep.tile([P, T], U8, name="tab_scales", tag="area_b", align_bytes=64)
-        centre_sb = keep.tile([P, R_PASSES, PACK], F32, name="centre_sb")
-        gain_sb = keep.tile([P, R_PASSES, PACK], F32, name="gain_sb")
-        v_scales = [keep.tile([P, 2, S], U8, name="v_scales%d" % m, align_bytes=64) for m in range(2)]
-        warm = keep.tile([P, 1], F32, name="warm")
+        tab_scales = keep.tile([P, T], U8, name="tab_scales", tag="area_b", align_bytes=ALIGN)
+        centre_sb = keep.tile([P, GROUPS, PACK], F32, name="centre_sb")
+        gain_sb = keep.tile([P, GROUPS, PACK], F32, name="gain_sb")
+        v_scales = [keep.tile([P, 2, S], U8, name="v_scales%d" % n, align_bytes=ALIGN) for n in range(2)]
         picked_scales = keep.tile([P, S], U8, name="picked_scales")
         tab_words = {}
         w1_raw = {}
 
-        def load_w1(tag, pieces):
-            raw = keep.tile([P, len(pieces), PACK, PASS], F32, name="w1_raw", tag=tag, align_bytes=64)
+        def load_w1(area, pieces):
+            raw = keep.tile([P, len(pieces), PACK, PASS], F32, name="w1_raw", tag=area, align_bytes=ALIGN)
             for i, (b, a) in enumerate(pieces):
                 w1_raw[b, a] = raw[:, i]
                 nc.sync.dma_start(
                     out=w1_raw[b, a],
                     in_=w1[a * PASS:(a + 1) * PASS, b * PASS:(b + 1) * PASS].rearrange("(p j) c -> p j c", j=PACK))
 
-        def load_words(tag, m):
-            tab_words[m] = keep.tile([P, T], U32, name="tab_words", tag=tag, align_bytes=64)
+        def load_words(area, n):
+            tab_words[n] = keep.tile([P, T], U32, name="tab_words", tag=area, align_bytes=ALIGN)
             nc.sync.dma_start(
-                out=tab_words[m][:].bitcast(I32),
-                in_=tab[m, 0:PASS * T].rearrange("(p x) -> p x", p=P).bitcast(I32))
+                out=tab_words[n][:].bitcast(I32),
+                in_=tab[n, 0:PASS * T].rearrange("(p x) -> p x", p=P).bitcast(I32))
 
-        def place_scales(m):
-            for q in range(4):
+        def place_scales(n):
+            for q in range(QUADRANTS):
                 nc.sync.dma_start(
-                    out=v_scales[m][32 * q:32 * q + 4, :, :].bitcast(I32),
-                    in_=picked_scales[32 * m + 8 * q:32 * m + 8 * q + 8, :].bitcast(I32))
+                    out=v_scales[n][32 * q:32 * q + 4, :, :].bitcast(I32),
+                    in_=picked_scales[32 * n + 8 * q:32 * n + 8 * q + 8, :].bitcast(I32))
 
         v_words = {}
 
-        def pick_words(m):
-            picked = keep.tile([P, S], U32, name="picked%d" % m)
-            nc.vector.tensor_copy(picked[:], tab_words[m][:].indirect(offsets[:]))
-            parted = keep.tile([P, 2, S], U16, name="parted%d" % m, align_bytes=64)
+        def pick_words(n):
+            picked = keep.tile([P, S], U32, name="picked%d" % n)
+            nc.vector.tensor_copy(picked[:], tab_words[n][:].indirect(offsets[:]))
+            parted = keep.tile([P, 2, S], U16, name="parted%d" % n, align_bytes=ALIGN)
             nc.vector.tensor_copy(parted[:], picked[:].bitcast(U16).rearrange("p (j h) -> p h j", h=2))
-            v_words[m] = parted
+            v_words[n] = parted
 
         w1_grouped = {}
-        w1_q = {}
+        w1_mx = {}
 
         def group_w1(b, a, t0, t1, on_scalar):
-            grouped = ring.tile([P, t1 - t0, P, PACK], BF16, name="w1_grouped", align_bytes=64, bufs=4)
+            grouped = ring.tile([P, t1 - t0, P, PACK], BF16, name="w1_grouped", align_bytes=ALIGN, bufs=4)
             dst = grouped[:].rearrange("p t m j -> p m j t")
             src = w1_raw[b, a].rearrange("p j (m t) -> p j m t", t=PACK)[:, :, :, t0:t1].rearrange("p j m t -> p m j t")
             if on_scalar:
@@ -85,170 +87,167 @@ def tile_list_redshift_gaussian_bumps_kernel(tc, tab, offs, w1, centre, gain, w2
 
         def quantise_w1(b, a, t0):
             grouped, t1 = w1_grouped[b, a, t0]
-            codes = keep.tile([P, (t1 - t0) * P], U32, name="w1_codes%d%d%d" % (b, a, t0), align_bytes=64)
-            scales = keep.tile([P, (t1 - t0) * P], U8, name="w1_scales%d%d%d" % (b, a, t0), align_bytes=64)
+            codes = keep.tile([P, (t1 - t0) * P], U32, name="w1_codes%d%d%d" % (b, a, t0), align_bytes=ALIGN)
+            scales = keep.tile([P, (t1 - t0) * P], U8, name="w1_scales%d%d%d" % (b, a, t0), align_bytes=ALIGN)
             nc.vector.quantize_mx(out=codes[:].bitcast(FP8X4), scales=scales[:],
                                   in_=grouped[:].rearrange("p t m j -> p (t m j)"))
             for t in range(t0, t1):
                 cols = slice((t - t0) * P, (t - t0 + 1) * P)
-                w1_q[b, a, t] = (codes[:, cols], scales[:, cols])
+                w1_mx[b, a, t] = (codes[:, cols], scales[:, cols])
 
         banks = {}
 
         def project(b, half):
             cols = slice(half * BANK, (half + 1) * BANK)
             for a in range(K_PASSES):
-                m, h = divmod(a, 2)
+                n, h = divmod(a, 2)
                 for t in range(PACK):
                     if a == 0:
                         banks[b, half, t] = psum.tile([P, BANK], F32, name="bank")
-                    codes, scales = w1_q[b, a, t]
+                    codes, scales = w1_mx[b, a, t]
                     nc.tensor.matmul_mx(
                         out=banks[b, half, t][:],
                         lhsT=codes.bitcast(FP8X4), lhsT_scale=scales,
-                        rhs=v_words[m][:, h, cols].bitcast(FP4X4), rhs_scale=v_scales[m][:, h, cols],
+                        rhs=v_words[n][:, h, cols].bitcast(FP4X4), rhs_scale=v_scales[n][:, h, cols],
                         start=(a == 0), stop=(a == K_PASSES - 1))
 
         def square(sq, b, j0, width):
             half, c0 = divmod(j0, BANK)
             for t in range(PACK):
-                src = banks[b, half, t][:, c0:c0 + width]
-                nc.scalar.activation(out=sq[:, t, c0:c0 + width], in_=src, func=ACT.Square,
-                                     bias=centre_sb[:, b, t:t + 1], scale=-1.0)
-            assert width % P == 0
-
-        h_q = {}
+                nc.scalar.activation(out=sq[:, t, c0:c0 + width], in_=banks[b, half, t][:, c0:c0 + width],
+                                     func=ACT.Square, bias=centre_sb[:, b, t:t + 1], scale=-1.0)
 
         def bell(sq, c0, width):
             e = ring.tile([P, PACK, width], F32, name="bell", bufs=4)
             nc.scalar.activation(out=e[:], in_=sq[:, :, c0:c0 + width], func=ACT.Exp, scale=-1.0)
             return e
 
-        def bump(e, b, j0, width, parts, held=None):
+        h_mx = {}
+
+        def bump(e, b, j0, width, parts, held):
             step = width // parts
-            planes = []
+            scaled = []
             woven = []
             for c0 in range(0, width, step):
-                if held and c0 == 0:
-                    pl = keep.tile([P, PACK, step], BF16, name="planes_held", tag=held, align_bytes=64)
+                if held and c0 > 0:
+                    rounded = keep.tile([P, PACK, step], BF16, name="h_held", tag=held, align_bytes=ALIGN)
                 else:
-                    pl = ring.tile([P, PACK, step], BF16, name="planes", bufs=3)
+                    rounded = ring.tile([P, PACK, step], BF16, name="h_rounded", bufs=3)
                 for t in range(PACK):
-                    nc.vector.tensor_scalar(out=pl[:, t, :], in0=e[:, t, c0:c0 + step],
+                    nc.vector.tensor_scalar(out=rounded[:, t, :], in0=e[:, t, c0:c0 + step],
                                             scalar1=gain_sb[:, b, t:t + 1], scalar2=None, op0=ALU.mult)
-                planes.append(pl)
-            for pl in planes:
-                hb = ring.tile([P, step, PACK], BF16, name="hb", align_bytes=64, bufs=3)
+                scaled.append(rounded)
+            for rounded in scaled:
+                hb = ring.tile([P, step, PACK], BF16, name="h_woven", align_bytes=ALIGN, bufs=3)
                 nc.vector.tensor_copy(out=hb[:].rearrange("p (c i) t -> p c t i", i=4),
-                                      in_=pl[:].rearrange("p t (c i) -> p c t i", i=4))
+                                      in_=rounded[:].rearrange("p t (c i) -> p c t i", i=4))
                 woven.append(hb)
             for i, hb in enumerate(woven):
                 j1 = j0 + i * step
-                codes = keep.tile([P, step], U32, name="h_codes%d_%d" % (b, j1), align_bytes=64)
-                scales = keep.tile([P, step], U8, name="h_scales%d_%d" % (b, j1), align_bytes=64)
+                codes = keep.tile([P, step], U32, name="h_codes%d_%d" % (b, j1), align_bytes=ALIGN)
+                scales = keep.tile([P, step], U8, name="h_scales%d_%d" % (b, j1), align_bytes=ALIGN)
                 nc.vector.quantize_mx(out=codes[:].bitcast(FP8X4), scales=scales[:],
                                       in_=hb[:].rearrange("p j t -> p (j t)"))
-                for j in range(j1, j1 + step, P):
-                    h_q[b, j] = (codes, scales, j - j1)
-
-        def read_out(dst, u, j0, width):
-            for b in range(R_PASSES):
-                codes, scales, c0 = h_q[b, j0]
-                nc.tensor.matmul_mx(
-                    out=dst,
-                    lhsT=w2w[:, b, 2 * P * u:2 * P * (u + 1)].bitcast(FP4X4),
-                    lhsT_scale=w2s[:, b, P * u:P * (u + 1)],
-                    rhs=codes[:, c0:c0 + width].bitcast(FP8X4),
-                    rhs_scale=scales[:, c0:c0 + width],
-                    start=(b == 0), stop=(b == R_PASSES - 1))
+                for c in range(0, step, P):
+                    h_mx[b, j1 + c] = (codes[:, c:c + P], scales[:, c:c + P])
 
         out_rows = out.rearrange("(u p) j -> p u j", p=P)
 
         def finish(staged, j0, width):
             acc = psum.tile([P, BANK], F32, name="bank")
-            for u in range(2):
+            for u in range(N // P):
                 for c in range(0, width, P):
-                    read_out(acc[:, u * width + c:u * width + c + P], u, j0 + c, P)
+                    for b in range(GROUPS):
+                        codes, scales = h_mx[b, j0 + c]
+                        nc.tensor.matmul_mx(
+                            out=acc[:, u * width + c:u * width + c + P],
+                            lhsT=w2w[:, b, 2 * P * u:2 * P * (u + 1)].bitcast(FP4X4),
+                            lhsT_scale=w2s[:, b, P * u:P * (u + 1)],
+                            rhs=codes.bitcast(FP8X4), rhs_scale=scales,
+                            start=(b == 0), stop=(b == GROUPS - 1))
             rows = staged[:, 2 * j0:2 * (j0 + width)]
             nc.scalar.copy(out=rows, in_=acc[:, 0:2 * width])
             nc.sync.dma_start(out=out_rows[:, :, j0:j0 + width], in_=rows.rearrange("p (u j) -> p u j", u=2))
 
         nc.vector.memset(tab_scales[64:128, :].bitcast(I32), 0)
-        for m in range(2):
-            nc.vector.memset(v_scales[m][:].rearrange("p h j -> p (h j)").bitcast(I32), 0)
-        nc.vector.memset(warm[:], 0.0)
-        nc.scalar.activation(out=warm[:], in_=warm[:], func=ACT.Exp)
+        for n in range(2):
+            nc.vector.memset(v_scales[n][:].rearrange("p h j -> p (h j)").bitcast(I32), 0)
 
         nc.sync.dma_start(offsets[:], offs)
-        for m in range(2):
+        for n in range(2):
             nc.sync.dma_start(
-                out=tab_scales[32 * m:32 * m + 32, :].bitcast(I32),
-                in_=tab[m, PASS * T:].rearrange("(h q t) -> q h t", h=2, q=16).bitcast(I32))
+                out=tab_scales[32 * n:32 * n + 32, :].bitcast(I32),
+                in_=tab[n, PASS * T:].rearrange("(h q t) -> q h t", h=2, q=16).bitcast(I32))
         load_w1("area_c", [(0, 0)])
         load_words("area_a", 0)
-        nc.sync.dma_start(out=centre_sb[:], in_=centre.rearrange("(b p t) -> p b t", p=P, t=PACK))
-        nc.sync.dma_start(out=gain_sb[:], in_=gain.rearrange("(b p t) -> p b t", p=P, t=PACK))
+        load_w1("area_e", [(0, 1)])
+        nc.gpsimd.dma_start(out=centre_sb[:], in_=centre.rearrange("(b p t) -> p b t", p=P, t=PACK))
+        nc.gpsimd.dma_start(out=gain_sb[:], in_=gain.rearrange("(b p t) -> p b t", p=P, t=PACK))
 
         nc.vector.tensor_copy(picked_scales[:], tab_scales[:].indirect(offsets[:]))
         place_scales(0)
         load_words("area_b", 1)
         place_scales(1)
+
         group_w1(0, 0, 0, 4, True)
-        load_w1("area_c", [(0, 1), (0, 2)])
+        load_w1("area_c", [(0, 2)])
         quantise_w1(0, 0, 0)
         pick_words(0)
         load_w1("area_a", [(0, 3), (1, 0)])
+        group_w1(0, 1, 0, 4, True)
+        load_w1("area_e", [(1, 1)])
+        quantise_w1(0, 1, 0)
         pick_words(1)
-        load_w1("area_b", [(1, 1), (1, 2)])
-        for a in range(1, K_PASSES):
-            group_w1(0, a, 2, 4, True)
-            group_w1(0, a, 0, 2, False)
-            quantise_w1(0, a, 0)
-            quantise_w1(0, a, 2)
-            if a == 2:
-                load_w1("area_c", [(1, 3)])
+        load_w1("area_b", [(1, 2), (1, 3)])
+        group_w1(0, 2, 0, 2, True)
+        group_w1(0, 2, 2, 4, True)
+        group_w1(0, 3, 2, 4, True)
+        quantise_w1(0, 2, 0)
+        group_w1(0, 3, 0, 2, False)
+        quantise_w1(0, 2, 2)
+        quantise_w1(0, 3, 0)
+        quantise_w1(0, 3, 2)
         project(0, 0)
         project(0, 1)
         sq = ring.tile([P, PACK, BANK], F32, name="sq")
         square(sq, 0, 0, BANK)
+
         for a in range(K_PASSES):
             group_w1(1, a, 0, 2, False)
             group_w1(1, a, 2, 4, False)
             quantise_w1(1, a, 0)
             quantise_w1(1, a, 2)
-        w2w = keep.tile([P, R_PASSES, 2 * N], U8, name="w2w", tag="area_a", align_bytes=64)
+
+        w2w = keep.tile([P, GROUPS, 2 * N], U8, name="w2w", tag="area_a", align_bytes=ALIGN)
         nc.sync.dma_start(out=w2w[:].bitcast(I32), in_=w2_words.rearrange("a p c -> p a c").bitcast(I32))
-        w2s = keep.tile([P, R_PASSES, N], U8, name="w2s", tag="area_b", align_bytes=64)
+        w2s = keep.tile([P, GROUPS, N], U8, name="w2s", tag="area_e", align_bytes=ALIGN)
         nc.vector.memset(w2s[:].rearrange("p a c -> p (a c)").bitcast(I32), 0)
-        for q in range(4):
+        for q in range(QUADRANTS):
             nc.sync.dma_start(
                 out=w2s[32 * q:32 * q + 4, :, :].bitcast(I32),
                 in_=w2_scales[:, 4 * q:4 * q + 4, :].rearrange("a r c -> r a c").bitcast(I32))
-        e00 = bell(sq, 0, BANK)
+
+        first_bell = bell(sq, 0, BANK)
         sq = ring.tile([P, PACK, BANK], F32, name="sq")
         square(sq, 0, BANK, BANK)
-        e01 = bell(sq, 0, BANK)
+        second_bell = bell(sq, 0, BANK)
         project(1, 0)
         project(1, 1)
-        bump(e00, 0, 0, BANK, 1, "area_c")
-        bump(e01, 0, BANK, BANK, 2)
+        bump(first_bell, 0, 0, BANK, 2, "area_b")
+        bump(second_bell, 0, BANK, BANK, 2, None)
         sq = ring.tile([P, PACK, BANK], F32, name="sq")
         square(sq, 1, 0, BANK)
-        e = bell(sq, 0, BANK)
-        bump(e, 1, 0, BANK, 2)
+        bump(bell(sq, 0, BANK), 1, 0, BANK, 2, None)
+
         sq = keep.tile([P, PACK, BANK], F32, name="sq_last", tag="area_d")
-        square(sq, 1, BANK, 256)
-        e = bell(sq, 0, 256)
-        bump(e, 1, BANK, 256, 2)
-        square(sq, 1, 768, 256)
-        e2 = bell(sq, 256, 128)
-        e3 = bell(sq, 384, 128)
-        assert S == 2 * BANK
-        bump(e2, 1, 768, 128, 1)
-        bump(e3, 1, 896, 128, 1)
+        square(sq, 1, BANK, CHUNK)
+        bump(bell(sq, 0, CHUNK), 1, BANK, CHUNK, 2, None)
+        square(sq, 1, BANK + CHUNK, CHUNK)
+        last_bells = [bell(sq, c0, P) for c0 in range(CHUNK, BANK, P)]
+        for i, e in enumerate(last_bells):
+            bump(e, 1, BANK + CHUNK + i * P, P, 1, None)
         staged = keep.tile([P, 2 * S], F32, name="staged", tag="area_d")
-        finish(staged, 0, 256)
-        finish(staged, 256, 256)
-        finish(staged, 512, 256)
-        finish(staged, 768, 128)
-        finish(staged, 896, 128)
+        for j0 in range(0, S - CHUNK, CHUNK):
+            finish(staged, j0, CHUNK)
+        for j0 in range(S - CHUNK, S, P):
+            finish(staged, j0, P)

@@ -32,222 +32,217 @@ def tile_list_redshift_gaussian_bumps_kernel(tc, tab, offs, w1, centre, gain, w2
     with ExitStack() as ctx:
         keep = ctx.enter_context(tc.tile_pool(name="keep", bufs=1))
         ring = ctx.enter_context(tc.tile_pool(name="ring", bufs=2))
+        early = ctx.enter_context(tc.tile_pool(name="early", bufs=1))
         psum = ctx.enter_context(tc.psum_pool(name="psum", bufs=8))
 
         offsets = keep.tile([P, S // 16], U16, name="offsets")
-        tab_scales = keep.tile([P, T], U8, name="tab_scales", tag="area_b", align_bytes=ALIGN)
-        centre_sb = keep.tile([P, GROUPS, PACK], F32, name="centre_sb")
-        gain_sb = keep.tile([P, GROUPS, PACK], F32, name="gain_sb")
-        v_scales = [keep.tile([P, 2, S], U8, name="v_scales%d" % n, align_bytes=ALIGN) for n in range(2)]
+        v_scales = keep.tile([P, K_PASSES, S], U8, name="v_scales", align_bytes=ALIGN)
         picked_scales = keep.tile([P, S], U8, name="picked_scales")
         tab_words = {}
         w1_raw = {}
 
-        def load_w1(area, pieces):
-            raw = keep.tile([P, len(pieces), PACK, PASS], F32, name="w1_raw", tag=area, align_bytes=ALIGN)
-            for i, (b, a) in enumerate(pieces):
-                w1_raw[b, a] = raw[:, i]
-                nc.sync.dma_start(
-                    out=w1_raw[b, a],
-                    in_=w1[a * PASS:(a + 1) * PASS, b * PASS:(b + 1) * PASS].rearrange("(p j) c -> p j c", j=PACK))
+        def load_w1(pool, b, a, offset=None):
+            w1_raw[b, a] = pool.tile([P, PACK, PASS], F32, name="w1_raw%d%d" % (b, a), offset=offset)
+            nc.sync.dma_start(
+                out=w1_raw[b, a][:],
+                in_=w1[a * PASS:(a + 1) * PASS, b * PASS:(b + 1) * PASS].rearrange("(p j) c -> p j c", j=PACK))
 
-        def load_words(area, n):
-            tab_words[n] = keep.tile([P, T], U32, name="tab_words", tag=area, align_bytes=ALIGN)
+        def load_words(pool, n, offset=None):
+            tab_words[n] = pool.tile([P, T], U32, name="tab_words%d" % n, offset=offset)
             nc.sync.dma_start(
                 out=tab_words[n][:].bitcast(I32),
                 in_=tab[n, 0:PASS * T].rearrange("(p x) -> p x", p=P).bitcast(I32))
 
-        def place_scales(n):
-            for q in range(QUADRANTS):
-                nc.sync.dma_start(
-                    out=v_scales[n][32 * q:32 * q + 4, :, :].bitcast(I32),
-                    in_=picked_scales[32 * n + 8 * q:32 * n + 8 * q + 8, :].bitcast(I32))
-
-        v_words = {}
-
-        def pick_words(n):
-            picked = keep.tile([P, S], U32, name="picked%d" % n)
-            nc.vector.tensor_copy(picked[:], tab_words[n][:].indirect(offsets[:]))
-            parted = keep.tile([P, 2, S], U16, name="parted%d" % n, align_bytes=ALIGN)
-            nc.vector.tensor_copy(parted[:], picked[:].bitcast(U16).rearrange("p (j h) -> p h j", h=2))
-            v_words[n] = parted
-
-        w1_grouped = {}
-        w1_mx = {}
-
-        def group_w1(b, a, t0, t1, on_scalar):
-            grouped = ring.tile([P, t1 - t0, P, PACK], BF16, name="w1_grouped", align_bytes=ALIGN, bufs=4)
-            dst = grouped[:].rearrange("p t m j -> p m j t")
-            src = w1_raw[b, a].rearrange("p j (m t) -> p j m t", t=PACK)[:, :, :, t0:t1].rearrange("p j m t -> p m j t")
-            if on_scalar:
-                nc.scalar.copy(out=dst, in_=src)
-            else:
-                nc.vector.tensor_copy(out=dst, in_=src)
-            w1_grouped[b, a, t0] = (grouped, t1)
-
-        def quantise_w1(b, a, t0):
-            grouped, t1 = w1_grouped[b, a, t0]
-            codes = keep.tile([P, (t1 - t0) * P], U32, name="w1_codes%d%d%d" % (b, a, t0), align_bytes=ALIGN)
-            scales = keep.tile([P, (t1 - t0) * P], U8, name="w1_scales%d%d%d" % (b, a, t0), align_bytes=ALIGN)
-            nc.vector.quantize_mx(out=codes[:].bitcast(FP8X4), scales=scales[:],
-                                  in_=grouped[:].rearrange("p t m j -> p (t m j)"))
-            for t in range(t0, t1):
-                cols = slice((t - t0) * P, (t - t0 + 1) * P)
-                w1_mx[b, a, t] = (codes[:, cols], scales[:, cols])
-
-        banks = {}
-
-        def project(b, half):
-            cols = slice(half * BANK, (half + 1) * BANK)
+        nc.sync.dma_start(offsets[:], offs)
+        with tc.tile_pool(name="window", bufs=1) as window:
+            tab_scales = window.tile([P, T], U8, name="tab_scales")
+            for first in (0, 96):
+                nc.vector.memset(tab_scales[first:first + 32, :].bitcast(I32), 0)
+            nc.vector.memset(v_scales[:].rearrange("p a j -> p (a j)").bitcast(I32), 0)
             for a in range(K_PASSES):
                 n, h = divmod(a, 2)
-                for t in range(PACK):
-                    if a == 0:
-                        banks[b, half, t] = psum.tile([P, BANK], F32, name="bank")
-                    codes, scales = w1_mx[b, a, t]
-                    nc.tensor.matmul_mx(
-                        out=banks[b, half, t][:],
-                        lhsT=codes.bitcast(FP8X4), lhsT_scale=scales,
-                        rhs=v_words[n][:, h, cols].bitcast(FP4X4), rhs_scale=v_scales[n][:, h, cols],
-                        start=(a == 0), stop=(a == K_PASSES - 1))
+                nc.sync.dma_start(
+                    out=tab_scales[32 + a:96:K_PASSES, :].bitcast(I32),
+                    in_=tab[n, PASS * T:].rearrange("(h q t) -> h q t", h=2, q=16)[h].bitcast(I32))
+            load_words(keep, 0)
+            load_words(early, 1, 0)
+            centre_sb = keep.tile([P, GROUPS, PACK], F32, name="centre_sb")
+            gain_sb = keep.tile([P, GROUPS, PACK], F32, name="gain_sb")
+            nc.sync.dma_start(out=centre_sb[:], in_=centre.rearrange("(b p t) -> p b t", p=P, t=PACK))
+            nc.sync.dma_start(out=gain_sb[:], in_=gain.rearrange("(b p t) -> p b t", p=P, t=PACK))
+            shift = keep.tile([P, GROUPS, PACK], F32, name="shift")
+            nc.scalar.activation(out=shift[:], in_=centre_sb[:], func=ACT.Copy, scale=-1.0)
+            nc.vector.tensor_copy(picked_scales[:], tab_scales[:].indirect(offsets[:]))
+        for q in range(QUADRANTS):
+            first = 32 + 16 * q
+            nc.sync.dma_start(out=v_scales[32 * q:32 * q + 4, :, :].bitcast(I32),
+                              in_=picked_scales[first:first + 16, :].bitcast(I32))
 
-        def square(sq, b, j0, width):
-            half, c0 = divmod(j0, BANK)
-            for t in range(PACK):
-                nc.scalar.activation(out=sq[:, t, c0:c0 + width], in_=banks[b, half, t][:, c0:c0 + width],
-                                     func=ACT.Square, bias=centre_sb[:, b, t:t + 1], scale=-1.0)
-
-        def bell(sq, c0, width):
-            e = ring.tile([P, PACK, width], F32, name="bell", bufs=4)
-            nc.scalar.activation(out=e[:], in_=sq[:, :, c0:c0 + width], func=ACT.Exp, scale=-1.0)
-            return e
-
-        h_mx = {}
-
-        def bump(e, b, j0, width, parts, held):
-            step = width // parts
-            scaled = []
-            woven = []
-            for c0 in range(0, width, step):
-                if held and c0 > 0:
-                    rounded = keep.tile([P, PACK, step], BF16, name="h_held", tag=held, align_bytes=ALIGN)
-                else:
-                    rounded = ring.tile([P, PACK, step], BF16, name="h_rounded", bufs=3)
-                for t in range(PACK):
-                    nc.vector.tensor_scalar(out=rounded[:, t, :], in0=e[:, t, c0:c0 + step],
-                                            scalar1=gain_sb[:, b, t:t + 1], scalar2=None, op0=ALU.mult)
-                scaled.append(rounded)
-            for rounded in scaled:
-                hb = ring.tile([P, step, PACK], BF16, name="h_woven", align_bytes=ALIGN, bufs=3)
-                nc.vector.tensor_copy(out=hb[:].rearrange("p (c i) t -> p c t i", i=4),
-                                      in_=rounded[:].rearrange("p t (c i) -> p c t i", i=4))
-                woven.append(hb)
-            for i, hb in enumerate(woven):
-                j1 = j0 + i * step
-                codes = keep.tile([P, step], U32, name="h_codes%d_%d" % (b, j1), align_bytes=ALIGN)
-                scales = keep.tile([P, step], U8, name="h_scales%d_%d" % (b, j1), align_bytes=ALIGN)
-                nc.vector.quantize_mx(out=codes[:].bitcast(FP8X4), scales=scales[:],
-                                      in_=hb[:].rearrange("p j t -> p (j t)"))
-                for c in range(0, step, P):
-                    h_mx[b, j1 + c] = (codes[:, c:c + P], scales[:, c:c + P])
-
-        out_rows = out.rearrange("(u p) j -> p u j", p=P)
-
-        def finish(staged, j0, width):
-            acc = psum.tile([P, BANK], F32, name="bank")
-            for u in range(N // P):
-                for c in range(0, width, P):
-                    for b in range(GROUPS):
-                        codes, scales = h_mx[b, j0 + c]
-                        nc.tensor.matmul_mx(
-                            out=acc[:, u * width + c:u * width + c + P],
-                            lhsT=w2w[:, b, 2 * P * u:2 * P * (u + 1)].bitcast(FP4X4),
-                            lhsT_scale=w2s[:, b, P * u:P * (u + 1)],
-                            rhs=codes.bitcast(FP8X4), rhs_scale=scales,
-                            start=(b == 0), stop=(b == GROUPS - 1))
-            rows = staged[:, 2 * j0:2 * (j0 + width)]
-            nc.scalar.copy(out=rows, in_=acc[:, 0:2 * width])
-            nc.sync.dma_start(out=out_rows[:, :, j0:j0 + width], in_=rows.rearrange("p (u j) -> p u j", u=2))
-
-        nc.vector.memset(tab_scales[64:128, :].bitcast(I32), 0)
-        for n in range(2):
-            nc.vector.memset(v_scales[n][:].rearrange("p h j -> p (h j)").bitcast(I32), 0)
-
-        nc.sync.dma_start(offsets[:], offs)
-        for n in range(2):
-            nc.sync.dma_start(
-                out=tab_scales[32 * n:32 * n + 32, :].bitcast(I32),
-                in_=tab[n, PASS * T:].rearrange("(h q t) -> q h t", h=2, q=16).bitcast(I32))
-        load_w1("area_c", [(0, 0)])
-        load_words("area_a", 0)
-        load_w1("area_e", [(0, 1)])
-        nc.gpsimd.dma_start(out=centre_sb[:], in_=centre.rearrange("(b p t) -> p b t", p=P, t=PACK))
-        nc.gpsimd.dma_start(out=gain_sb[:], in_=gain.rearrange("(b p t) -> p b t", p=P, t=PACK))
-
-        nc.vector.tensor_copy(picked_scales[:], tab_scales[:].indirect(offsets[:]))
-        place_scales(0)
-        load_words("area_b", 1)
-        place_scales(1)
-
-        group_w1(0, 0, 0, 4, True)
-        load_w1("area_c", [(0, 2)])
-        quantise_w1(0, 0, 0)
-        pick_words(0)
-        load_w1("area_a", [(0, 3), (1, 0)])
-        group_w1(0, 1, 0, 4, True)
-        load_w1("area_e", [(1, 1)])
-        quantise_w1(0, 1, 0)
-        pick_words(1)
-        load_w1("area_b", [(1, 2), (1, 3)])
-        group_w1(0, 2, 0, 2, True)
-        group_w1(0, 2, 2, 4, True)
-        group_w1(0, 3, 2, 4, True)
-        quantise_w1(0, 2, 0)
-        group_w1(0, 3, 0, 2, False)
-        quantise_w1(0, 2, 2)
-        quantise_w1(0, 3, 0)
-        quantise_w1(0, 3, 2)
-        project(0, 0)
-        project(0, 1)
-        sq = ring.tile([P, PACK, BANK], F32, name="sq")
-        square(sq, 0, 0, BANK)
-
+        late = ctx.enter_context(tc.tile_pool(name="late", bufs=1))
+        RAW = 4 * PACK * PASS
+        small = 8 * RAW
         for a in range(K_PASSES):
-            group_w1(1, a, 0, 2, False)
-            group_w1(1, a, 2, 4, False)
-            quantise_w1(1, a, 0)
-            quantise_w1(1, a, 2)
-
-        w2w = keep.tile([P, GROUPS, 2 * N], U8, name="w2w", tag="area_a", align_bytes=ALIGN)
+            load_w1(late, 0, a, a * RAW)
+        for a in range(K_PASSES):
+            load_w1(late, 1, a, (4 + a) * RAW)
+        w2w = late.tile([P, GROUPS, 2 * N], U8, name="w2w", align_bytes=ALIGN, offset=small + 128)
         nc.sync.dma_start(out=w2w[:].bitcast(I32), in_=w2_words.rearrange("a p c -> p a c").bitcast(I32))
-        w2s = keep.tile([P, GROUPS, N], U8, name="w2s", tag="area_e", align_bytes=ALIGN)
+        w2s = late.tile([P, GROUPS, N], U8, name="w2s", align_bytes=ALIGN, offset=small + 128 + 4 * N)
         nc.vector.memset(w2s[:].rearrange("p a c -> p (a c)").bitcast(I32), 0)
         for q in range(QUADRANTS):
             nc.sync.dma_start(
                 out=w2s[32 * q:32 * q + 4, :, :].bitcast(I32),
                 in_=w2_scales[:, 4 * q:4 * q + 4, :].rearrange("a r c -> r a c").bitcast(I32))
 
-        first_bell = bell(sq, 0, BANK)
-        sq = ring.tile([P, PACK, BANK], F32, name="sq")
-        square(sq, 0, BANK, BANK)
-        second_bell = bell(sq, 0, BANK)
-        project(1, 0)
-        project(1, 1)
-        bump(first_bell, 0, 0, BANK, 2, "area_b")
-        bump(second_bell, 0, BANK, BANK, 2, None)
-        sq = ring.tile([P, PACK, BANK], F32, name="sq")
-        square(sq, 1, 0, BANK)
-        bump(bell(sq, 0, BANK), 1, 0, BANK, 2, None)
+        v_words = {}
+        picked = keep.tile([P, S], U32, name="picked")
+        for n in range(2):
+            nc.vector.tensor_copy(picked[:], tab_words[n][:].indirect(offsets[:]))
+            v_words[n] = keep.tile([P, 2, S], U16, name="parted%d" % n, align_bytes=ALIGN)
+            nc.vector.tensor_copy(v_words[n][:], picked[:].bitcast(U16).rearrange("p (j h) -> p h j", h=2))
+        stage = early.tile([P, PACK * PASS], BF16, name="stage", align_bytes=ALIGN, offset=0)
 
-        sq = keep.tile([P, PACK, BANK], F32, name="sq_last", tag="area_d")
-        square(sq, 1, BANK, CHUNK)
-        bump(bell(sq, 0, CHUNK), 1, BANK, CHUNK, 2, None)
-        square(sq, 1, BANK + CHUNK, CHUNK)
-        last_bells = [bell(sq, c0, P) for c0 in range(CHUNK, BANK, P)]
-        for i, e in enumerate(last_bells):
-            bump(e, 1, BANK + CHUNK + i * P, P, 1, None)
-        staged = keep.tile([P, 2 * S], F32, name="staged", tag="area_d")
+        w1_grouped = {}
+        w1_mx = {}
+
+        def group_w1(b, a, t0, t1, on_scalar, place):
+            grouped = stage[:, place * PASS:(place + t1 - t0) * PASS]
+            dst = grouped.rearrange("p (t m j) -> p m j t", m=P, j=PACK)
+            src = w1_raw[b, a][:].rearrange("p j (m t) -> p j m t", t=PACK)[:, :, :, t0:t1].rearrange("p j m t -> p m j t")
+            if on_scalar:
+                nc.scalar.activation(out=dst, in_=src, func=ACT.Copy)
+            else:
+                nc.vector.tensor_copy(out=dst, in_=src)
+            w1_grouped[b, a, t0] = (grouped, t1)
+
+        def quantise_w1(b, a, t0, pool=keep, offset=None):
+            grouped, t1 = w1_grouped[b, a, t0]
+            codes = pool.tile([P, (t1 - t0) * P], U32, name="w1_codes%d%d%d" % (b, a, t0), align_bytes=ALIGN, offset=offset)
+            scales = keep.tile([P, (t1 - t0) * P], U8, name="w1_scales%d%d%d" % (b, a, t0), align_bytes=ALIGN)
+            nc.vector.quantize_mx(out=codes[:].bitcast(FP8X4), scales=scales[:],
+                                  in_=grouped)
+            for t in range(t0, t1):
+                cols = slice((t - t0) * P, (t - t0 + 1) * P)
+                w1_mx[b, a, t] = (codes[:, cols], scales[:, cols])
+
+        banks = {}
+
+        def project(b, half, steps):
+            cols = slice(half * BANK, (half + 1) * BANK)
+            done = [0] * PACK
+            for a, t in steps:
+                n, h = divmod(a, 2)
+                if done[t] == 0:
+                    banks[b, half, t] = psum.tile([P, BANK], F32, name="bank")
+                codes, scales = w1_mx[b, a, t]
+                nc.tensor.matmul_mx(
+                    out=banks[b, half, t][:],
+                    lhsT=codes.bitcast(FP8X4), lhsT_scale=scales,
+                    rhs=v_words[n][:, h, cols].bitcast(FP4X4), rhs_scale=v_scales[:, a, cols],
+                    start=(done[t] == 0), stop=(done[t] == K_PASSES - 1))
+                done[t] = done[t] + 1
+
+        def as_loaded(passes):
+            return [(a, t) for a in passes for t in range(PACK)]
+
+        def by_tile(passes):
+            return [(a, t) for t in range(PACK) for a in passes]
+
+        def square(b, j0, width):
+            half, c0 = divmod(j0, BANK)
+            sq = ring.tile([P, PACK, width], F32, name="sq", bufs=2)
+            for t in range(PACK):
+                nc.scalar.activation(out=sq[:, t, :], in_=banks[b, half, t][:, c0:c0 + width],
+                                     func=ACT.Square, bias=shift[:, b, t:t + 1])
+            return sq
+
+        bells = {}
+
+        def bell(sq, b, j0, c0, width):
+            e = ring.tile([P, PACK, width], F32, name="bell", tag="bell%d" % width, bufs=(1 if width == BANK else 3))
+            nc.scalar.activation(out=e[:], in_=sq[:, :, c0:c0 + width], func=ACT.Exp, scale=-1.0)
+            bells[b, j0 + c0] = (e, width)
+
+        h_mx = {}
+
+        woven = {}
+
+        def weave(b, j0, hb=None):
+            e, width = bells[b, j0]
+            if hb is None:
+                hb = ring.tile([P, width * PACK], BF16, name="h_woven", align_bytes=ALIGN, bufs=3)[:]
+            nc.vector.tensor_tensor(
+                out=hb.rearrange("p (c i t) -> p c t i", i=2, t=PACK),
+                in0=e[:].rearrange("p t (c i) -> p c t i", i=2),
+                in1=gain_sb[:, b, :].unsqueeze(1).unsqueeze(3).to_broadcast([P, width // 2, PACK, 2]),
+                op=ALU.mult)
+            woven[b, j0] = (hb, width)
+
+        def quantise_h(b, j0):
+            hb, width = woven[b, j0]
+            codes = keep.tile([P, width], U32, name="h_codes%d_%d" % (b, j0), align_bytes=ALIGN)
+            scales = keep.tile([P, width], U8, name="h_scales%d_%d" % (b, j0), align_bytes=ALIGN)
+            nc.vector.quantize_mx(out=codes[:].bitcast(FP8X4), scales=scales[:], in_=hb)
+            for c in range(0, width, P):
+                h_mx[b, j0 + c] = (codes, scales, c)
+
+        out_rows = out.rearrange("(u p) j -> p u j", p=P)
+
+        def finish(j0, width, on_scalar):
+            acc = psum.tile([P, BANK], F32, name="bank")
+            for u in range(N // P):
+                for b in range(GROUPS):
+                    codes, scales, c = h_mx[b, j0]
+                    nc.tensor.matmul_mx(
+                        out=acc[:, u * width:(u + 1) * width],
+                        lhsT=w2w[:, b, 2 * P * u:2 * P * (u + 1)].bitcast(FP4X4),
+                        lhsT_scale=w2s[:, b, P * u:P * (u + 1)],
+                        rhs=codes[:, c:c + width].bitcast(FP8X4), rhs_scale=scales[:, c:c + width],
+                        start=(b == 0), stop=(b == GROUPS - 1))
+            staged = keep.tile([P, 2 * width], F32, name="staged%d" % j0)
+            if on_scalar:
+                nc.scalar.copy(out=staged[:], in_=acc[:, 0:2 * width])
+            else:
+                nc.vector.tensor_copy(out=staged[:], in_=acc[:, 0:2 * width])
+            nc.sync.dma_start(out=out_rows[:, :, j0:j0 + width], in_=staged[:].rearrange("p (u j) -> p u j", u=2))
+
+        for a in range(K_PASSES):
+            group_w1(0, a, 0, 2, False, 2 * (a % 2))
+            group_w1(0, a, 2, 4, True, 2 - 2 * (a % 2))
+            quantise_w1(0, a, 0)
+            quantise_w1(0, a, 2)
+        project(0, 0, as_loaded(range(4)))
+        project(0, 1, as_loaded([0]) + by_tile([3, 1, 2]))
+        for j0 in (0, CHUNK):
+            bell(square(0, j0, CHUNK), 0, j0, 0, CHUNK)
+        bell(square(0, BANK, BANK), 0, BANK, 0, BANK)
+
+        for a in range(K_PASSES):
+            group_w1(1, a, 0, 2, False, 0)
+            group_w1(1, a, 2, 4, False, 2)
+            quantise_w1(1, a, 0)
+            quantise_w1(1, a, 2)
+            if a == 1:
+                weave(0, 0, stage[:, 0:PACK * CHUNK])
+                quantise_h(0, 0)
+        project(1, 0, as_loaded(range(4)))
+        project(1, 1, by_tile([3, 0, 1, 2]))
+        held = late.tile([P, PACK * (S - CHUNK)], BF16, name="held", align_bytes=ALIGN, offset=7 * RAW)
+        weave(0, CHUNK, held[:, 0:PACK * CHUNK])
+        weave(0, BANK, held[:, PACK * CHUNK:])
+        quantise_h(0, CHUNK)
+        quantise_h(0, BANK)
+        sq = square(1, 0, BANK)
+        for c0 in (0, CHUNK):
+            bell(sq, 1, 0, c0, CHUNK)
+        bell(square(1, BANK, CHUNK), 1, BANK, 0, CHUNK)
+        sq = square(1, BANK + CHUNK, CHUNK)
+        for c0 in (0, P):
+            bell(sq, 1, BANK + CHUNK, c0, P)
+        for j0 in (0, CHUNK, BANK, BANK + CHUNK, S - P):
+            weave(1, j0)
+            quantise_h(1, j0)
         for j0 in range(0, S - CHUNK, CHUNK):
-            finish(staged, j0, CHUNK)
-        for j0 in range(S - CHUNK, S, P):
-            finish(staged, j0, P)
+            finish(j0, CHUNK, True)
+        finish(S - CHUNK, P, False)
+        finish(S - P, P, False)

@@ -1,6 +1,7 @@
 from contextlib import ExitStack
 
 import concourse.mybir as mybir
+from concourse.masks import make_identity
 
 K, T, S, H, N = 2048, 4096, 1024, 1024, 256
 FLOPS = 2 * K * H * S + 2 * H * N * S
@@ -66,12 +67,18 @@ def tile_list_redshift_gaussian_bumps_kernel(tc, tab, offs, w1, centre, gain, w2
                     in_=tab[n, PASS * T:].rearrange("(h q t) -> h q t", h=2, q=16)[h].bitcast(I32))
             load_words(keep, 0)
             load_words(early, 1, 0)
-            centre_sb = keep.tile([P, GROUPS, PACK], F32, name="centre_sb")
-            gain_sb = keep.tile([P, GROUPS, PACK], F32, name="gain_sb")
-            nc.sync.dma_start(out=centre_sb[:], in_=centre.rearrange("(b p t) -> p b t", p=P, t=PACK))
-            nc.sync.dma_start(out=gain_sb[:], in_=gain.rearrange("(b p t) -> p b t", p=P, t=PACK))
-            shift = keep.tile([P, GROUPS, PACK], F32, name="shift")
-            nc.scalar.activation(out=shift[:], in_=centre_sb[:], func=ACT.Copy, scale=-1.0)
+            rows = keep.tile([P, PASS], F32, name="rows")
+            nc.gpsimd.memset(rows[:], 0.0)
+            nc.sync.dma_start(out=rows[0:GROUPS, :], in_=centre.rearrange("(b c) -> b c", b=GROUPS))
+            nc.sync.dma_start(out=rows[GROUPS:2 * GROUPS, :], in_=gain.rearrange("(b c) -> b c", b=GROUPS))
+            identity = keep.tile([P, P], F32, name="identity")
+            make_identity(nc, identity[:])
+            turned = psum.tile([P, BANK], F32, name="bank")
+            for t in range(PACK):
+                nc.tensor.transpose(turned[:, t * P:(t + 1) * P], rows[:, t::PACK], identity[:])
+            consts = keep.tile([P, PACK, 2 * GROUPS], F32, name="consts")
+            nc.scalar.activation(out=consts[:], in_=turned[:].rearrange("p (t c) -> p t c", t=PACK)[:, :, 0:2 * GROUPS],
+                                 func=ACT.Copy)
             nc.vector.tensor_copy(picked_scales[:], tab_scales[:].indirect(offsets[:]))
         for q in range(QUADRANTS):
             first = 32 + 16 * q
@@ -148,18 +155,20 @@ def tile_list_redshift_gaussian_bumps_kernel(tc, tab, offs, w1, centre, gain, w2
         def by_tile(passes):
             return [(a, t) for t in range(PACK) for a in passes]
 
-        def square(b, j0, width):
+        def square(b, j0, width, sq=None):
             half, c0 = divmod(j0, BANK)
-            sq = ring.tile([P, PACK, width], F32, name="sq", bufs=2)
+            if sq is None:
+                sq = ring.tile([P, PACK, width], F32, name="sq", bufs=2)
             for t in range(PACK):
                 nc.scalar.activation(out=sq[:, t, :], in_=banks[b, half, t][:, c0:c0 + width],
-                                     func=ACT.Square, bias=shift[:, b, t:t + 1])
+                                     func=ACT.Square, bias=consts[:, t, b:b + 1], scale=-1.0)
             return sq
 
         bells = {}
 
-        def bell(sq, b, j0, c0, width):
-            e = ring.tile([P, PACK, width], F32, name="bell", tag="bell%d" % width, bufs=(1 if width == BANK else 3))
+        def bell(sq, b, j0, c0, width, e=None):
+            if e is None:
+                e = ring.tile([P, PACK, width], F32, name="bell", tag="bell%d" % width, bufs=(1 if width == BANK else 3))
             nc.scalar.activation(out=e[:], in_=sq[:, :, c0:c0 + width], func=ACT.Exp, scale=-1.0)
             bells[b, j0 + c0] = (e, width)
 
@@ -174,13 +183,14 @@ def tile_list_redshift_gaussian_bumps_kernel(tc, tab, offs, w1, centre, gain, w2
             nc.vector.tensor_tensor(
                 out=hb.rearrange("p (c i t) -> p c t i", i=2, t=PACK),
                 in0=e[:].rearrange("p t (c i) -> p c t i", i=2),
-                in1=gain_sb[:, b, :].unsqueeze(1).unsqueeze(3).to_broadcast([P, width // 2, PACK, 2]),
+                in1=consts[:, :, GROUPS + b].unsqueeze(1).unsqueeze(3).to_broadcast([P, width // 2, PACK, 2]),
                 op=ALU.mult)
             woven[b, j0] = (hb, width)
 
-        def quantise_h(b, j0):
+        def quantise_h(b, j0, codes=None):
             hb, width = woven[b, j0]
-            codes = keep.tile([P, width], U32, name="h_codes%d_%d" % (b, j0), align_bytes=ALIGN)
+            if codes is None:
+                codes = keep.tile([P, width], U32, name="h_codes%d_%d" % (b, j0), align_bytes=ALIGN)
             scales = keep.tile([P, width], U8, name="h_scales%d_%d" % (b, j0), align_bytes=ALIGN)
             nc.vector.quantize_mx(out=codes[:].bitcast(FP8X4), scales=scales[:], in_=hb)
             for c in range(0, width, P):
@@ -188,23 +198,23 @@ def tile_list_redshift_gaussian_bumps_kernel(tc, tab, offs, w1, centre, gain, w2
 
         out_rows = out.rearrange("(u p) j -> p u j", p=P)
 
-        def finish(j0, width, on_scalar):
+        def finish(j0, width, on_scalar, staged):
             acc = psum.tile([P, BANK], F32, name="bank")
-            for u in range(N // P):
-                for b in range(GROUPS):
+            for b in range(GROUPS):
+                for u in range(N // P):
                     codes, scales, c = h_mx[b, j0]
                     nc.tensor.matmul_mx(
                         out=acc[:, u * width:(u + 1) * width],
                         lhsT=w2w[:, b, 2 * P * u:2 * P * (u + 1)].bitcast(FP4X4),
                         lhsT_scale=w2s[:, b, P * u:P * (u + 1)],
                         rhs=codes[:, c:c + width].bitcast(FP8X4), rhs_scale=scales[:, c:c + width],
-                        start=(b == 0), stop=(b == GROUPS - 1))
-            staged = keep.tile([P, 2 * width], F32, name="staged%d" % j0)
+                        start=(b == 0 and u == 0), stop=(b == GROUPS - 1 and u == N // P - 1))
             if on_scalar:
-                nc.scalar.copy(out=staged[:], in_=acc[:, 0:2 * width])
+                nc.scalar.copy(out=staged, in_=acc[:, 0:2 * width])
             else:
-                nc.vector.tensor_copy(out=staged[:], in_=acc[:, 0:2 * width])
-            nc.sync.dma_start(out=out_rows[:, :, j0:j0 + width], in_=staged[:].rearrange("p (u j) -> p u j", u=2))
+                for c0 in range(0, 2 * width, CHUNK):
+                    nc.vector.tensor_copy(out=staged[:, c0:c0 + CHUNK], in_=acc[:, c0:c0 + CHUNK])
+            nc.sync.dma_start(out=out_rows[:, :, j0:j0 + width], in_=staged.rearrange("p (u j) -> p u j", u=2))
 
         for a in range(K_PASSES):
             group_w1(0, a, 0, 2, False, 2 * (a % 2))
@@ -212,9 +222,10 @@ def tile_list_redshift_gaussian_bumps_kernel(tc, tab, offs, w1, centre, gain, w2
             quantise_w1(0, a, 0)
             quantise_w1(0, a, 2)
         project(0, 0, as_loaded(range(4)))
-        project(0, 1, as_loaded([0]) + by_tile([3, 1, 2]))
-        for j0 in (0, CHUNK):
-            bell(square(0, j0, CHUNK), 0, j0, 0, CHUNK)
+        project(0, 1, by_tile([3, 0, 1, 2]))
+        sq = square(0, 0, BANK)
+        for c0 in (0, CHUNK):
+            bell(sq, 0, 0, c0, CHUNK)
         bell(square(0, BANK, BANK), 0, BANK, 0, BANK)
 
         for a in range(K_PASSES):
@@ -236,13 +247,18 @@ def tile_list_redshift_gaussian_bumps_kernel(tc, tab, offs, w1, centre, gain, w2
         for c0 in (0, CHUNK):
             bell(sq, 1, 0, c0, CHUNK)
         bell(square(1, BANK, CHUNK), 1, BANK, 0, CHUNK)
-        sq = square(1, BANK + CHUNK, CHUNK)
-        for c0 in (0, P):
-            bell(sq, 1, BANK + CHUNK, c0, P)
-        for j0 in (0, CHUNK, BANK, BANK + CHUNK, S - P):
-            weave(1, j0)
-            quantise_h(1, j0)
-        for j0 in range(0, S - CHUNK, CHUNK):
-            finish(j0, CHUNK, True)
-        finish(S - CHUNK, P, False)
-        finish(S - P, P, False)
+        bell(square(1, S - CHUNK, P), 1, S - CHUNK, 0, P)
+        bell(square(1, S - P, P, late.tile([P, PACK, P], F32, name="sq_last", offset=0)), 1, S - P, 0, P)
+        for pair in ((0, CHUNK), (BANK,), (S - CHUNK,), (S - P,)):
+            for j0 in pair:
+                weave(1, j0)
+            for j0 in pair:
+                quantise_h(1, j0)
+        staged = late.tile([P, 6 * CHUNK], F32, name="staged", offset=0)
+        staged_first = keep.tile([P, 2 * CHUNK], F32, name="staged_first")
+        finish(0, CHUNK, False, staged_first[:])
+        finish(CHUNK, CHUNK, True, staged[:, 0:2 * CHUNK])
+        finish(BANK, CHUNK, True, staged[:, 2 * CHUNK:4 * CHUNK])
+        staged_last = staged[:, 4 * CHUNK:]
+        finish(S - CHUNK, P, True, staged_last[:, 0:CHUNK])
+        finish(S - P, P, False, staged_last[:, CHUNK:])

@@ -76,8 +76,8 @@ def tile_list_redshift_gaussian_bumps_kernel(tc, tab, offs, w1, centre, gain, w2
             turned = psum.tile([P, BANK], F32, name="bank")
             for t in range(PACK):
                 nc.tensor.transpose(turned[:, t * P:(t + 1) * P], rows[:, t::PACK], identity[:])
-            consts = keep.tile([P, PACK, 2 * GROUPS], F32, name="consts")
-            nc.scalar.activation(out=consts[:], in_=turned[:].rearrange("p (t c) -> p t c", t=PACK)[:, :, 0:2 * GROUPS],
+            consts = keep.tile([P, 2 * GROUPS, PACK], F32, name="consts")
+            nc.scalar.activation(out=consts[:], in_=turned[:].rearrange("p (t c) -> p c t", t=PACK)[:, 0:2 * GROUPS, :],
                                  func=ACT.Copy)
             nc.vector.tensor_copy(picked_scales[:], tab_scales[:].indirect(offsets[:]))
         for q in range(QUADRANTS):
@@ -161,7 +161,7 @@ def tile_list_redshift_gaussian_bumps_kernel(tc, tab, offs, w1, centre, gain, w2
                 sq = ring.tile([P, PACK, width], F32, name="sq", bufs=2)
             for t in range(PACK):
                 nc.scalar.activation(out=sq[:, t, :], in_=banks[b, half, t][:, c0:c0 + width],
-                                     func=ACT.Square, bias=consts[:, t, b:b + 1], scale=-1.0)
+                                     func=ACT.Square, bias=consts[:, b, t:t + 1], scale=-1.0)
             return sq
 
         bells = {}
@@ -183,7 +183,7 @@ def tile_list_redshift_gaussian_bumps_kernel(tc, tab, offs, w1, centre, gain, w2
             nc.vector.tensor_tensor(
                 out=hb.rearrange("p (c i t) -> p c t i", i=2, t=PACK),
                 in0=e[:].rearrange("p t (c i) -> p c t i", i=2),
-                in1=consts[:, :, GROUPS + b].unsqueeze(1).unsqueeze(3).to_broadcast([P, width // 2, PACK, 2]),
+                in1=consts[:, GROUPS + b, :].unsqueeze(1).unsqueeze(3).to_broadcast([P, width // 2, PACK, 2]),
                 op=ALU.mult)
             woven[b, j0] = (hb, width)
 

@@ -80,7 +80,7 @@ def tile_list_redshift_gaussian_bumps_kernel(tc, tab, offs, w1, centre, gain, w2
             nc.scalar.activation(out=consts[:], in_=turned[:].rearrange("p (t c) -> p c t", t=PACK)[:, 0:2 * GROUPS, :],
                                  func=ACT.Copy)
             nc.vector.tensor_copy(picked_scales[:], tab_scales[:].indirect(offsets[:]))
-        for q in range(QUADRANTS):
+        for q in (0, 2, 1, 3):
             first = 32 + 16 * q
             nc.sync.dma_start(out=v_scales[32 * q:32 * q + 4, :, :].bitcast(I32),
                               in_=picked_scales[first:first + 16, :].bitcast(I32))
@@ -228,14 +228,21 @@ def tile_list_redshift_gaussian_bumps_kernel(tc, tab, offs, w1, centre, gain, w2
             bell(sq, 0, 0, c0, CHUNK)
         bell(square(0, BANK, BANK), 0, BANK, 0, BANK)
 
-        for a in range(K_PASSES):
+        for a in range(2):
             group_w1(1, a, 0, 2, False, 0)
             group_w1(1, a, 2, 4, False, 2)
             quantise_w1(1, a, 0)
             quantise_w1(1, a, 2)
-            if a == 1:
-                weave(0, 0, stage[:, 0:PACK * CHUNK])
-                quantise_h(0, 0)
+        weave(0, 0, stage[:, 0:PACK * CHUNK])
+        group_w1(1, 2, 0, 2, False, 2)
+        quantise_h(0, 0)
+        group_w1(1, 2, 2, 4, False, 0)
+        quantise_w1(1, 2, 0)
+        quantise_w1(1, 2, 2)
+        group_w1(1, 3, 0, 2, False, 0)
+        group_w1(1, 3, 2, 4, False, 2)
+        quantise_w1(1, 3, 0)
+        quantise_w1(1, 3, 2)
         project(1, 0, as_loaded(range(4)))
         project(1, 1, by_tile([3, 0, 1, 2]))
         held = late.tile([P, PACK * (S - CHUNK)], BF16, name="held", align_bytes=ALIGN, offset=7 * RAW)
@@ -248,17 +255,37 @@ def tile_list_redshift_gaussian_bumps_kernel(tc, tab, offs, w1, centre, gain, w2
             bell(sq, 1, 0, c0, CHUNK)
         bell(square(1, BANK, CHUNK), 1, BANK, 0, CHUNK)
         bell(square(1, S - CHUNK, P), 1, S - CHUNK, 0, P)
-        bell(square(1, S - P, P, late.tile([P, PACK, P], F32, name="sq_last", offset=0)), 1, S - P, 0, P)
-        for pair in ((0, CHUNK), (BANK,), (S - CHUNK,), (S - P,)):
+        sq = square(1, S - P, P, late.tile([P, PACK, P], F32, name="sq_last", offset=0))
+        for c0 in (0, P // 2):
+            bell(sq, 1, S - P, c0, P // 2)
+        for pair in ((0, CHUNK), (BANK,), (S - CHUNK,)):
             for j0 in pair:
                 weave(1, j0)
             for j0 in pair:
                 quantise_h(1, j0)
+        last = keep.tile([P, PASS], BF16, name="last", align_bytes=ALIGN)
+        for c0 in (0, P // 2):
+            weave(1, S - P + c0, last[:, PACK * c0:PACK * (c0 + P // 2)])
+        woven[1, S - P] = (last[:], P)
+        quantise_h(1, S - P)
         staged = late.tile([P, 6 * CHUNK], F32, name="staged", offset=0)
         staged_first = keep.tile([P, 2 * CHUNK], F32, name="staged_first")
-        finish(0, CHUNK, False, staged_first[:])
+        finish(0, CHUNK, True, staged_first[:])
         finish(CHUNK, CHUNK, True, staged[:, 0:2 * CHUNK])
         finish(BANK, CHUNK, True, staged[:, 2 * CHUNK:4 * CHUNK])
         staged_last = staged[:, 4 * CHUNK:]
         finish(S - CHUNK, P, True, staged_last[:, 0:CHUNK])
-        finish(S - P, P, False, staged_last[:, CHUNK:])
+        accs = [psum.tile([P, BANK], F32, name="bank") for u in range(N // P)]
+        for b in range(GROUPS):
+            for u in range(N // P):
+                codes, scales, c = h_mx[b, S - P]
+                nc.tensor.matmul_mx(
+                    out=accs[u][:, 0:P],
+                    lhsT=w2w[:, b, 2 * P * u:2 * P * (u + 1)].bitcast(FP4X4),
+                    lhsT_scale=w2s[:, b, P * u:P * (u + 1)],
+                    rhs=codes[:, c:c + P].bitcast(FP8X4), rhs_scale=scales[:, c:c + P],
+                    start=(b == 0), stop=(b == GROUPS - 1))
+        nc.scalar.copy(out=staged_last[:, CHUNK:CHUNK + P], in_=accs[0][:, 0:P])
+        nc.scalar.dma_start(out=out_rows[:, 0, S - P:S], in_=staged_last[:, CHUNK:CHUNK + P])
+        nc.vector.tensor_copy(out=staged_last[:, CHUNK + P:], in_=accs[1][:, 0:P])
+        nc.sync.dma_start(out=out_rows[:, 1, S - P:S], in_=staged_last[:, CHUNK + P:])

@@ -222,7 +222,7 @@ def tile_list_redshift_gaussian_bumps_kernel(tc, tab, offs, w1, centre, gain, w2
             quantise_w1(0, a, 0)
             quantise_w1(0, a, 2)
         project(0, 0, as_loaded(range(4)))
-        project(0, 1, by_tile([3, 0, 1, 2]))
+        project(0, 1, as_loaded([0]) + by_tile([3, 1, 2]))
         sq = square(0, 0, BANK)
         for c0 in (0, CHUNK):
             bell(sq, 0, 0, c0, CHUNK)
@@ -244,7 +244,7 @@ def tile_list_redshift_gaussian_bumps_kernel(tc, tab, offs, w1, centre, gain, w2
         quantise_w1(1, 3, 0)
         quantise_w1(1, 3, 2)
         project(1, 0, as_loaded(range(4)))
-        project(1, 1, by_tile([3, 0, 1, 2]))
+        project(1, 1, as_loaded([0]) + by_tile([3, 1, 2]))
         held = late.tile([P, PACK * (S - CHUNK)], BF16, name="held", align_bytes=ALIGN, offset=7 * RAW)
         weave(0, CHUNK, held[:, 0:PACK * CHUNK])
         weave(0, BANK, held[:, PACK * CHUNK:])

@@ -269,23 +269,8 @@ def tile_list_redshift_gaussian_bumps_kernel(tc, tab, offs, w1, centre, gain, w2
         woven[1, S - P] = (last[:], P)
         quantise_h(1, S - P)
         staged = late.tile([P, 6 * CHUNK], F32, name="staged", offset=0)
-        staged_first = keep.tile([P, 2 * CHUNK], F32, name="staged_first")
-        finish(0, CHUNK, True, staged_first[:])
-        finish(CHUNK, CHUNK, True, staged[:, 0:2 * CHUNK])
-        finish(BANK, CHUNK, True, staged[:, 2 * CHUNK:4 * CHUNK])
-        staged_last = staged[:, 4 * CHUNK:]
-        finish(S - CHUNK, P, True, staged_last[:, 0:CHUNK])
-        accs = [psum.tile([P, BANK], F32, name="bank") for u in range(N // P)]
-        for b in range(GROUPS):
-            for u in range(N // P):
-                codes, scales, c = h_mx[b, S - P]
-                nc.tensor.matmul_mx(
-                    out=accs[u][:, 0:P],
-                    lhsT=w2w[:, b, 2 * P * u:2 * P * (u + 1)].bitcast(FP4X4),
-                    lhsT_scale=w2s[:, b, P * u:P * (u + 1)],
-                    rhs=codes[:, c:c + P].bitcast(FP8X4), rhs_scale=scales[:, c:c + P],
-                    start=(b == 0), stop=(b == GROUPS - 1))
-        nc.scalar.copy(out=staged_last[:, CHUNK:CHUNK + P], in_=accs[0][:, 0:P])
-        nc.scalar.dma_start(out=out_rows[:, 0, S - P:S], in_=staged_last[:, CHUNK:CHUNK + P])
-        nc.vector.tensor_copy(out=staged_last[:, CHUNK + P:], in_=accs[1][:, 0:P])
-        nc.sync.dma_start(out=out_rows[:, 1, S - P:S], in_=staged_last[:, CHUNK + P:])
+        for j0 in range(0, S - CHUNK, CHUNK):
+            finish(j0, CHUNK, True, staged[:, 2 * j0:2 * (j0 + CHUNK)])
+        staged_last = keep.tile([P, 2 * CHUNK], F32, name="staged_last")
+        finish(S - CHUNK, P, False, staged_last[:, 0:CHUNK])
+        finish(S - P, P, False, staged_last[:, CHUNK:])

@@ -57,6 +57,8 @@ def tile_list_redshift_gaussian_bumps_kernel(tc, tab, offs, w1, centre, gain, w2
         nc.sync.dma_start(offsets[:], offs)
         with tc.tile_pool(name="window", bufs=1) as window:
             tab_scales = window.tile([P, T], U8, name="tab_scales")
+            rows = keep.tile([P, PASS], F32, name="rows")
+            nc.vector.memset(rows[:], 0.0)
             for first in (0, 96):
                 nc.vector.memset(tab_scales[first:first + 32, :].bitcast(I32), 0)
             nc.vector.memset(v_scales[:].rearrange("p a j -> p (a j)").bitcast(I32), 0)
@@ -66,11 +68,9 @@ def tile_list_redshift_gaussian_bumps_kernel(tc, tab, offs, w1, centre, gain, w2
                     out=tab_scales[32 + a:96:K_PASSES, :].bitcast(I32),
                     in_=tab[n, PASS * T:].rearrange("(h q t) -> h q t", h=2, q=16)[h].bitcast(I32))
             load_words(keep, 0)
-            load_words(early, 1, 0)
-            rows = keep.tile([P, PASS], F32, name="rows")
-            nc.gpsimd.memset(rows[:], 0.0)
             nc.sync.dma_start(out=rows[0:GROUPS, :], in_=centre.rearrange("(b c) -> b c", b=GROUPS))
             nc.sync.dma_start(out=rows[GROUPS:2 * GROUPS, :], in_=gain.rearrange("(b c) -> b c", b=GROUPS))
+            load_words(early, 1, 0)
             identity = keep.tile([P, P], F32, name="identity")
             make_identity(nc, identity[:])
             turned = psum.tile([P, BANK], F32, name="bank")

@@ -209,12 +209,15 @@ def tile_list_redshift_gaussian_bumps_kernel(tc, tab, offs, w1, centre, gain, w2
                         lhsT_scale=w2s[:, b, P * u:P * (u + 1)],
                         rhs=codes[:, c:c + width].bitcast(FP8X4), rhs_scale=scales[:, c:c + width],
                         start=(b == 0 and u == 0), stop=(b == GROUPS - 1 and u == N // P - 1))
-            if on_scalar:
-                nc.scalar.copy(out=staged, in_=acc[:, 0:2 * width])
-            else:
-                for c0 in range(0, 2 * width, CHUNK):
-                    nc.vector.tensor_copy(out=staged[:, c0:c0 + CHUNK], in_=acc[:, c0:c0 + CHUNK])
-            nc.sync.dma_start(out=out_rows[:, :, j0:j0 + width], in_=staged.rearrange("p (u j) -> p u j", u=2))
+            step = 2 // len(staged)
+            for i, part in enumerate(staged):
+                source = acc[:, i * step * width:(i + 1) * step * width]
+                if on_scalar:
+                    nc.scalar.copy(out=part, in_=source)
+                else:
+                    nc.vector.tensor_copy(out=part, in_=source)
+                nc.sync.dma_start(out=out_rows[:, i * step:(i + 1) * step, j0:j0 + width],
+                                  in_=part.rearrange("p (u j) -> p u j", u=step))
 
         for a in range(K_PASSES):
             group_w1(0, a, 0, 2, False, 2 * (a % 2))
@@ -254,23 +257,28 @@ def tile_list_redshift_gaussian_bumps_kernel(tc, tab, offs, w1, centre, gain, w2
         for c0 in (0, CHUNK):
             bell(sq, 1, 0, c0, CHUNK)
         bell(square(1, BANK, CHUNK), 1, BANK, 0, CHUNK)
-        bell(square(1, S - CHUNK, P), 1, S - CHUNK, 0, P)
+        bell(square(1, S - CHUNK, P, late.tile([P, PACK, P], F32, name="sq_seventh", offset=RAW)), 1, S - CHUNK, 0, P)
         sq = square(1, S - P, P, late.tile([P, PACK, P], F32, name="sq_last", offset=0))
         for c0 in (0, P // 2):
             bell(sq, 1, S - P, c0, P // 2)
-        for pair in ((0, CHUNK), (BANK,), (S - CHUNK,)):
-            for j0 in pair:
-                weave(1, j0)
-            for j0 in pair:
-                quantise_h(1, j0)
+        both = keep.tile([P, PACK * BANK], BF16, name="both", align_bytes=ALIGN)
+        for j0 in (0, CHUNK):
+            weave(1, j0, both[:, PACK * j0:PACK * (j0 + CHUNK)])
+        woven[1, 0] = (both[:], BANK)
+        quantise_h(1, 0)
+        for j0 in (BANK, S - CHUNK):
+            weave(1, j0)
+            quantise_h(1, j0)
         last = keep.tile([P, PASS], BF16, name="last", align_bytes=ALIGN)
         for c0 in (0, P // 2):
             weave(1, S - P + c0, last[:, PACK * c0:PACK * (c0 + P // 2)])
         woven[1, S - P] = (last[:], P)
         quantise_h(1, S - P)
+        staged_first = late.tile([P, CHUNK], F32, name="staged_first", offset=RAW)
         staged = late.tile([P, 6 * CHUNK], F32, name="staged", offset=0)
-        for j0 in range(0, S - CHUNK, CHUNK):
-            finish(j0, CHUNK, True, staged[:, 2 * j0:2 * (j0 + CHUNK)])
-        staged_last = keep.tile([P, 2 * CHUNK], F32, name="staged_last")
-        finish(S - CHUNK, P, False, staged_last[:, 0:CHUNK])
-        finish(S - P, P, False, staged_last[:, CHUNK:])
+        finish(0, CHUNK, True, [staged_first[:], staged[:, 0:CHUNK]])
+        finish(CHUNK, CHUNK, True, [staged[:, CHUNK:3 * CHUNK]])
+        finish(BANK, CHUNK, True, [staged[:, 3 * CHUNK:5 * CHUNK]])
+        finish(S - CHUNK, P, True, [staged[:, 5 * CHUNK:]])
+        staged_last = keep.tile([P, CHUNK], F32, name="staged_last")
+        finish(S - P, P, False, [staged_last[:]])

@@ -26,6 +26,7 @@ QUADRANTS = 4
 K_PASSES = K // PASS
 GROUPS = H // PASS
 ALIGN = 64
+LN_RANGE = 60
 
 
 def tile_list_redshift_gaussian_bumps_kernel(tc, tab, offs, w1, centre, gain, w2_words, w2_scales, out):
@@ -79,6 +80,18 @@ def tile_list_redshift_gaussian_bumps_kernel(tc, tab, offs, w1, centre, gain, w2
             consts = keep.tile([P, 2 * GROUPS, PACK], F32, name="consts")
             nc.scalar.activation(out=consts[:], in_=turned[:].rearrange("p (t c) -> p c t", t=PACK)[:, 0:2 * GROUPS, :],
                                  func=ACT.Copy)
+            gains = consts[:, GROUPS:, :]
+            size = keep.tile([P, GROUPS, PACK], F32, name="size")
+            nc.scalar.activation(out=size[:], in_=gains, func=ACT.Abs)
+            bounded = keep.tile([P, GROUPS, PACK], F32, name="bounded")
+            nc.gpsimd.tensor_scalar(out=bounded[:], in0=size[:], scalar1=2.0 ** -LN_RANGE, scalar2=2.0 ** LN_RANGE,
+                                    op0=ALU.max, op1=ALU.min)
+            log_gain = keep.tile([P, GROUPS, PACK], F32, name="log_gain")
+            nc.scalar.activation(out=log_gain[:], in_=bounded[:], func=ACT.Ln)
+            inverse = keep.tile([P, GROUPS, PACK], F32, name="inverse")
+            nc.scalar.activation(out=inverse[:], in_=log_gain[:], func=ACT.Exp, scale=-1.0)
+            signs = keep.tile([P, GROUPS, PACK], F32, name="signs")
+            nc.gpsimd.tensor_tensor(out=signs[:], in0=gains, in1=inverse[:], op=ALU.mult)
             nc.vector.tensor_copy(picked_scales[:], tab_scales[:].indirect(offsets[:]))
         for q in (0, 2, 1, 3):
             first = 32 + 16 * q
@@ -107,30 +120,32 @@ def tile_list_redshift_gaussian_bumps_kernel(tc, tab, offs, w1, centre, gain, w2
             nc.vector.tensor_copy(picked[:], tab_words[n][:].indirect(offsets[:]))
             v_words[n] = keep.tile([P, 2, S], U16, name="parted%d" % n, align_bytes=ALIGN)
             nc.vector.tensor_copy(v_words[n][:], picked[:].bitcast(U16).rearrange("p (j h) -> p h j", h=2))
-        stage = early.tile([P, PACK * PASS], BF16, name="stage", align_bytes=ALIGN, offset=0)
+        stage = early.tile([P, 2 * PACK * PASS], BF16, name="stage", align_bytes=ALIGN, offset=0)
 
         w1_grouped = {}
         w1_mx = {}
 
-        def group_w1(b, a, t0, t1, on_scalar, place):
-            grouped = stage[:, place * PASS:(place + t1 - t0) * PASS]
-            dst = grouped.rearrange("p (t m j) -> p m j t", m=P, j=PACK)
-            src = w1_raw[b, a][:].rearrange("p j (m t) -> p j m t", t=PACK)[:, :, :, t0:t1].rearrange("p j m t -> p m j t")
+        def group_w1(b, a, t0, on_scalar, place, area=stage):
+            pair = area[:, place * PASS:(place + 2) * PASS]
+            dst = pair.rearrange("p (t m j) -> p m j t", t=2, j=PACK)
+            src = w1_raw[b, a][:].rearrange("p j (m t) -> p j m t", t=PACK)[:, :, :, t0:t0 + 2].rearrange("p j m t -> p m j t")
             if on_scalar:
                 nc.scalar.activation(out=dst, in_=src, func=ACT.Copy)
             else:
                 nc.vector.tensor_copy(out=dst, in_=src)
-            w1_grouped[b, a, t0] = (grouped, t1)
+            w1_grouped[b, a, t0] = (area, place)
+            w1_grouped[b, a, t0 + 1] = (area, place + 1)
 
-        def quantise_w1(b, a, t0, pool=keep, offset=None):
-            grouped, t1 = w1_grouped[b, a, t0]
-            codes = pool.tile([P, (t1 - t0) * P], U32, name="w1_codes%d%d%d" % (b, a, t0), align_bytes=ALIGN, offset=offset)
-            scales = keep.tile([P, (t1 - t0) * P], U8, name="w1_scales%d%d%d" % (b, a, t0), align_bytes=ALIGN)
-            nc.vector.quantize_mx(out=codes[:].bitcast(FP8X4), scales=scales[:],
-                                  in_=grouped)
-            for t in range(t0, t1):
-                cols = slice((t - t0) * P, (t - t0 + 1) * P)
-                w1_mx[b, a, t] = (codes[:, cols], scales[:, cols])
+        def quantise_w1(b, a, t0, count, codes=None):
+            area, place = w1_grouped[b, a, t0]
+            if codes is None:
+                codes = keep.tile([P, count * P], U32, name="w1_codes%d%d%d" % (b, a, t0), align_bytes=ALIGN)[:]
+            scales = keep.tile([P, count * P], U8, name="w1_scales%d%d%d" % (b, a, t0), align_bytes=ALIGN)
+            nc.vector.quantize_mx(out=codes.bitcast(FP8X4), scales=scales[:],
+                                  in_=area[:, place * PASS:(place + count) * PASS])
+            for i in range(count):
+                cols = slice(i * P, (i + 1) * P)
+                w1_mx[b, a, t0 + i] = (codes[:, cols], scales[:, cols])
 
         banks = {}
 
@@ -155,50 +170,58 @@ def tile_list_redshift_gaussian_bumps_kernel(tc, tab, offs, w1, centre, gain, w2
         def by_tile(passes):
             return [(a, t) for t in range(PACK) for a in passes]
 
-        def square(b, j0, width, sq=None):
-            half, c0 = divmod(j0, BANK)
-            if sq is None:
-                sq = ring.tile([P, PACK, width], F32, name="sq", bufs=2)
-            for t in range(PACK):
-                nc.scalar.activation(out=sq[:, t, :], in_=banks[b, half, t][:, c0:c0 + width],
-                                     func=ACT.Square, bias=consts[:, b, t:t + 1], scale=-1.0)
-            return sq
+        planes = {}
 
-        bells = {}
+        def bumps(b, chunks):
+            waiting = []
 
-        def bell(sq, b, j0, c0, width, e=None):
-            if e is None:
-                e = ring.tile([P, PACK, width], F32, name="bell", tag="bell%d" % width, bufs=(1 if width == BANK else 3))
-            nc.scalar.activation(out=e[:], in_=sq[:, :, c0:c0 + width], func=ACT.Exp, scale=-1.0)
-            bells[b, j0 + c0] = (e, width)
+            def bell():
+                j0, t, sq = waiting.pop(0)
+                nc.scalar.activation(out=planes[b, j0][:, t, :], in_=sq, func=ACT.Exp, scale=-1.0,
+                                     bias=log_gain[:, b, t:t + 1])
+
+            for j0, width, ahead in chunks:
+                half, c0 = divmod(j0, BANK)
+                planes[b, j0] = keep.tile([P, PACK, width], BF16, name="planes%d_%d" % (b, j0))
+                for t in range(PACK):
+                    sq = ring.tile([P, BANK], F32, name="sq", bufs=4)
+                    nc.scalar.activation(out=sq[:, 0:width], in_=banks[b, half, t][:, c0:c0 + width],
+                                         func=ACT.Square, bias=consts[:, b, t:t + 1], scale=-1.0)
+                    waiting.append((j0, t, sq[:, 0:width]))
+                    while len(waiting) > ahead:
+                        bell()
+            while waiting:
+                bell()
+
+        signed = {}
+
+        def sign(b, j0, t):
+            nc.vector.tensor_scalar(out=signed[b, j0][:, t, :], in0=planes[b, j0][:, t, :], scalar1=signs[:, b, t:t + 1], scalar2=None, op0=ALU.mult)
+
+        def weave(b, j0, c0, width, woven):
+            nc.vector.tensor_copy(
+                out=woven.rearrange("p (c i t) -> p c t i", i=PACK, t=PACK),
+                in_=signed[b, j0][:, :, c0:c0 + width].rearrange("p t (c i) -> p c t i", i=PACK))
+
+        def weave_signed(b, j0, width, woven):
+            nc.vector.tensor_tensor(
+                out=woven.rearrange("p (c i t) -> p c t i", i=PACK, t=PACK),
+                in0=planes[b, j0][:].rearrange("p t (c i) -> p c t i", i=PACK),
+                in1=signs[:, b, :].unsqueeze(1).unsqueeze(3).to_broadcast([P, width // PACK, PACK, PACK]),
+                op=ALU.mult)
 
         h_mx = {}
 
-        woven = {}
-
-        def weave(b, j0, hb=None):
-            e, width = bells[b, j0]
-            if hb is None:
-                hb = ring.tile([P, width * PACK], BF16, name="h_woven", align_bytes=ALIGN, bufs=3)[:]
-            nc.vector.tensor_tensor(
-                out=hb.rearrange("p (c i t) -> p c t i", i=2, t=PACK),
-                in0=e[:].rearrange("p t (c i) -> p c t i", i=2),
-                in1=consts[:, GROUPS + b, :].unsqueeze(1).unsqueeze(3).to_broadcast([P, width // 2, PACK, 2]),
-                op=ALU.mult)
-            woven[b, j0] = (hb, width)
-
-        def quantise_h(b, j0, codes=None):
-            hb, width = woven[b, j0]
-            if codes is None:
-                codes = keep.tile([P, width], U32, name="h_codes%d_%d" % (b, j0), align_bytes=ALIGN)
+        def quantise_h(b, j0, width, woven):
+            codes = keep.tile([P, width], U32, name="h_codes%d_%d" % (b, j0), align_bytes=ALIGN)
             scales = keep.tile([P, width], U8, name="h_scales%d_%d" % (b, j0), align_bytes=ALIGN)
-            nc.vector.quantize_mx(out=codes[:].bitcast(FP8X4), scales=scales[:], in_=hb)
+            nc.vector.quantize_mx(out=codes[:].bitcast(FP8X4), scales=scales[:], in_=woven)
             for c in range(0, width, P):
                 h_mx[b, j0 + c] = (codes, scales, c)
 
         out_rows = out.rearrange("(u p) j -> p u j", p=P)
 
-        def finish(j0, width, on_scalar, staged):
+        def finish(j0, width, on_scalar):
             acc = psum.tile([P, BANK], F32, name="bank")
             for b in range(GROUPS):
                 for u in range(N // P):
@@ -209,76 +232,71 @@ def tile_list_redshift_gaussian_bumps_kernel(tc, tab, offs, w1, centre, gain, w2
                         lhsT_scale=w2s[:, b, P * u:P * (u + 1)],
                         rhs=codes[:, c:c + width].bitcast(FP8X4), rhs_scale=scales[:, c:c + width],
                         start=(b == 0 and u == 0), stop=(b == GROUPS - 1 and u == N // P - 1))
-            step = 2 // len(staged)
-            for i, part in enumerate(staged):
-                source = acc[:, i * step * width:(i + 1) * step * width]
-                if on_scalar:
-                    nc.scalar.copy(out=part, in_=source)
-                else:
-                    nc.vector.tensor_copy(out=part, in_=source)
-                nc.sync.dma_start(out=out_rows[:, i * step:(i + 1) * step, j0:j0 + width],
-                                  in_=part.rearrange("p (u j) -> p u j", u=step))
+            staged = keep.tile([P, 2 * width], F32, name="staged%d" % j0)
+            if on_scalar:
+                nc.scalar.copy(out=staged[:], in_=acc[:, 0:2 * width])
+            else:
+                nc.vector.tensor_copy(out=staged[:], in_=acc[:, 0:2 * width])
+            nc.sync.dma_start(out=out_rows[:, :, j0:j0 + width], in_=staged[:].rearrange("p (u j) -> p u j", u=2))
 
-        for a in range(K_PASSES):
-            group_w1(0, a, 0, 2, False, 2 * (a % 2))
-            group_w1(0, a, 2, 4, True, 2 - 2 * (a % 2))
-            quantise_w1(0, a, 0)
-            quantise_w1(0, a, 2)
+        for a in range(K_PASSES - 1):
+            group_w1(0, a, 0, False, 2 * (a % 2))
+            group_w1(0, a, 2, True, 2 - 2 * (a % 2))
+            quantise_w1(0, a, 0, 2)
+            quantise_w1(0, a, 2, 2)
+        first_pair = early.tile([P, 2 * PASS], BF16, name="first_pair", align_bytes=ALIGN, offset=4 * PACK * PASS)
+        group_w1(0, 3, 0, False, 0, first_pair)
+        group_w1(0, 3, 2, True, 0)
+        quantise_w1(0, 3, 0, 1)
+        quantise_w1(0, 3, 1, 1)
+        second_codes = early.tile([P, 2 * P], U32, name="second_codes", align_bytes=ALIGN, offset=4 * PACK * PASS)
+        quantise_w1(0, 3, 2, 2, second_codes[:])
         project(0, 0, as_loaded(range(4)))
-        project(0, 1, as_loaded([0]) + by_tile([3, 1, 2]))
-        sq = square(0, 0, BANK)
-        for c0 in (0, CHUNK):
-            bell(sq, 0, 0, c0, CHUNK)
-        bell(square(0, BANK, BANK), 0, BANK, 0, BANK)
+        project(0, 1, by_tile([3, 0, 1, 2]))
+        bumps(0, [(0, BANK, 1), (BANK, BANK, 1)])
+        signed[0, 0] = planes[0, 0]
 
-        for a in range(2):
-            group_w1(1, a, 0, 2, False, 0)
-            group_w1(1, a, 2, 4, False, 2)
-            quantise_w1(1, a, 0)
-            quantise_w1(1, a, 2)
-        weave(0, 0, stage[:, 0:PACK * CHUNK])
-        group_w1(1, 2, 0, 2, False, 2)
-        quantise_h(0, 0)
-        group_w1(1, 2, 2, 4, False, 0)
-        quantise_w1(1, 2, 0)
-        quantise_w1(1, 2, 2)
-        group_w1(1, 3, 0, 2, False, 0)
-        group_w1(1, 3, 2, 4, False, 2)
-        quantise_w1(1, 3, 0)
-        quantise_w1(1, 3, 2)
+        for a, ready in ((0, [0]), (1, [1, 2]), (2, [])):
+            group_w1(1, a, 0, False, 2)
+            group_w1(1, a, 2, False, 0)
+            quantise_w1(1, a, 0, 2)
+            quantise_w1(1, a, 2, 2)
+            for t in ready:
+                sign(0, 0, t)
+        group_w1(1, 3, 0, False, 2)
+        sign(0, 0, 3)
+        quantise_w1(1, 3, 0, 1)
+        quantise_w1(1, 3, 1, 1)
+        group_w1(1, 3, 2, False, 1)
+        weave(0, 0, CHUNK, CHUNK, stage[:, 3 * PASS:5 * PASS])
+        quantise_w1(1, 3, 2, 2)
         project(1, 0, as_loaded(range(4)))
-        project(1, 1, as_loaded([0]) + by_tile([3, 1, 2]))
-        held = late.tile([P, PACK * (S - CHUNK)], BF16, name="held", align_bytes=ALIGN, offset=7 * RAW)
-        weave(0, CHUNK, held[:, 0:PACK * CHUNK])
-        weave(0, BANK, held[:, PACK * CHUNK:])
-        quantise_h(0, CHUNK)
-        quantise_h(0, BANK)
-        sq = square(1, 0, BANK)
-        for c0 in (0, CHUNK):
-            bell(sq, 1, 0, c0, CHUNK)
-        bell(square(1, BANK, CHUNK), 1, BANK, 0, CHUNK)
-        bell(square(1, S - CHUNK, P, late.tile([P, PACK, P], F32, name="sq_seventh", offset=RAW)), 1, S - CHUNK, 0, P)
-        sq = square(1, S - P, P, late.tile([P, PACK, P], F32, name="sq_last", offset=0))
-        for c0 in (0, P // 2):
-            bell(sq, 1, S - P, c0, P // 2)
-        both = keep.tile([P, PACK * BANK], BF16, name="both", align_bytes=ALIGN)
+        project(1, 1, by_tile([3, 0, 1, 2]))
+        signed[0, BANK] = late.tile([P, PACK, BANK], BF16, name="signed", offset=7 * RAW)
+        sign(0, BANK, 0)
+        sign(0, BANK, 1)
+        weave(0, 0, 0, CHUNK, stage[:, PASS:3 * PASS])
+        sign(0, BANK, 2)
+        sign(0, BANK, 3)
+        quantise_h(0, 0, BANK, stage[:, PASS:5 * PASS])
+        woven = keep.tile([P, PACK * BANK], BF16, name="woven0", align_bytes=ALIGN)
+        weave(0, BANK, 0, BANK, woven[:])
+        quantise_h(0, BANK, BANK, woven[:])
+
+        bumps(1, [(0, BANK, 1), (BANK, CHUNK, 1), (S - CHUNK, P, 2), (S - P, P, 2)])
+        woven = keep.tile([P, PACK * S], BF16, name="woven1", align_bytes=ALIGN)
+        signed[1, 0] = planes[1, 0]
+        for t in range(PACK):
+            sign(1, 0, t)
         for j0 in (0, CHUNK):
-            weave(1, j0, both[:, PACK * j0:PACK * (j0 + CHUNK)])
-        woven[1, 0] = (both[:], BANK)
-        quantise_h(1, 0)
-        for j0 in (BANK, S - CHUNK):
-            weave(1, j0)
-            quantise_h(1, j0)
-        last = keep.tile([P, PASS], BF16, name="last", align_bytes=ALIGN)
-        for c0 in (0, P // 2):
-            weave(1, S - P + c0, last[:, PACK * c0:PACK * (c0 + P // 2)])
-        woven[1, S - P] = (last[:], P)
-        quantise_h(1, S - P)
-        staged_first = late.tile([P, CHUNK], F32, name="staged_first", offset=RAW)
-        staged = late.tile([P, 6 * CHUNK], F32, name="staged", offset=0)
-        finish(0, CHUNK, True, [staged_first[:], staged[:, 0:CHUNK]])
-        finish(CHUNK, CHUNK, True, [staged[:, CHUNK:3 * CHUNK]])
-        finish(BANK, CHUNK, True, [staged[:, 3 * CHUNK:5 * CHUNK]])
-        finish(S - CHUNK, P, True, [staged[:, 5 * CHUNK:]])
-        staged_last = keep.tile([P, CHUNK], F32, name="staged_last")
-        finish(S - P, P, False, [staged_last[:]])
+            weave(1, 0, j0, CHUNK, woven[:, PACK * j0:PACK * (j0 + CHUNK)])
+        for j0 in (0, CHUNK):
+            quantise_h(1, j0, CHUNK, woven[:, PACK * j0:PACK * (j0 + CHUNK)])
+        for j0, width in ((BANK, CHUNK), (S - CHUNK, P), (S - P, P)):
+            weave_signed(1, j0, width, woven[:, PACK * j0:PACK * (j0 + width)])
+            quantise_h(1, j0, width, woven[:, PACK * j0:PACK * (j0 + width)])
+        finish(0, CHUNK, True)
+        finish(CHUNK, CHUNK, True)
+        finish(BANK, CHUNK, True)
+        finish(S - CHUNK, P, True)
+        finish(S - P, P, False)

@@ -118,9 +118,17 @@ def tile_list_redshift_gaussian_bumps_kernel(tc, tab, offs, w1, centre, gain, w2
         picked = keep.tile([P, S], U32, name="picked")
         for n in range(2):
             nc.vector.tensor_copy(picked[:], tab_words[n][:].indirect(offsets[:]))
-            v_words[n] = keep.tile([P, 2, S], U16, name="parted%d" % n, align_bytes=ALIGN)
-            nc.vector.tensor_copy(v_words[n][:], picked[:].bitcast(U16).rearrange("p (j h) -> p h j", h=2))
-        stage = early.tile([P, 2 * PACK * PASS], BF16, name="stage", align_bytes=ALIGN, offset=0)
+            if n == 0:
+                parted = keep.tile([P, 2, S], U16, name="parted", align_bytes=ALIGN)
+                nc.vector.tensor_copy(parted[:], picked[:].bitcast(U16).rearrange("p (j h) -> p h j", h=2))
+                v_words[0], v_words[1] = parted[:, 0, :], parted[:, 1, :]
+
+        def part_second(h, pool, offset=None):
+            words = pool.tile([P, S], U16, name="parted%d" % h, align_bytes=ALIGN, offset=offset)
+            nc.vector.tensor_copy(words[:], picked[:].bitcast(U16)[:, h::2])
+            v_words[2 + h] = words[:]
+
+        stage = early.tile([P, 3 * PACK * PASS], BF16, name="stage", align_bytes=ALIGN, offset=0)
 
         w1_grouped = {}
         w1_mx = {}
@@ -153,14 +161,13 @@ def tile_list_redshift_gaussian_bumps_kernel(tc, tab, offs, w1, centre, gain, w2
             cols = slice(half * BANK, (half + 1) * BANK)
             done = [0] * PACK
             for a, t in steps:
-                n, h = divmod(a, 2)
                 if done[t] == 0:
                     banks[b, half, t] = psum.tile([P, BANK], F32, name="bank")
                 codes, scales = w1_mx[b, a, t]
                 nc.tensor.matmul_mx(
                     out=banks[b, half, t][:],
                     lhsT=codes.bitcast(FP8X4), lhsT_scale=scales,
-                    rhs=v_words[n][:, h, cols].bitcast(FP4X4), rhs_scale=v_scales[:, a, cols],
+                    rhs=v_words[a][:, cols].bitcast(FP4X4), rhs_scale=v_scales[:, a, cols],
                     start=(done[t] == 0), stop=(done[t] == K_PASSES - 1))
                 done[t] = done[t] + 1
 
@@ -172,42 +179,38 @@ def tile_list_redshift_gaussian_bumps_kernel(tc, tab, offs, w1, centre, gain, w2
 
         planes = {}
 
-        def bumps(b, chunks):
-            waiting = []
+        def square(b, j0, width, t, sq):
+            half, c0 = divmod(j0, BANK)
+            nc.scalar.activation(out=sq, in_=banks[b, half, t][:, c0:c0 + width],
+                                 func=ACT.Square, bias=consts[:, b, t:t + 1], scale=-1.0)
 
-            def bell():
-                j0, t, sq = waiting.pop(0)
-                nc.scalar.activation(out=planes[b, j0][:, t, :], in_=sq, func=ACT.Exp, scale=-1.0,
-                                     bias=log_gain[:, b, t:t + 1])
+        def as_planes(area):
+            return area.rearrange("p (c t j) -> p c t j", t=PACK, j=CHUNK)
 
-            for j0, width, ahead in chunks:
-                half, c0 = divmod(j0, BANK)
-                planes[b, j0] = keep.tile([P, PACK, width], BF16, name="planes%d_%d" % (b, j0))
-                for t in range(PACK):
-                    sq = ring.tile([P, BANK], F32, name="sq", bufs=4)
-                    nc.scalar.activation(out=sq[:, 0:width], in_=banks[b, half, t][:, c0:c0 + width],
-                                         func=ACT.Square, bias=consts[:, b, t:t + 1], scale=-1.0)
-                    waiting.append((j0, t, sq[:, 0:width]))
-                    while len(waiting) > ahead:
-                        bell()
-            while waiting:
-                bell()
+        def bell_plane(b, half, t, sq):
+            nc.scalar.activation(out=planes[b, half][:, :, t, :], in_=sq.rearrange("p (c j) -> p c j", j=CHUNK),
+                                 func=ACT.Exp, scale=-1.0, bias=log_gain[:, b, t:t + 1])
+
+        def bell_plain(sq, e):
+            nc.scalar.activation(out=e, in_=sq, func=ACT.Exp, scale=-1.0)
 
         signed = {}
 
-        def sign(b, j0, t):
-            nc.vector.tensor_scalar(out=signed[b, j0][:, t, :], in0=planes[b, j0][:, t, :], scalar1=signs[:, b, t:t + 1], scalar2=None, op0=ALU.mult)
+        def sign(b, half, t):
+            nc.vector.tensor_scalar(out=signed[b, half][:, :, t, :], in0=planes[b, half][:, :, t, :],
+                                    scalar1=signs[:, b, t:t + 1], scalar2=None, op0=ALU.mult)
 
-        def weave(b, j0, c0, width, woven):
-            nc.vector.tensor_copy(
-                out=woven.rearrange("p (c i t) -> p c t i", i=PACK, t=PACK),
-                in_=signed[b, j0][:, :, c0:c0 + width].rearrange("p t (c i) -> p c t i", i=PACK))
+        def weave(b, half, woven):
+            for c in range(BANK // CHUNK):
+                nc.vector.tensor_copy(
+                    out=woven[:, c * PACK * CHUNK:(c + 1) * PACK * CHUNK].rearrange("p (c i t) -> p c t i", i=PACK, t=PACK),
+                    in_=signed[b, half][:, c].rearrange("p t (c i) -> p c t i", i=PACK))
 
-        def weave_signed(b, j0, width, woven):
+        def weave_gain(b, e, width, woven):
             nc.vector.tensor_tensor(
-                out=woven.rearrange("p (c i t) -> p c t i", i=PACK, t=PACK),
-                in0=planes[b, j0][:].rearrange("p t (c i) -> p c t i", i=PACK),
-                in1=signs[:, b, :].unsqueeze(1).unsqueeze(3).to_broadcast([P, width // PACK, PACK, PACK]),
+                out=woven.rearrange("p (c i t) -> p c t i", i=2, t=PACK),
+                in0=e.rearrange("p t (c i) -> p c t i", i=2),
+                in1=consts[:, GROUPS + b, :].unsqueeze(1).unsqueeze(3).to_broadcast([P, width // 2, PACK, 2]),
                 op=ALU.mult)
 
         h_mx = {}
@@ -221,7 +224,7 @@ def tile_list_redshift_gaussian_bumps_kernel(tc, tab, offs, w1, centre, gain, w2
 
         out_rows = out.rearrange("(u p) j -> p u j", p=P)
 
-        def finish(j0, width, on_scalar):
+        def finish(j0, width, on_scalar, staged):
             acc = psum.tile([P, BANK], F32, name="bank")
             for b in range(GROUPS):
                 for u in range(N // P):
@@ -232,71 +235,147 @@ def tile_list_redshift_gaussian_bumps_kernel(tc, tab, offs, w1, centre, gain, w2
                         lhsT_scale=w2s[:, b, P * u:P * (u + 1)],
                         rhs=codes[:, c:c + width].bitcast(FP8X4), rhs_scale=scales[:, c:c + width],
                         start=(b == 0 and u == 0), stop=(b == GROUPS - 1 and u == N // P - 1))
-            staged = keep.tile([P, 2 * width], F32, name="staged%d" % j0)
-            if on_scalar:
-                nc.scalar.copy(out=staged[:], in_=acc[:, 0:2 * width])
-            else:
-                nc.vector.tensor_copy(out=staged[:], in_=acc[:, 0:2 * width])
-            nc.sync.dma_start(out=out_rows[:, :, j0:j0 + width], in_=staged[:].rearrange("p (u j) -> p u j", u=2))
+            step = 2 // len(staged)
+            for i, part in enumerate(staged):
+                source = acc[:, i * step * width:(i + 1) * step * width]
+                if on_scalar:
+                    nc.scalar.copy(out=part, in_=source)
+                else:
+                    nc.vector.tensor_copy(out=part, in_=source)
+                nc.sync.dma_start(out=out_rows[:, i * step:(i + 1) * step, j0:j0 + width],
+                                  in_=part.rearrange("p (u j) -> p u j", u=step))
 
         for a in range(K_PASSES - 1):
-            group_w1(0, a, 0, False, 2 * (a % 2))
+            if a == 0:
+                opening = early.tile([P, 2 * PASS], BF16, name="opening", align_bytes=ALIGN, offset=7 * PACK * PASS)
+                group_w1(0, a, 0, False, 0, opening)
+            else:
+                group_w1(0, a, 0, False, 2 * (a % 2))
             group_w1(0, a, 2, True, 2 - 2 * (a % 2))
+            if a == 0:
+                part_second(0, keep)
             quantise_w1(0, a, 0, 2)
             quantise_w1(0, a, 2, 2)
-        first_pair = early.tile([P, 2 * PASS], BF16, name="first_pair", align_bytes=ALIGN, offset=4 * PACK * PASS)
+            if a == 0:
+                part_second(1, early, 7 * PACK * PASS)
+        first_pair = early.tile([P, 2 * PASS], BF16, name="first_pair", align_bytes=ALIGN, offset=6 * PACK * PASS)
         group_w1(0, 3, 0, False, 0, first_pair)
         group_w1(0, 3, 2, True, 0)
         quantise_w1(0, 3, 0, 1)
         quantise_w1(0, 3, 1, 1)
-        second_codes = early.tile([P, 2 * P], U32, name="second_codes", align_bytes=ALIGN, offset=4 * PACK * PASS)
+        second_codes = early.tile([P, 2 * P], U32, name="second_codes", align_bytes=ALIGN, offset=6 * PACK * PASS)
         quantise_w1(0, 3, 2, 2, second_codes[:])
         project(0, 0, as_loaded(range(4)))
-        project(0, 1, by_tile([3, 0, 1, 2]))
-        bumps(0, [(0, BANK, 1), (BANK, BANK, 1)])
-        signed[0, 0] = planes[0, 0]
+        project(0, 1, as_loaded([0]) + by_tile([3, 1, 2]))
+        for b, half in ((0, 1), (1, 0)):
+            planes[b, half] = as_planes(keep.tile([P, PACK * BANK], BF16, name="planes%d" % b)[:])
 
-        for a, ready in ((0, [0]), (1, [1, 2]), (2, [])):
+        def slots(first, count):
+            return stage[:, first * PASS:(first + count) * PASS]
+
+        def plane_squares():
+            return ring.tile([P, BANK], F32, name="sq", bufs=3)[:]
+
+        sq_open = keep.tile([P, PACK, BANK], F32, name="sq_open")
+        bell_first = keep.tile([P, PACK, CHUNK], F32, name="bell_first")
+        bell_second = late.tile([P, PACK, CHUNK], F32, name="bell_second", offset=0)
+        for t in range(PACK):
+            square(0, 0, BANK, t, sq_open[:, t, :])
+        sq = {}
+        for t in range(PACK):
+            sq[t] = plane_squares()
+            square(0, BANK, BANK, t, sq[t])
+            if t == 0:
+                bell_plain(sq_open[:, :, 0:CHUNK], bell_first[:])
+            else:
+                bell_plane(0, 1, t - 1, sq[t - 1])
+        bell_plain(sq_open[:, :, CHUNK:BANK], bell_second[:])
+        bell_plane(0, 1, PACK - 1, sq[PACK - 1])
+
+        for a in range(2):
             group_w1(1, a, 0, False, 2)
             group_w1(1, a, 2, False, 0)
             quantise_w1(1, a, 0, 2)
             quantise_w1(1, a, 2, 2)
-            for t in ready:
-                sign(0, 0, t)
-        group_w1(1, 3, 0, False, 2)
-        sign(0, 0, 3)
+        weave_gain(0, bell_first[:, :, P:CHUNK], P, slots(2, 1))
+        group_w1(1, 2, 0, False, 0)
+        group_w1(1, 2, 2, False, 3)
+        quantise_w1(1, 2, 0, 2)
+        quantise_w1(1, 2, 2, 2)
+        weave_gain(0, bell_first[:, :, 0:P], P, slots(1, 1))
+        group_w1(1, 3, 0, False, 3)
+        quantise_h(0, 0, CHUNK, slots(1, 2))
         quantise_w1(1, 3, 0, 1)
         quantise_w1(1, 3, 1, 1)
-        group_w1(1, 3, 2, False, 1)
-        weave(0, 0, CHUNK, CHUNK, stage[:, 3 * PASS:5 * PASS])
+        group_w1(1, 3, 2, False, 2)
+        weave_gain(0, bell_second[:, :, P:CHUNK], P, slots(4, 1))
         quantise_w1(1, 3, 2, 2)
         project(1, 0, as_loaded(range(4)))
-        project(1, 1, by_tile([3, 0, 1, 2]))
-        signed[0, BANK] = late.tile([P, PACK, BANK], BF16, name="signed", offset=7 * RAW)
-        sign(0, BANK, 0)
-        sign(0, BANK, 1)
-        weave(0, 0, 0, CHUNK, stage[:, PASS:3 * PASS])
-        sign(0, BANK, 2)
-        sign(0, BANK, 3)
-        quantise_h(0, 0, BANK, stage[:, PASS:5 * PASS])
-        woven = keep.tile([P, PACK * BANK], BF16, name="woven0", align_bytes=ALIGN)
-        weave(0, BANK, 0, BANK, woven[:])
-        quantise_h(0, BANK, BANK, woven[:])
+        project(1, 1, as_loaded([0]) + by_tile([3, 1, 2]))
+        signed[0, 1] = as_planes(late.tile([P, PACK * BANK], BF16, name="signed0", offset=7 * RAW)[:])
+        sign(0, 1, 0)
+        sign(0, 1, 1)
+        weave_gain(0, bell_second[:, :, 0:P], P, slots(3, 1))
+        sign(0, 1, 2)
+        sign(0, 1, 3)
+        quantise_h(0, CHUNK, CHUNK, slots(3, 2))
+        held = keep.tile([P, PACK * BANK], BF16, name="woven0", align_bytes=ALIGN)
+        weave(0, 1, held[:])
 
-        bumps(1, [(0, BANK, 1), (BANK, CHUNK, 1), (S - CHUNK, P, 2), (S - P, P, 2)])
-        woven = keep.tile([P, PACK * S], BF16, name="woven1", align_bytes=ALIGN)
-        signed[1, 0] = planes[1, 0]
+        third = keep.tile([P, PACK, CHUNK], F32, name="sq_third")
+        seventh = late.tile([P, PACK, P], F32, name="sq_seventh", offset=RAW)
+        eighth = late.tile([P, PACK, P], F32, name="sq_eighth", offset=2 * RAW)
+        bell_third = keep.tile([P, PACK, CHUNK], F32, name="bell_third")
+        bell_seventh = keep.tile([P, PACK, P], F32, name="bell_seventh")
+        bell_eighth = keep.tile([P, 2, PACK, P // 2], F32, name="bell_eighth")
         for t in range(PACK):
-            sign(1, 0, t)
+            sq[t] = plane_squares()
+            square(1, 0, BANK, t, sq[t])
+            if t > 0:
+                bell_plane(1, 0, t - 1, sq[t - 1])
+        square(1, BANK, CHUNK, 0, third[:, 0, :])
+        bell_plane(1, 0, PACK - 1, sq[PACK - 1])
+        for t in range(1, PACK):
+            square(1, BANK, CHUNK, t, third[:, t, :])
+        for t in range(2):
+            square(1, S - CHUNK, P, t, seventh[:, t, :])
+        bell_plain(third[:], bell_third[:])
+        for t in range(2, PACK):
+            square(1, S - CHUNK, P, t, seventh[:, t, :])
+        for t in range(2):
+            square(1, S - P, P, t, eighth[:, t, :])
+        bell_plain(seventh[:], bell_seventh[:])
+        for t in range(2, PACK):
+            square(1, S - P, P, t, eighth[:, t, :])
+        for i in range(2):
+            bell_plain(eighth[:, :, i * P // 2:(i + 1) * P // 2], bell_eighth[:, i])
+
+        woven = keep.tile([P, PACK * S], BF16, name="woven1", align_bytes=ALIGN)
+
+        def columns(j0, width):
+            return woven[:, PACK * j0:PACK * (j0 + width)]
+
+        signed[1, 0] = as_planes(late.tile([P, PACK * BANK], BF16, name="signed1", offset=0)[:])
+        sign(1, 0, 0)
+        sign(1, 0, 1)
+        quantise_h(0, BANK, BANK, held[:])
+        sign(1, 0, 2)
+        sign(1, 0, 3)
+        weave(1, 0, columns(0, BANK))
         for j0 in (0, CHUNK):
-            weave(1, 0, j0, CHUNK, woven[:, PACK * j0:PACK * (j0 + CHUNK)])
-        for j0 in (0, CHUNK):
-            quantise_h(1, j0, CHUNK, woven[:, PACK * j0:PACK * (j0 + CHUNK)])
-        for j0, width in ((BANK, CHUNK), (S - CHUNK, P), (S - P, P)):
-            weave_signed(1, j0, width, woven[:, PACK * j0:PACK * (j0 + width)])
-            quantise_h(1, j0, width, woven[:, PACK * j0:PACK * (j0 + width)])
-        finish(0, CHUNK, True)
-        finish(CHUNK, CHUNK, True)
-        finish(BANK, CHUNK, True)
-        finish(S - CHUNK, P, True)
-        finish(S - P, P, False)
+            quantise_h(1, j0, CHUNK, columns(j0, CHUNK))
+        weave_gain(1, bell_third[:], CHUNK, columns(BANK, CHUNK))
+        weave_gain(1, bell_seventh[:], P, columns(S - CHUNK, P))
+        quantise_h(1, BANK, CHUNK, columns(BANK, CHUNK))
+        quantise_h(1, S - CHUNK, P, columns(S - CHUNK, P))
+        for i in range(2):
+            weave_gain(1, bell_eighth[:, i], P // 2, columns(S - P + i * P // 2, P // 2))
+        quantise_h(1, S - P, P, columns(S - P, P))
+        staged_first = late.tile([P, CHUNK], F32, name="staged_first", offset=RAW)
+        staged = late.tile([P, 6 * CHUNK], F32, name="staged", offset=2 * RAW)
+        finish(0, CHUNK, True, [staged_first[:], staged[:, 0:CHUNK]])
+        finish(CHUNK, CHUNK, True, [staged[:, CHUNK:3 * CHUNK]])
+        finish(BANK, CHUNK, True, [staged[:, 3 * CHUNK:5 * CHUNK]])
+        finish(S - CHUNK, P, True, [staged[:, 5 * CHUNK:]])
+        staged_last = keep.tile([P, CHUNK], F32, name="staged_last")
+        finish(S - P, P, False, [staged_last[:]])

@@ -43,10 +43,12 @@ def tile_list_redshift_gaussian_bumps_kernel(tc, tab, offs, w1, centre, gain, w2
         tab_words = {}
         w1_raw = {}
 
-        def load_w1(pool, b, a, offset=None):
-            w1_raw[b, a] = pool.tile([P, PACK, PASS], F32, name="w1_raw%d%d" % (b, a), offset=offset)
+        def load_w1(pool, b, a, offset=None, area=None):
+            if area is None:
+                area = pool.tile([P, PACK * PASS], F32, name="w1_raw%d%d" % (b, a), offset=offset)[:]
+            w1_raw[b, a] = area.rearrange("p (j c) -> p j c", j=PACK)
             nc.sync.dma_start(
-                out=w1_raw[b, a][:],
+                out=w1_raw[b, a],
                 in_=w1[a * PASS:(a + 1) * PASS, b * PASS:(b + 1) * PASS].rearrange("(p j) c -> p j c", j=PACK))
 
         def load_words(pool, n, offset=None):
@@ -103,8 +105,11 @@ def tile_list_redshift_gaussian_bumps_kernel(tc, tab, offs, w1, centre, gain, w2
         small = 8 * RAW
         for a in range(K_PASSES):
             load_w1(late, 0, a, a * RAW)
-        for a in range(K_PASSES):
+        for a in range(2):
             load_w1(late, 1, a, (4 + a) * RAW)
+        raw_end = late.tile([P, 2 * PACK * PASS], F32, name="raw_end", offset=6 * RAW)
+        for a in range(2):
+            load_w1(late, 1, 2 + a, area=raw_end[:, a * PACK * PASS:(a + 1) * PACK * PASS])
         w2w = late.tile([P, GROUPS, 2 * N], U8, name="w2w", align_bytes=ALIGN, offset=small + 128)
         nc.sync.dma_start(out=w2w[:].bitcast(I32), in_=w2_words.rearrange("a p c -> p a c").bitcast(I32))
         w2s = late.tile([P, GROUPS, N], U8, name="w2s", align_bytes=ALIGN, offset=small + 128 + 4 * N)
@@ -133,10 +138,10 @@ def tile_list_redshift_gaussian_bumps_kernel(tc, tab, offs, w1, centre, gain, w2
         w1_grouped = {}
         w1_mx = {}
 
-        def group_w1(b, a, t0, on_scalar, place, area=stage):
+        def group_w1(b, a, t0, on_scalar, place, area=stage, rows=slice(0, P)):
             pair = area[:, place * PASS:(place + 2) * PASS]
-            dst = pair.rearrange("p (t m j) -> p m j t", t=2, j=PACK)
-            src = w1_raw[b, a][:].rearrange("p j (m t) -> p j m t", t=PACK)[:, :, :, t0:t0 + 2].rearrange("p j m t -> p m j t")
+            dst = pair.rearrange("p (t m j) -> p m j t", t=2, j=PACK)[:, rows]
+            src = w1_raw[b, a].rearrange("p j (m t) -> p m j t", t=PACK)[:, rows, :, t0:t0 + 2]
             if on_scalar:
                 nc.scalar.activation(out=dst, in_=src, func=ACT.Copy)
             else:
@@ -185,10 +190,10 @@ def tile_list_redshift_gaussian_bumps_kernel(tc, tab, offs, w1, centre, gain, w2
                                  func=ACT.Square, bias=consts[:, b, t:t + 1], scale=-1.0)
 
         def as_planes(area):
-            return area.rearrange("p (c t j) -> p c t j", t=PACK, j=CHUNK)
+            return area.rearrange("p (t j) -> p t j", t=PACK)
 
         def bell_plane(b, half, t, sq):
-            nc.scalar.activation(out=planes[b, half][:, :, t, :], in_=sq.rearrange("p (c j) -> p c j", j=CHUNK),
+            nc.scalar.activation(out=planes[b, half][:, t, :], in_=sq,
                                  func=ACT.Exp, scale=-1.0, bias=log_gain[:, b, t:t + 1])
 
         def bell_plain(sq, e):
@@ -197,14 +202,14 @@ def tile_list_redshift_gaussian_bumps_kernel(tc, tab, offs, w1, centre, gain, w2
         signed = {}
 
         def sign(b, half, t):
-            nc.vector.tensor_scalar(out=signed[b, half][:, :, t, :], in0=planes[b, half][:, :, t, :],
+            nc.vector.tensor_scalar(out=signed[b, half][:, t, :], in0=planes[b, half][:, t, :],
                                     scalar1=signs[:, b, t:t + 1], scalar2=None, op0=ALU.mult)
 
         def weave(b, half, woven):
             for c in range(BANK // CHUNK):
                 nc.vector.tensor_copy(
                     out=woven[:, c * PACK * CHUNK:(c + 1) * PACK * CHUNK].rearrange("p (c i t) -> p c t i", i=PACK, t=PACK),
-                    in_=signed[b, half][:, c].rearrange("p t (c i) -> p c t i", i=PACK))
+                    in_=signed[b, half][:, :, c * CHUNK:(c + 1) * CHUNK].rearrange("p t (c i) -> p c t i", i=PACK))
 
         def weave_gain(b, e, width, woven):
             nc.vector.tensor_tensor(
@@ -250,8 +255,8 @@ def tile_list_redshift_gaussian_bumps_kernel(tc, tab, offs, w1, centre, gain, w2
                 opening = early.tile([P, 2 * PASS], BF16, name="opening", align_bytes=ALIGN, offset=7 * PACK * PASS)
                 group_w1(0, a, 0, False, 0, opening)
             else:
-                group_w1(0, a, 0, False, 2 * (a % 2))
-            group_w1(0, a, 2, True, 2 - 2 * (a % 2))
+                group_w1(0, a, 0, False, 4 * (a % 2))
+            group_w1(0, a, 2, True, 4 - 4 * (a % 2))
             if a == 0:
                 part_second(0, keep)
             quantise_w1(0, a, 0, 2)
@@ -286,41 +291,40 @@ def tile_list_redshift_gaussian_bumps_kernel(tc, tab, offs, w1, centre, gain, w2
             sq[t] = plane_squares()
             square(0, BANK, BANK, t, sq[t])
             if t == 0:
-                bell_plain(sq_open[:, :, 0:CHUNK], bell_first[:])
+                bell_plain(sq_open[:, :, CHUNK:BANK], bell_first[:])
             else:
                 bell_plane(0, 1, t - 1, sq[t - 1])
-        bell_plain(sq_open[:, :, CHUNK:BANK], bell_second[:])
+        bell_plain(sq_open[:, :, 0:CHUNK], bell_second[:])
         bell_plane(0, 1, PACK - 1, sq[PACK - 1])
 
         for a in range(2):
-            group_w1(1, a, 0, False, 2)
+            group_w1(1, a, 0, False, 4)
             group_w1(1, a, 2, False, 0)
             quantise_w1(1, a, 0, 2)
             quantise_w1(1, a, 2, 2)
-        weave_gain(0, bell_first[:, :, P:CHUNK], P, slots(2, 1))
+        weave_gain(0, bell_first[:, :, P:CHUNK], P, slots(5, 1))
         group_w1(1, 2, 0, False, 0)
         group_w1(1, 2, 2, False, 3)
         quantise_w1(1, 2, 0, 2)
         quantise_w1(1, 2, 2, 2)
-        weave_gain(0, bell_first[:, :, 0:P], P, slots(1, 1))
+        border = PACK * PASS
+        signed[0, 1] = as_planes(raw_end[:, border - 3 * BANK // 2:border + BANK // 2].bitcast(BF16))
+        for t in range(PACK - 1):
+            sign(0, 1, t)
         group_w1(1, 3, 0, False, 3)
-        quantise_h(0, 0, CHUNK, slots(1, 2))
+        group_w1(1, 3, 2, False, 1, rows=slice(0, P // 2))
         quantise_w1(1, 3, 0, 1)
         quantise_w1(1, 3, 1, 1)
-        group_w1(1, 3, 2, False, 2)
-        weave_gain(0, bell_second[:, :, P:CHUNK], P, slots(4, 1))
+        group_w1(1, 3, 2, True, 1, rows=slice(P // 2, P))
+        weave_gain(0, bell_first[:, :, 0:P], P, slots(4, 1))
         quantise_w1(1, 3, 2, 2)
         project(1, 0, as_loaded(range(4)))
         project(1, 1, as_loaded([0]) + by_tile([3, 1, 2]))
-        signed[0, 1] = as_planes(late.tile([P, PACK * BANK], BF16, name="signed0", offset=7 * RAW)[:])
-        sign(0, 1, 0)
-        sign(0, 1, 1)
-        weave_gain(0, bell_second[:, :, 0:P], P, slots(3, 1))
-        sign(0, 1, 2)
-        sign(0, 1, 3)
-        quantise_h(0, CHUNK, CHUNK, slots(3, 2))
+        sign(0, 1, PACK - 1)
+        weave_gain(0, bell_second[:], CHUNK, slots(2, 2))
         held = keep.tile([P, PACK * BANK], BF16, name="woven0", align_bytes=ALIGN)
         weave(0, 1, held[:])
+        quantise_h(0, 0, BANK, slots(2, 4))
 
         third = keep.tile([P, PACK, CHUNK], F32, name="sq_third")
         seventh = late.tile([P, PACK, P], F32, name="sq_seventh", offset=RAW)
@@ -333,9 +337,8 @@ def tile_list_redshift_gaussian_bumps_kernel(tc, tab, offs, w1, centre, gain, w2
             square(1, 0, BANK, t, sq[t])
             if t > 0:
                 bell_plane(1, 0, t - 1, sq[t - 1])
-        square(1, BANK, CHUNK, 0, third[:, 0, :])
         bell_plane(1, 0, PACK - 1, sq[PACK - 1])
-        for t in range(1, PACK):
+        for t in range(PACK):
             square(1, BANK, CHUNK, t, third[:, t, :])
         for t in range(2):
             square(1, S - CHUNK, P, t, seventh[:, t, :])
@@ -358,18 +361,19 @@ def tile_list_redshift_gaussian_bumps_kernel(tc, tab, offs, w1, centre, gain, w2
         signed[1, 0] = as_planes(late.tile([P, PACK * BANK], BF16, name="signed1", offset=0)[:])
         sign(1, 0, 0)
         sign(1, 0, 1)
-        quantise_h(0, BANK, BANK, held[:])
+        quantise_h(0, BANK, CHUNK, held[:, 0:PACK * CHUNK])
         sign(1, 0, 2)
         sign(1, 0, 3)
+        quantise_h(0, S - CHUNK, CHUNK, held[:, PACK * CHUNK:])
         weave(1, 0, columns(0, BANK))
         for j0 in (0, CHUNK):
             quantise_h(1, j0, CHUNK, columns(j0, CHUNK))
         weave_gain(1, bell_third[:], CHUNK, columns(BANK, CHUNK))
         weave_gain(1, bell_seventh[:], P, columns(S - CHUNK, P))
         quantise_h(1, BANK, CHUNK, columns(BANK, CHUNK))
-        quantise_h(1, S - CHUNK, P, columns(S - CHUNK, P))
         for i in range(2):
             weave_gain(1, bell_eighth[:, i], P // 2, columns(S - P + i * P // 2, P // 2))
+        quantise_h(1, S - CHUNK, P, columns(S - CHUNK, P))
         quantise_h(1, S - P, P, columns(S - P, P))
         staged_first = late.tile([P, CHUNK], F32, name="staged_first", offset=RAW)
         staged = late.tile([P, 6 * CHUNK], F32, name="staged", offset=2 * RAW)

@@ -308,9 +308,8 @@ def tile_list_redshift_gaussian_bumps_kernel(tc, tab, offs, w1, centre, gain, w2
         quantise_w1(1, 2, 0, 2)
         quantise_w1(1, 2, 2, 2)
         border = PACK * PASS
-        signed[0, 1] = as_planes(raw_end[:, border - 3 * BANK // 2:border + BANK // 2].bitcast(BF16))
-        for t in range(PACK - 1):
-            sign(0, 1, t)
+        signed[0, 1] = as_planes(raw_end[:, border - BANK // 2:border + 3 * BANK // 2].bitcast(BF16))
+        sign(0, 1, 0)
         group_w1(1, 3, 0, False, 3)
         group_w1(1, 3, 2, False, 1, rows=slice(0, P // 2))
         quantise_w1(1, 3, 0, 1)
@@ -320,7 +319,8 @@ def tile_list_redshift_gaussian_bumps_kernel(tc, tab, offs, w1, centre, gain, w2
         quantise_w1(1, 3, 2, 2)
         project(1, 0, as_loaded(range(4)))
         project(1, 1, as_loaded([0]) + by_tile([3, 1, 2]))
-        sign(0, 1, PACK - 1)
+        for t in range(1, PACK):
+            sign(0, 1, t)
         weave_gain(0, bell_second[:], CHUNK, slots(2, 2))
         held = keep.tile([P, PACK * BANK], BF16, name="woven0", align_bytes=ALIGN)
         weave(0, 1, held[:])

@@ -23,10 +23,13 @@ PASS = P * PACK
 BANK = 512
 CHUNK = 256
 QUADRANTS = 4
+BLOCKS = 16
 K_PASSES = K // PASS
 GROUPS = H // PASS
 ALIGN = 64
 LN_RANGE = 60
+PIECE = 4 * PACK * PASS
+SLOT = 2 * PASS
 
 
 def tile_list_redshift_gaussian_bumps_kernel(tc, tab, offs, w1, centre, gain, w2_words, w2_scales, out):
@@ -51,25 +54,25 @@ def tile_list_redshift_gaussian_bumps_kernel(tc, tab, offs, w1, centre, gain, w2
                 out=w1_raw[b, a],
                 in_=w1[a * PASS:(a + 1) * PASS, b * PASS:(b + 1) * PASS].rearrange("(p j) c -> p j c", j=PACK))
 
-        def load_words(pool, n, offset=None):
-            tab_words[n] = pool.tile([P, T], U32, name="tab_words%d" % n, offset=offset)
+        def load_words(pool, pair, offset=None):
+            tab_words[pair] = pool.tile([P, T], U32, name="tab_words%d" % pair, offset=offset)
             nc.sync.dma_start(
-                out=tab_words[n][:].bitcast(I32),
-                in_=tab[n, 0:PASS * T].rearrange("(p x) -> p x", p=P).bitcast(I32))
+                out=tab_words[pair][:].bitcast(I32),
+                in_=tab[pair, 0:PASS * T].rearrange("(p x) -> p x", p=P).bitcast(I32))
 
         nc.sync.dma_start(offsets[:], offs)
         with tc.tile_pool(name="window", bufs=1) as window:
             tab_scales = window.tile([P, T], U8, name="tab_scales")
             rows = keep.tile([P, PASS], F32, name="rows")
             nc.vector.memset(rows[:], 0.0)
-            for first in (0, 96):
-                nc.vector.memset(tab_scales[first:first + 32, :].bitcast(I32), 0)
+            for unused in (0, 96):
+                nc.vector.memset(tab_scales[unused:unused + 32, :].bitcast(I32), 0)
             nc.vector.memset(v_scales[:].rearrange("p a j -> p (a j)").bitcast(I32), 0)
             for a in range(K_PASSES):
-                n, h = divmod(a, 2)
+                pair, side = divmod(a, 2)
                 nc.sync.dma_start(
                     out=tab_scales[32 + a:96:K_PASSES, :].bitcast(I32),
-                    in_=tab[n, PASS * T:].rearrange("(h q t) -> h q t", h=2, q=16)[h].bitcast(I32))
+                    in_=tab[pair, PASS * T:].rearrange("(s g x) -> s g x", s=2, g=BLOCKS)[side].bitcast(I32))
             load_words(keep, 0)
             nc.sync.dma_start(out=rows[0:GROUPS, :], in_=centre.rearrange("(b c) -> b c", b=GROUPS))
             nc.sync.dma_start(out=rows[GROUPS:2 * GROUPS, :], in_=gain.rearrange("(b c) -> b c", b=GROUPS))
@@ -96,23 +99,23 @@ def tile_list_redshift_gaussian_bumps_kernel(tc, tab, offs, w1, centre, gain, w2
             nc.gpsimd.tensor_tensor(out=signs[:], in0=gains, in1=inverse[:], op=ALU.mult)
             nc.vector.tensor_copy(picked_scales[:], tab_scales[:].indirect(offsets[:]))
         for q in (0, 2, 1, 3):
-            first = 32 + 16 * q
+            source = 32 + BLOCKS * q
             nc.sync.dma_start(out=v_scales[32 * q:32 * q + 4, :, :].bitcast(I32),
-                              in_=picked_scales[first:first + 16, :].bitcast(I32))
+                              in_=picked_scales[source:source + BLOCKS, :].bitcast(I32))
 
         late = ctx.enter_context(tc.tile_pool(name="late", bufs=1))
-        RAW = 4 * PACK * PASS
-        small = 8 * RAW
         for a in range(K_PASSES):
-            load_w1(late, 0, a, a * RAW)
+            load_w1(late, 0, a, a * PIECE)
         for a in range(2):
-            load_w1(late, 1, a, (4 + a) * RAW)
-        raw_end = late.tile([P, 2 * PACK * PASS], F32, name="raw_end", offset=6 * RAW)
-        for a in range(2):
-            load_w1(late, 1, 2 + a, area=raw_end[:, a * PACK * PASS:(a + 1) * PACK * PASS])
-        w2w = late.tile([P, GROUPS, 2 * N], U8, name="w2w", align_bytes=ALIGN, offset=small + 128)
+            load_w1(late, 1, a, (K_PASSES + a) * PIECE)
+        border = PACK * PASS
+        raw_end = late.tile([P, 2 * border], F32, name="raw_end", offset=(K_PASSES + 2) * PIECE)
+        for i in range(2):
+            load_w1(late, 1, 2 + i, area=raw_end[:, i * border:(i + 1) * border])
+        w2_offset = GROUPS * K_PASSES * PIECE + 2 * ALIGN
+        w2w = late.tile([P, GROUPS, 2 * N], U8, name="w2w", align_bytes=ALIGN, offset=w2_offset)
         nc.sync.dma_start(out=w2w[:].bitcast(I32), in_=w2_words.rearrange("a p c -> p a c").bitcast(I32))
-        w2s = late.tile([P, GROUPS, N], U8, name="w2s", align_bytes=ALIGN, offset=small + 128 + 4 * N)
+        w2s = late.tile([P, GROUPS, N], U8, name="w2s", align_bytes=ALIGN, offset=w2_offset + GROUPS * 2 * N)
         nc.vector.memset(w2s[:].rearrange("p a c -> p (a c)").bitcast(I32), 0)
         for q in range(QUADRANTS):
             nc.sync.dma_start(
@@ -121,27 +124,27 @@ def tile_list_redshift_gaussian_bumps_kernel(tc, tab, offs, w1, centre, gain, w2
 
         v_words = {}
         picked = keep.tile([P, S], U32, name="picked")
-        for n in range(2):
-            nc.vector.tensor_copy(picked[:], tab_words[n][:].indirect(offsets[:]))
-            if n == 0:
-                parted = keep.tile([P, 2, S], U16, name="parted", align_bytes=ALIGN)
-                nc.vector.tensor_copy(parted[:], picked[:].bitcast(U16).rearrange("p (j h) -> p h j", h=2))
-                v_words[0], v_words[1] = parted[:, 0, :], parted[:, 1, :]
+        nc.vector.tensor_copy(picked[:], tab_words[0][:].indirect(offsets[:]))
+        parted = keep.tile([P, 2, S], U16, name="parted", align_bytes=ALIGN)
+        nc.vector.tensor_copy(parted[:], picked[:].bitcast(U16).rearrange("p (j s) -> p s j", s=2))
+        v_words[0], v_words[1] = parted[:, 0, :], parted[:, 1, :]
+        nc.vector.tensor_copy(picked[:], tab_words[1][:].indirect(offsets[:]))
 
-        def part_second(h, pool, offset=None):
-            words = pool.tile([P, S], U16, name="parted%d" % h, align_bytes=ALIGN, offset=offset)
-            nc.vector.tensor_copy(words[:], picked[:].bitcast(U16)[:, h::2])
-            v_words[2 + h] = words[:]
+        def part_second(side, pool, offset=None):
+            words = pool.tile([P, S], U16, name="parted%d" % side, align_bytes=ALIGN, offset=offset)
+            nc.vector.tensor_copy(words[:], picked[:].bitcast(U16)[:, side::2])
+            v_words[2 + side] = words[:]
 
-        stage = early.tile([P, 3 * PACK * PASS], BF16, name="stage", align_bytes=ALIGN, offset=0)
+        STAGE_SLOTS = 12
+        stage = early.tile([P, STAGE_SLOTS * PASS], BF16, name="stage", align_bytes=ALIGN, offset=0)
 
         w1_grouped = {}
         w1_mx = {}
 
-        def group_w1(b, a, t0, on_scalar, place, area=stage, rows=slice(0, P)):
-            pair = area[:, place * PASS:(place + 2) * PASS]
-            dst = pair.rearrange("p (t m j) -> p m j t", t=2, j=PACK)[:, rows]
-            src = w1_raw[b, a].rearrange("p j (m t) -> p m j t", t=PACK)[:, rows, :, t0:t0 + 2]
+        def group_w1(b, a, t0, on_scalar, place, area=stage, outputs=slice(0, P)):
+            both = area[:, place * PASS:(place + 2) * PASS]
+            dst = both.rearrange("p (t m j) -> p m j t", t=2, j=PACK)[:, outputs]
+            src = w1_raw[b, a].rearrange("p j (m t) -> p m j t", t=PACK)[:, outputs, :, t0:t0 + 2]
             if on_scalar:
                 nc.scalar.activation(out=dst, in_=src, func=ACT.Copy)
             else:
@@ -162,10 +165,10 @@ def tile_list_redshift_gaussian_bumps_kernel(tc, tab, offs, w1, centre, gain, w2
 
         banks = {}
 
-        def project(b, half, steps):
+        def project(b, half, order):
             cols = slice(half * BANK, (half + 1) * BANK)
             done = [0] * PACK
-            for a, t in steps:
+            for a, t in order:
                 if done[t] == 0:
                     banks[b, half, t] = psum.tile([P, BANK], F32, name="bank")
                 codes, scales = w1_mx[b, a, t]
@@ -182,6 +185,10 @@ def tile_list_redshift_gaussian_bumps_kernel(tc, tab, offs, w1, centre, gain, w2
         def by_tile(passes):
             return [(a, t) for t in range(PACK) for a in passes]
 
+        def project_group(b):
+            project(b, 0, as_loaded(range(K_PASSES)))
+            project(b, 1, as_loaded([0]) + by_tile([3, 1, 2]))
+
         planes = {}
 
         def square(b, j0, width, t, sq):
@@ -196,8 +203,8 @@ def tile_list_redshift_gaussian_bumps_kernel(tc, tab, offs, w1, centre, gain, w2
             nc.scalar.activation(out=planes[b, half][:, t, :], in_=sq,
                                  func=ACT.Exp, scale=-1.0, bias=log_gain[:, b, t:t + 1])
 
-        def bell_plain(sq, e):
-            nc.scalar.activation(out=e, in_=sq, func=ACT.Exp, scale=-1.0)
+        def bell_plain(sq, bell):
+            nc.scalar.activation(out=bell, in_=sq, func=ACT.Exp, scale=-1.0)
 
         signed = {}
 
@@ -211,10 +218,10 @@ def tile_list_redshift_gaussian_bumps_kernel(tc, tab, offs, w1, centre, gain, w2
                     out=woven[:, c * PACK * CHUNK:(c + 1) * PACK * CHUNK].rearrange("p (c i t) -> p c t i", i=PACK, t=PACK),
                     in_=signed[b, half][:, :, c * CHUNK:(c + 1) * CHUNK].rearrange("p t (c i) -> p c t i", i=PACK))
 
-        def weave_gain(b, e, width, woven):
+        def weave_gain(b, bell, width, woven):
             nc.vector.tensor_tensor(
                 out=woven.rearrange("p (c i t) -> p c t i", i=2, t=PACK),
-                in0=e.rearrange("p t (c i) -> p c t i", i=2),
+                in0=bell.rearrange("p t (c i) -> p c t i", i=2),
                 in1=consts[:, GROUPS + b, :].unsqueeze(1).unsqueeze(3).to_broadcast([P, width // 2, PACK, 2]),
                 op=ALU.mult)
 
@@ -240,43 +247,42 @@ def tile_list_redshift_gaussian_bumps_kernel(tc, tab, offs, w1, centre, gain, w2
                         lhsT_scale=w2s[:, b, P * u:P * (u + 1)],
                         rhs=codes[:, c:c + width].bitcast(FP8X4), rhs_scale=scales[:, c:c + width],
                         start=(b == 0 and u == 0), stop=(b == GROUPS - 1 and u == N // P - 1))
-            step = 2 // len(staged)
+            share = N // P // len(staged)
             for i, part in enumerate(staged):
-                source = acc[:, i * step * width:(i + 1) * step * width]
+                result = acc[:, i * share * width:(i + 1) * share * width]
                 if on_scalar:
-                    nc.scalar.copy(out=part, in_=source)
+                    nc.scalar.copy(out=part, in_=result)
                 else:
-                    nc.vector.tensor_copy(out=part, in_=source)
-                nc.sync.dma_start(out=out_rows[:, i * step:(i + 1) * step, j0:j0 + width],
-                                  in_=part.rearrange("p (u j) -> p u j", u=step))
+                    nc.vector.tensor_copy(out=part, in_=result)
+                nc.sync.dma_start(out=out_rows[:, i * share:(i + 1) * share, j0:j0 + width],
+                                  in_=part.rearrange("p (u j) -> p u j", u=share))
 
-        for a in range(K_PASSES - 1):
-            if a == 0:
-                opening = early.tile([P, 2 * PASS], BF16, name="opening", align_bytes=ALIGN, offset=7 * PACK * PASS)
-                group_w1(0, a, 0, False, 0, opening)
-            else:
-                group_w1(0, a, 0, False, 4 * (a % 2))
-            group_w1(0, a, 2, True, 4 - 4 * (a % 2))
-            if a == 0:
-                part_second(0, keep)
+        opening_offset = (STAGE_SLOTS + 2) * SLOT
+        opening = early.tile([P, 2 * PASS], BF16, name="opening", align_bytes=ALIGN, offset=opening_offset)
+        group_w1(0, 0, 0, False, 0, opening)
+        group_w1(0, 0, 2, True, 4)
+        part_second(0, keep)
+        quantise_w1(0, 0, 0, 2)
+        quantise_w1(0, 0, 2, 2)
+        part_second(1, early, opening_offset)
+        for a, vector_place, scalar_place in ((1, 4, 0), (2, 0, 4)):
+            group_w1(0, a, 0, False, vector_place)
+            group_w1(0, a, 2, True, scalar_place)
             quantise_w1(0, a, 0, 2)
             quantise_w1(0, a, 2, 2)
-            if a == 0:
-                part_second(1, early, 7 * PACK * PASS)
-        first_pair = early.tile([P, 2 * PASS], BF16, name="first_pair", align_bytes=ALIGN, offset=6 * PACK * PASS)
-        group_w1(0, 3, 0, False, 0, first_pair)
+        leading = early.tile([P, 2 * PASS], BF16, name="leading", align_bytes=ALIGN, offset=STAGE_SLOTS * SLOT)
+        group_w1(0, 3, 0, False, 0, leading)
         group_w1(0, 3, 2, True, 0)
         quantise_w1(0, 3, 0, 1)
         quantise_w1(0, 3, 1, 1)
-        second_codes = early.tile([P, 2 * P], U32, name="second_codes", align_bytes=ALIGN, offset=6 * PACK * PASS)
+        second_codes = early.tile([P, 2 * P], U32, name="second_codes", align_bytes=ALIGN, offset=STAGE_SLOTS * SLOT)
         quantise_w1(0, 3, 2, 2, second_codes[:])
-        project(0, 0, as_loaded(range(4)))
-        project(0, 1, as_loaded([0]) + by_tile([3, 1, 2]))
+        project_group(0)
         for b, half in ((0, 1), (1, 0)):
             planes[b, half] = as_planes(keep.tile([P, PACK * BANK], BF16, name="planes%d" % b)[:])
 
-        def slots(first, count):
-            return stage[:, first * PASS:(first + count) * PASS]
+        def slots(place, count):
+            return stage[:, place * PASS:(place + count) * PASS]
 
         def plane_squares():
             return ring.tile([P, BANK], F32, name="sq", bufs=3)[:]
@@ -286,16 +292,16 @@ def tile_list_redshift_gaussian_bumps_kernel(tc, tab, offs, w1, centre, gain, w2
         bell_second = late.tile([P, PACK, CHUNK], F32, name="bell_second", offset=0)
         for t in range(PACK):
             square(0, 0, BANK, t, sq_open[:, t, :])
-        sq = {}
+        plane_sq = {}
         for t in range(PACK):
-            sq[t] = plane_squares()
-            square(0, BANK, BANK, t, sq[t])
+            plane_sq[t] = plane_squares()
+            square(0, BANK, BANK, t, plane_sq[t])
             if t == 0:
                 bell_plain(sq_open[:, :, CHUNK:BANK], bell_first[:])
             else:
-                bell_plane(0, 1, t - 1, sq[t - 1])
+                bell_plane(0, 1, t - 1, plane_sq[t - 1])
         bell_plain(sq_open[:, :, 0:CHUNK], bell_second[:])
-        bell_plane(0, 1, PACK - 1, sq[PACK - 1])
+        bell_plane(0, 1, PACK - 1, plane_sq[PACK - 1])
 
         for a in range(2):
             group_w1(1, a, 0, False, 4)
@@ -307,37 +313,36 @@ def tile_list_redshift_gaussian_bumps_kernel(tc, tab, offs, w1, centre, gain, w2
         group_w1(1, 2, 2, False, 3)
         quantise_w1(1, 2, 0, 2)
         quantise_w1(1, 2, 2, 2)
-        border = PACK * PASS
-        signed[0, 1] = as_planes(raw_end[:, border - BANK // 2:border + 3 * BANK // 2].bitcast(BF16))
+        plane_words = BANK // 2
+        signed[0, 1] = as_planes(raw_end[:, border - plane_words:border + 3 * plane_words].bitcast(BF16))
         sign(0, 1, 0)
         group_w1(1, 3, 0, False, 3)
-        group_w1(1, 3, 2, False, 1, rows=slice(0, P // 2))
+        group_w1(1, 3, 2, False, 1, outputs=slice(0, P // 2))
         quantise_w1(1, 3, 0, 1)
         quantise_w1(1, 3, 1, 1)
-        group_w1(1, 3, 2, True, 1, rows=slice(P // 2, P))
+        group_w1(1, 3, 2, True, 1, outputs=slice(P // 2, P))
         weave_gain(0, bell_first[:, :, 0:P], P, slots(4, 1))
         quantise_w1(1, 3, 2, 2)
-        project(1, 0, as_loaded(range(4)))
-        project(1, 1, as_loaded([0]) + by_tile([3, 1, 2]))
+        project_group(1)
         for t in range(1, PACK):
             sign(0, 1, t)
         weave_gain(0, bell_second[:], CHUNK, slots(2, 2))
-        held = keep.tile([P, PACK * BANK], BF16, name="woven0", align_bytes=ALIGN)
-        weave(0, 1, held[:])
+        woven0 = keep.tile([P, PACK * BANK], BF16, name="woven0", align_bytes=ALIGN)
+        weave(0, 1, woven0[:])
         quantise_h(0, 0, BANK, slots(2, 4))
 
         third = keep.tile([P, PACK, CHUNK], F32, name="sq_third")
-        seventh = late.tile([P, PACK, P], F32, name="sq_seventh", offset=RAW)
-        eighth = late.tile([P, PACK, P], F32, name="sq_eighth", offset=2 * RAW)
+        seventh = late.tile([P, PACK, P], F32, name="sq_seventh", offset=PIECE)
+        eighth = late.tile([P, PACK, P], F32, name="sq_eighth", offset=2 * PIECE)
         bell_third = keep.tile([P, PACK, CHUNK], F32, name="bell_third")
-        bell_seventh = keep.tile([P, PACK, P], F32, name="bell_seventh")
+        bell_seventh = keep.tile([P, 2, PACK, P // 2], F32, name="bell_seventh")
         bell_eighth = keep.tile([P, 2, PACK, P // 2], F32, name="bell_eighth")
         for t in range(PACK):
-            sq[t] = plane_squares()
-            square(1, 0, BANK, t, sq[t])
+            plane_sq[t] = plane_squares()
+            square(1, 0, BANK, t, plane_sq[t])
             if t > 0:
-                bell_plane(1, 0, t - 1, sq[t - 1])
-        bell_plane(1, 0, PACK - 1, sq[PACK - 1])
+                bell_plane(1, 0, t - 1, plane_sq[t - 1])
+        bell_plane(1, 0, PACK - 1, plane_sq[PACK - 1])
         for t in range(PACK):
             square(1, BANK, CHUNK, t, third[:, t, :])
         for t in range(2):
@@ -347,39 +352,39 @@ def tile_list_redshift_gaussian_bumps_kernel(tc, tab, offs, w1, centre, gain, w2
             square(1, S - CHUNK, P, t, seventh[:, t, :])
         for t in range(2):
             square(1, S - P, P, t, eighth[:, t, :])
-        bell_plain(seventh[:], bell_seventh[:])
+        bell_plain(seventh[:, :, 0:P // 2], bell_seventh[:, 0])
         for t in range(2, PACK):
             square(1, S - P, P, t, eighth[:, t, :])
+        bell_plain(seventh[:, :, P // 2:P], bell_seventh[:, 1])
         for i in range(2):
             bell_plain(eighth[:, :, i * P // 2:(i + 1) * P // 2], bell_eighth[:, i])
 
-        woven = keep.tile([P, PACK * S], BF16, name="woven1", align_bytes=ALIGN)
+        woven1 = keep.tile([P, PACK * S], BF16, name="woven1", align_bytes=ALIGN)
 
         def columns(j0, width):
-            return woven[:, PACK * j0:PACK * (j0 + width)]
+            return woven1[:, PACK * j0:PACK * (j0 + width)]
 
         signed[1, 0] = as_planes(late.tile([P, PACK * BANK], BF16, name="signed1", offset=0)[:])
-        sign(1, 0, 0)
-        sign(1, 0, 1)
-        quantise_h(0, BANK, CHUNK, held[:, 0:PACK * CHUNK])
-        sign(1, 0, 2)
-        sign(1, 0, 3)
-        quantise_h(0, S - CHUNK, CHUNK, held[:, PACK * CHUNK:])
+        for c in range(BANK // CHUNK):
+            sign(1, 0, 2 * c)
+            sign(1, 0, 2 * c + 1)
+            quantise_h(0, BANK + c * CHUNK, CHUNK, woven0[:, c * PACK * CHUNK:(c + 1) * PACK * CHUNK])
         weave(1, 0, columns(0, BANK))
         for j0 in (0, CHUNK):
             quantise_h(1, j0, CHUNK, columns(j0, CHUNK))
         weave_gain(1, bell_third[:], CHUNK, columns(BANK, CHUNK))
-        weave_gain(1, bell_seventh[:], P, columns(S - CHUNK, P))
+        weave_gain(1, bell_seventh[:, 0], P // 2, columns(S - CHUNK, P // 2))
         quantise_h(1, BANK, CHUNK, columns(BANK, CHUNK))
+        weave_gain(1, bell_seventh[:, 1], P // 2, columns(S - CHUNK + P // 2, P // 2))
         for i in range(2):
             weave_gain(1, bell_eighth[:, i], P // 2, columns(S - P + i * P // 2, P // 2))
         quantise_h(1, S - CHUNK, P, columns(S - CHUNK, P))
         quantise_h(1, S - P, P, columns(S - P, P))
-        staged_first = late.tile([P, CHUNK], F32, name="staged_first", offset=RAW)
-        staged = late.tile([P, 6 * CHUNK], F32, name="staged", offset=2 * RAW)
-        finish(0, CHUNK, True, [staged_first[:], staged[:, 0:CHUNK]])
-        finish(CHUNK, CHUNK, True, [staged[:, CHUNK:3 * CHUNK]])
-        finish(BANK, CHUNK, True, [staged[:, 3 * CHUNK:5 * CHUNK]])
-        finish(S - CHUNK, P, True, [staged[:, 5 * CHUNK:]])
+
+        staged_rest = late.tile([P, 7 * CHUNK], F32, name="staged", offset=2 * PIECE)
+        finish(0, CHUNK, True, [staged_rest[:, 0:CHUNK], staged_rest[:, CHUNK:2 * CHUNK]])
+        finish(CHUNK, CHUNK, True, [staged_rest[:, 2 * CHUNK:4 * CHUNK]])
+        finish(BANK, CHUNK, True, [staged_rest[:, 4 * CHUNK:6 * CHUNK]])
+        finish(S - CHUNK, P, True, [staged_rest[:, 6 * CHUNK:]])
         staged_last = keep.tile([P, CHUNK], F32, name="staged_last")
         finish(S - P, P, False, [staged_last[:]])

@@ -106,12 +106,11 @@ def tile_list_redshift_gaussian_bumps_kernel(tc, tab, offs, w1, centre, gain, w2
         late = ctx.enter_context(tc.tile_pool(name="late", bufs=1))
         for a in range(K_PASSES):
             load_w1(late, 0, a, a * PIECE)
-        for a in range(2):
-            load_w1(late, 1, a, (K_PASSES + a) * PIECE)
+        load_w1(late, 1, 0, K_PASSES * PIECE)
         border = PACK * PASS
-        raw_end = late.tile([P, 2 * border], F32, name="raw_end", offset=(K_PASSES + 2) * PIECE)
-        for i in range(2):
-            load_w1(late, 1, 2 + i, area=raw_end[:, i * border:(i + 1) * border])
+        raw_end = late.tile([P, 3 * border], F32, name="raw_end", offset=(K_PASSES + 1) * PIECE)
+        for i in range(3):
+            load_w1(late, 1, 1 + i, area=raw_end[:, i * border:(i + 1) * border])
         w2_offset = GROUPS * K_PASSES * PIECE + 2 * ALIGN
         w2w = late.tile([P, GROUPS, 2 * N], U8, name="w2w", align_bytes=ALIGN, offset=w2_offset)
         nc.sync.dma_start(out=w2w[:].bitcast(I32), in_=w2_words.rearrange("a p c -> p a c").bitcast(I32))
@@ -212,8 +211,8 @@ def tile_list_redshift_gaussian_bumps_kernel(tc, tab, offs, w1, centre, gain, w2
             nc.vector.tensor_scalar(out=signed[b, half][:, t, :], in0=planes[b, half][:, t, :],
                                     scalar1=signs[:, b, t:t + 1], scalar2=None, op0=ALU.mult)
 
-        def weave(b, half, woven):
-            for c in range(BANK // CHUNK):
+        def weave(b, half, woven, chunks=(0, 1)):
+            for c in chunks:
                 nc.vector.tensor_copy(
                     out=woven[:, c * PACK * CHUNK:(c + 1) * PACK * CHUNK].rearrange("p (c i t) -> p c t i", i=PACK, t=PACK),
                     in_=signed[b, half][:, :, c * CHUNK:(c + 1) * CHUNK].rearrange("p t (c i) -> p c t i", i=PACK))
@@ -278,8 +277,8 @@ def tile_list_redshift_gaussian_bumps_kernel(tc, tab, offs, w1, centre, gain, w2
         second_codes = early.tile([P, 2 * P], U32, name="second_codes", align_bytes=ALIGN, offset=STAGE_SLOTS * SLOT)
         quantise_w1(0, 3, 2, 2, second_codes[:])
         project_group(0)
-        for b, half in ((0, 1), (1, 0)):
-            planes[b, half] = as_planes(keep.tile([P, PACK * BANK], BF16, name="planes%d" % b)[:])
+        for b, half in ((0, 0), (0, 1), (1, 0)):
+            planes[b, half] = as_planes(keep.tile([P, PACK * BANK], BF16, name="planes%d%d" % (b, half))[:])
 
         def slots(place, count):
             return stage[:, place * PASS:(place + count) * PASS]
@@ -288,53 +287,56 @@ def tile_list_redshift_gaussian_bumps_kernel(tc, tab, offs, w1, centre, gain, w2
             return ring.tile([P, BANK], F32, name="sq", bufs=3)[:]
 
         sq_open = keep.tile([P, PACK, BANK], F32, name="sq_open")
-        bell_first = keep.tile([P, PACK, CHUNK], F32, name="bell_first")
-        bell_second = late.tile([P, PACK, CHUNK], F32, name="bell_second", offset=0)
         for t in range(PACK):
             square(0, 0, BANK, t, sq_open[:, t, :])
+        bell_plane(0, 0, 0, sq_open[:, 0, :])
+        bell_plane(0, 0, 1, sq_open[:, 1, :])
         plane_sq = {}
         for t in range(PACK):
             plane_sq[t] = plane_squares()
             square(0, BANK, BANK, t, plane_sq[t])
-            if t == 0:
-                bell_plain(sq_open[:, :, CHUNK:BANK], bell_first[:])
+            if t < 2:
+                bell_plane(0, 0, 2 + t, sq_open[:, 2 + t, :])
             else:
-                bell_plane(0, 1, t - 1, plane_sq[t - 1])
-        bell_plain(sq_open[:, :, 0:CHUNK], bell_second[:])
-        bell_plane(0, 1, PACK - 1, plane_sq[PACK - 1])
+                bell_plane(0, 1, t - 2, plane_sq[t - 2])
+        for t in range(2, PACK):
+            bell_plane(0, 1, t, plane_sq[t])
 
+        plane_words = BANK // 2
+        signed[0, 0] = as_planes(raw_end[:, border - 3 * plane_words:border + plane_words].bitcast(BF16))
+        signed[0, 1] = as_planes(raw_end[:, 2 * border:2 * border + PACK * plane_words].bitcast(BF16))
         for a in range(2):
             group_w1(1, a, 0, False, 4)
             group_w1(1, a, 2, False, 0)
             quantise_w1(1, a, 0, 2)
             quantise_w1(1, a, 2, 2)
-        weave_gain(0, bell_first[:, :, P:CHUNK], P, slots(5, 1))
+        for t in range(3):
+            sign(0, 0, t)
         group_w1(1, 2, 0, False, 0)
         group_w1(1, 2, 2, False, 3)
         quantise_w1(1, 2, 0, 2)
         quantise_w1(1, 2, 2, 2)
-        plane_words = BANK // 2
-        signed[0, 1] = as_planes(raw_end[:, border - plane_words:border + 3 * plane_words].bitcast(BF16))
-        sign(0, 1, 0)
+        sign(0, 0, 3)
         group_w1(1, 3, 0, False, 3)
         group_w1(1, 3, 2, False, 1, outputs=slice(0, P // 2))
         quantise_w1(1, 3, 0, 1)
         quantise_w1(1, 3, 1, 1)
         group_w1(1, 3, 2, True, 1, outputs=slice(P // 2, P))
-        weave_gain(0, bell_first[:, :, 0:P], P, slots(4, 1))
+        weave(0, 0, slots(2, 4), (1,))
         quantise_w1(1, 3, 2, 2)
         project_group(1)
-        for t in range(1, PACK):
+        for t in range(2):
             sign(0, 1, t)
-        weave_gain(0, bell_second[:], CHUNK, slots(2, 2))
-        woven0 = keep.tile([P, PACK * BANK], BF16, name="woven0", align_bytes=ALIGN)
-        weave(0, 1, woven0[:])
+        weave(0, 0, slots(2, 4), (0,))
+        for t in range(2, PACK):
+            sign(0, 1, t)
         quantise_h(0, 0, BANK, slots(2, 4))
-
+        woven0 = keep.tile([P, PACK * BANK], BF16, name="woven0", align_bytes=ALIGN)
         third = keep.tile([P, PACK, CHUNK], F32, name="sq_third")
-        seventh = late.tile([P, PACK, P], F32, name="sq_seventh", offset=PIECE)
-        eighth = late.tile([P, PACK, P], F32, name="sq_eighth", offset=2 * PIECE)
-        bell_third = keep.tile([P, PACK, CHUNK], F32, name="bell_third")
+        weave(0, 1, woven0[:])
+
+        fourth = late.tile([P, PACK, CHUNK], F32, name="sq_fourth", offset=2 * PIECE)
+        bell_third = keep.tile([P, 2, PACK, P], F32, name="bell_third")
         bell_seventh = keep.tile([P, 2, PACK, P // 2], F32, name="bell_seventh")
         bell_eighth = keep.tile([P, 2, PACK, P // 2], F32, name="bell_eighth")
         for t in range(PACK):
@@ -345,26 +347,21 @@ def tile_list_redshift_gaussian_bumps_kernel(tc, tab, offs, w1, centre, gain, w2
         bell_plane(1, 0, PACK - 1, plane_sq[PACK - 1])
         for t in range(PACK):
             square(1, BANK, CHUNK, t, third[:, t, :])
-        for t in range(2):
-            square(1, S - CHUNK, P, t, seventh[:, t, :])
-        bell_plain(third[:], bell_third[:])
-        for t in range(2, PACK):
-            square(1, S - CHUNK, P, t, seventh[:, t, :])
-        for t in range(2):
-            square(1, S - P, P, t, eighth[:, t, :])
-        bell_plain(seventh[:, :, 0:P // 2], bell_seventh[:, 0])
-        for t in range(2, PACK):
-            square(1, S - P, P, t, eighth[:, t, :])
-        bell_plain(seventh[:, :, P // 2:P], bell_seventh[:, 1])
         for i in range(2):
-            bell_plain(eighth[:, :, i * P // 2:(i + 1) * P // 2], bell_eighth[:, i])
+            for t in (2 * i, 2 * i + 1):
+                square(1, S - CHUNK, CHUNK, t, fourth[:, t, :])
+            bell_plain(third[:, :, i * P:(i + 1) * P], bell_third[:, i])
+        for i in range(2):
+            bell_plain(fourth[:, :, i * P // 2:(i + 1) * P // 2], bell_seventh[:, i])
+        for i in range(2):
+            bell_plain(fourth[:, :, P + i * P // 2:P + (i + 1) * P // 2], bell_eighth[:, i])
 
         woven1 = keep.tile([P, PACK * S], BF16, name="woven1", align_bytes=ALIGN)
 
         def columns(j0, width):
             return woven1[:, PACK * j0:PACK * (j0 + width)]
 
-        signed[1, 0] = as_planes(late.tile([P, PACK * BANK], BF16, name="signed1", offset=0)[:])
+        signed[1, 0] = signed[0, 1]
         for c in range(BANK // CHUNK):
             sign(1, 0, 2 * c)
             sign(1, 0, 2 * c + 1)
@@ -372,7 +369,8 @@ def tile_list_redshift_gaussian_bumps_kernel(tc, tab, offs, w1, centre, gain, w2
         weave(1, 0, columns(0, BANK))
         for j0 in (0, CHUNK):
             quantise_h(1, j0, CHUNK, columns(j0, CHUNK))
-        weave_gain(1, bell_third[:], CHUNK, columns(BANK, CHUNK))
+        for i in range(2):
+            weave_gain(1, bell_third[:, i], P, columns(BANK + i * P, P))
         weave_gain(1, bell_seventh[:, 0], P // 2, columns(S - CHUNK, P // 2))
         quantise_h(1, BANK, CHUNK, columns(BANK, CHUNK))
         weave_gain(1, bell_seventh[:, 1], P // 2, columns(S - CHUNK + P // 2, P // 2))

@@ -27,7 +27,8 @@ BLOCKS = 16
 K_PASSES = K // PASS
 GROUPS = H // PASS
 ALIGN = 64
-LN_RANGE = 60
+LAST = PACK - 1
+LN_RANGE = 64
 PIECE = 4 * PACK * PASS
 SLOT = 2 * PASS
 
@@ -88,15 +89,29 @@ def tile_list_redshift_gaussian_bumps_kernel(tc, tab, offs, w1, centre, gain, w2
             gains = consts[:, GROUPS:, :]
             size = keep.tile([P, GROUPS, PACK], F32, name="size")
             nc.scalar.activation(out=size[:], in_=gains, func=ACT.Abs)
-            bounded = keep.tile([P, GROUPS, PACK], F32, name="bounded")
-            nc.gpsimd.tensor_scalar(out=bounded[:], in0=size[:], scalar1=2.0 ** -LN_RANGE, scalar2=2.0 ** LN_RANGE,
+            factors = keep.tile([P, GROUPS, PACK + 2], F32, name="factors")
+            low, high = 2.0 ** -LN_RANGE, 2.0 ** LN_RANGE
+            nc.gpsimd.tensor_scalar(out=factors[:, :, 0:PACK], in0=size[:], scalar1=low, scalar2=high,
                                     op0=ALU.max, op1=ALU.min)
-            log_gain = keep.tile([P, GROUPS, PACK], F32, name="log_gain")
-            nc.scalar.activation(out=log_gain[:], in_=bounded[:], func=ACT.Ln)
-            inverse = keep.tile([P, GROUPS, PACK], F32, name="inverse")
-            nc.scalar.activation(out=inverse[:], in_=log_gain[:], func=ACT.Exp, scale=-1.0)
-            signs = keep.tile([P, GROUPS, PACK], F32, name="signs")
-            nc.gpsimd.tensor_tensor(out=signs[:], in0=gains, in1=inverse[:], op=ALU.mult)
+            below = keep.tile([P, GROUPS, 1], F32, name="below")
+            nc.gpsimd.tensor_scalar(out=below[:], in0=size[:, :, LAST:], scalar1=low, scalar2=high,
+                                    op0=ALU.min, op1=ALU.mult)
+            nc.gpsimd.tensor_scalar(out=factors[:, :, PACK:PACK + 1], in0=size[:, :, LAST:], scalar1=high, scalar2=low,
+                                    op0=ALU.max, op1=ALU.mult)
+            nc.gpsimd.tensor_scalar(out=factors[:, :, PACK + 1:], in0=below[:], scalar1=low, scalar2=None, op0=ALU.max)
+            logs = keep.tile([P, GROUPS, PACK + 2], F32, name="logs")
+            nc.scalar.activation(out=logs[:], in_=factors[:], func=ACT.Ln)
+            inverse = keep.tile([P, GROUPS, LAST], F32, name="inverse")
+            nc.scalar.activation(out=inverse[:], in_=logs[:, :, 0:LAST], func=ACT.Exp, scale=-1.0)
+            rests = keep.tile([P, GROUPS, LAST], F32, name="rests")
+            nc.gpsimd.tensor_tensor(out=rests[:], in0=gains[:, :, 0:LAST], in1=inverse[:], op=ALU.mult)
+            last_log = keep.tile([P, GROUPS, 1], F32, name="last_log")
+            nc.vector.tensor_reduce(out=last_log[:], in_=logs[:, :, LAST:], axis=mybir.AxisListType.X, op=ALU.add)
+            doubled = keep.tile([P, GROUPS, 1], F32, name="doubled")
+            nc.gpsimd.tensor_scalar(out=doubled[:], in0=gains[:, :, LAST:], scalar1=0.0, scalar2=2.0,
+                                    op0=ALU.is_ge, op1=ALU.mult)
+            last_sign = keep.tile([P, GROUPS, 1], F32, name="last_sign")
+            nc.gpsimd.tensor_scalar(out=last_sign[:], in0=doubled[:], scalar1=1.0, scalar2=None, op0=ALU.subtract)
             nc.vector.tensor_copy(picked_scales[:], tab_scales[:].indirect(offsets[:]))
         for q in (0, 2, 1, 3):
             source = 32 + BLOCKS * q
@@ -106,12 +121,14 @@ def tile_list_redshift_gaussian_bumps_kernel(tc, tab, offs, w1, centre, gain, w2
         late = ctx.enter_context(tc.tile_pool(name="late", bufs=1))
         for a in range(K_PASSES):
             load_w1(late, 0, a, a * PIECE)
-        load_w1(late, 1, 0, K_PASSES * PIECE)
         border = PACK * PASS
-        raw_end = late.tile([P, 3 * border], F32, name="raw_end", offset=(K_PASSES + 1) * PIECE)
-        for i in range(3):
-            load_w1(late, 1, 1 + i, area=raw_end[:, i * border:(i + 1) * border])
-        w2_offset = GROUPS * K_PASSES * PIECE + 2 * ALIGN
+        plane_words = BANK // 2
+        starts = [a * border + (plane_words if a >= 2 else 0) for a in range(K_PASSES)]
+        raw_words = starts[3] + 2 * border
+        raw_end = late.tile([P, raw_words], F32, name="raw_end", offset=K_PASSES * PIECE)
+        for a in range(K_PASSES):
+            load_w1(late, 1, a, area=raw_end[:, starts[a]:starts[a] + border])
+        w2_offset = K_PASSES * PIECE + 4 * raw_words
         w2w = late.tile([P, GROUPS, 2 * N], U8, name="w2w", align_bytes=ALIGN, offset=w2_offset)
         nc.sync.dma_start(out=w2w[:].bitcast(I32), in_=w2_words.rearrange("a p c -> p a c").bitcast(I32))
         w2s = late.tile([P, GROUPS, N], U8, name="w2s", align_bytes=ALIGN, offset=w2_offset + GROUPS * 2 * N)
@@ -198,31 +215,21 @@ def tile_list_redshift_gaussian_bumps_kernel(tc, tab, offs, w1, centre, gain, w2
         def as_planes(area):
             return area.rearrange("p (t j) -> p t j", t=PACK)
 
-        def bell_plane(b, half, t, sq):
-            nc.scalar.activation(out=planes[b, half][:, t, :], in_=sq,
-                                 func=ACT.Exp, scale=-1.0, bias=log_gain[:, b, t:t + 1])
-
-        def bell_plain(sq, bell):
-            nc.scalar.activation(out=bell, in_=sq, func=ACT.Exp, scale=-1.0)
-
         signed = {}
 
-        def sign(b, half, t):
-            nc.vector.tensor_scalar(out=signed[b, half][:, t, :], in0=planes[b, half][:, t, :],
-                                    scalar1=signs[:, b, t:t + 1], scalar2=None, op0=ALU.mult)
+        def bell_plane(b, unit, t, sq, cols=slice(None)):
+            target, bias = (signed, last_log[:, b, :]) if t == LAST else (planes, logs[:, b, t:t + 1])
+            nc.scalar.activation(out=target[b, unit][:, t, cols], in_=sq[:, cols], func=ACT.Exp, scale=-1.0, bias=bias)
 
-        def weave(b, half, woven, chunks=(0, 1)):
-            for c in chunks:
-                nc.vector.tensor_copy(
-                    out=woven[:, c * PACK * CHUNK:(c + 1) * PACK * CHUNK].rearrange("p (c i t) -> p c t i", i=PACK, t=PACK),
-                    in_=signed[b, half][:, :, c * CHUNK:(c + 1) * CHUNK].rearrange("p t (c i) -> p c t i", i=PACK))
+        def sign(b, unit, t):
+            nc.vector.tensor_scalar(out=signed[b, unit][:, t, :], in0=planes[b, unit][:, t, :],
+                                    scalar1=rests[:, b, t:t + 1], scalar2=last_sign[:, b, :], op0=ALU.mult, op1=ALU.mult)
 
-        def weave_gain(b, bell, width, woven):
-            nc.vector.tensor_tensor(
-                out=woven.rearrange("p (c i t) -> p c t i", i=2, t=PACK),
-                in0=bell.rearrange("p t (c i) -> p c t i", i=2),
-                in1=consts[:, GROUPS + b, :].unsqueeze(1).unsqueeze(3).to_broadcast([P, width // 2, PACK, 2]),
-                op=ALU.mult)
+        def weave(b, unit, woven, c0, width):
+            nc.vector.tensor_scalar(
+                out=woven[:, PACK * c0:PACK * (c0 + width)].rearrange("p (c i t) -> p c t i", i=PACK, t=PACK),
+                in0=signed[b, unit][:, :, c0:c0 + width].rearrange("p t (c i) -> p c t i", i=PACK),
+                scalar1=last_sign[:, b, :], scalar2=None, op0=ALU.mult)
 
         h_mx = {}
 
@@ -278,7 +285,15 @@ def tile_list_redshift_gaussian_bumps_kernel(tc, tab, offs, w1, centre, gain, w2
         quantise_w1(0, 3, 2, 2, second_codes[:])
         project_group(0)
         for b, half in ((0, 0), (0, 1), (1, 0)):
-            planes[b, half] = as_planes(keep.tile([P, PACK * BANK], BF16, name="planes%d%d" % (b, half))[:])
+            planes[b, half] = keep.tile([P, LAST, BANK], BF16, name="planes%d%d_wide" % (b, half))
+
+        def laid(first, pitch):
+            area = raw_end[:, first:first + PACK * pitch].bitcast(BF16)
+            return as_planes(area)[:, :, 0:BANK]
+
+        signed[0, 0] = laid(2 * border - LAST * plane_words, plane_words)
+        signed[0, 1] = laid(starts[3] - border // 2, border // 2)
+        signed[1, 0] = laid(starts[3] - border // 2, border // 2 + 96)
 
         def slots(place, count):
             return stage[:, place * PASS:(place + count) * PASS]
@@ -286,98 +301,92 @@ def tile_list_redshift_gaussian_bumps_kernel(tc, tab, offs, w1, centre, gain, w2
         def plane_squares():
             return ring.tile([P, BANK], F32, name="sq", bufs=3)[:]
 
+        for a in range(2):
+            group_w1(1, a, 0, False, 4)
+            group_w1(1, a, 2, False, 0)
+            quantise_w1(1, a, 0, 2)
+            quantise_w1(1, a, 2, 2)
+
         sq_open = keep.tile([P, PACK, BANK], F32, name="sq_open")
         for t in range(PACK):
             square(0, 0, BANK, t, sq_open[:, t, :])
         bell_plane(0, 0, 0, sq_open[:, 0, :])
         bell_plane(0, 0, 1, sq_open[:, 1, :])
         plane_sq = {}
-        for t in range(PACK):
+        between = ((0, 2), (1, 0), (0, LAST), (1, 1))
+        for t, (half, plane) in enumerate(between):
             plane_sq[t] = plane_squares()
             square(0, BANK, BANK, t, plane_sq[t])
-            if t < 2:
-                bell_plane(0, 0, 2 + t, sq_open[:, 2 + t, :])
-            else:
-                bell_plane(0, 1, t - 2, plane_sq[t - 2])
+            bell_plane(0, half, plane, plane_sq[plane] if half else sq_open[:, plane, :])
         for t in range(2, PACK):
             bell_plane(0, 1, t, plane_sq[t])
 
-        plane_words = BANK // 2
-        signed[0, 0] = as_planes(raw_end[:, border - 3 * plane_words:border + plane_words].bitcast(BF16))
-        signed[0, 1] = as_planes(raw_end[:, 2 * border:2 * border + PACK * plane_words].bitcast(BF16))
-        for a in range(2):
-            group_w1(1, a, 0, False, 4)
-            group_w1(1, a, 2, False, 0)
-            quantise_w1(1, a, 0, 2)
-            quantise_w1(1, a, 2, 2)
         for t in range(3):
             sign(0, 0, t)
         group_w1(1, 2, 0, False, 0)
         group_w1(1, 2, 2, False, 3)
         quantise_w1(1, 2, 0, 2)
         quantise_w1(1, 2, 2, 2)
-        sign(0, 0, 3)
+        sign(0, 1, 0)
         group_w1(1, 3, 0, False, 3)
         group_w1(1, 3, 2, False, 1, outputs=slice(0, P // 2))
         quantise_w1(1, 3, 0, 1)
         quantise_w1(1, 3, 1, 1)
         group_w1(1, 3, 2, True, 1, outputs=slice(P // 2, P))
-        weave(0, 0, slots(2, 4), (1,))
+        weave(0, 0, slots(2, 4), CHUNK, CHUNK)
         quantise_w1(1, 3, 2, 2)
         project_group(1)
-        for t in range(2):
-            sign(0, 1, t)
-        weave(0, 0, slots(2, 4), (0,))
-        for t in range(2, PACK):
+        weave(0, 0, slots(2, 4), 0, CHUNK)
+        for t in range(1, LAST):
             sign(0, 1, t)
         quantise_h(0, 0, BANK, slots(2, 4))
         woven0 = keep.tile([P, PACK * BANK], BF16, name="woven0", align_bytes=ALIGN)
-        third = keep.tile([P, PACK, CHUNK], F32, name="sq_third")
-        weave(0, 1, woven0[:])
+        for c0 in (0, CHUNK):
+            weave(0, 1, woven0[:], c0, CHUNK)
 
         fourth = late.tile([P, PACK, CHUNK], F32, name="sq_fourth", offset=2 * PIECE)
-        bell_third = keep.tile([P, 2, PACK, P], F32, name="bell_third")
-        bell_seventh = keep.tile([P, 2, PACK, P // 2], F32, name="bell_seventh")
-        bell_eighth = keep.tile([P, 2, PACK, P // 2], F32, name="bell_eighth")
+        third = keep.tile([P, PACK, CHUNK], F32, name="sq_third")
+        for unit in (1, 2):
+            planes[1, unit] = keep.tile([P, LAST, CHUNK], BF16, name="planes1%d" % unit)
+            signed[1, unit] = keep.tile([P, PACK, CHUNK], BF16, name="signed1%d" % unit)
         for t in range(PACK):
             plane_sq[t] = plane_squares()
             square(1, 0, BANK, t, plane_sq[t])
             if t > 0:
                 bell_plane(1, 0, t - 1, plane_sq[t - 1])
-        bell_plane(1, 0, PACK - 1, plane_sq[PACK - 1])
-        for t in range(PACK):
-            square(1, BANK, CHUNK, t, third[:, t, :])
-        for i in range(2):
-            for t in (2 * i, 2 * i + 1):
-                square(1, S - CHUNK, CHUNK, t, fourth[:, t, :])
-            bell_plain(third[:, :, i * P:(i + 1) * P], bell_third[:, i])
-        for i in range(2):
-            bell_plain(fourth[:, :, i * P // 2:(i + 1) * P // 2], bell_seventh[:, i])
-        for i in range(2):
-            bell_plain(fourth[:, :, P + i * P // 2:P + (i + 1) * P // 2], bell_eighth[:, i])
+        bell_plane(1, 0, LAST, plane_sq[LAST])
+        steps = [(unit, t, sq[:, t, :]) for unit, sq in ((1, third), (2, fourth)) for t in range(PACK)]
+        for i, (unit, t, sq) in enumerate(steps):
+            square(1, BANK + (unit - 1) * CHUNK, CHUNK, t, sq)
+            if i > 0:
+                bell_plane(1, *steps[i - 1])
+        for c0 in (0, P):
+            bell_plane(1, 2, LAST, fourth[:, LAST, :], slice(c0, c0 + P))
 
         woven1 = keep.tile([P, PACK * S], BF16, name="woven1", align_bytes=ALIGN)
 
         def columns(j0, width):
             return woven1[:, PACK * j0:PACK * (j0 + width)]
 
-        signed[1, 0] = signed[0, 1]
         for c in range(BANK // CHUNK):
-            sign(1, 0, 2 * c)
-            sign(1, 0, 2 * c + 1)
+            for t in range(2 * c, min(2 * c + 2, LAST)):
+                sign(1, 0, t)
             quantise_h(0, BANK + c * CHUNK, CHUNK, woven0[:, c * PACK * CHUNK:(c + 1) * PACK * CHUNK])
-        weave(1, 0, columns(0, BANK))
+        for c0 in (0, CHUNK):
+            weave(1, 0, columns(0, BANK), c0, CHUNK)
         for j0 in (0, CHUNK):
             quantise_h(1, j0, CHUNK, columns(j0, CHUNK))
-        for i in range(2):
-            weave_gain(1, bell_third[:, i], P, columns(BANK + i * P, P))
-        weave_gain(1, bell_seventh[:, 0], P // 2, columns(S - CHUNK, P // 2))
+        for t in range(LAST):
+            sign(1, 1, t)
+        weave(1, 1, columns(BANK, CHUNK), 0, CHUNK)
+        sign(1, 2, 0)
         quantise_h(1, BANK, CHUNK, columns(BANK, CHUNK))
-        weave_gain(1, bell_seventh[:, 1], P // 2, columns(S - CHUNK + P // 2, P // 2))
-        for i in range(2):
-            weave_gain(1, bell_eighth[:, i], P // 2, columns(S - P + i * P // 2, P // 2))
-        quantise_h(1, S - CHUNK, P, columns(S - CHUNK, P))
-        quantise_h(1, S - P, P, columns(S - P, P))
+        for t in range(1, LAST):
+            sign(1, 2, t)
+        for c0 in (0, P):
+            weave(1, 2, columns(S - CHUNK, CHUNK), c0, P)
+        for j0 in (S - CHUNK, S - P):
+            quantise_h(1, j0, P, columns(j0, P))
 
         staged_rest = late.tile([P, 7 * CHUNK], F32, name="staged", offset=2 * PIECE)
         finish(0, CHUNK, True, [staged_rest[:, 0:CHUNK], staged_rest[:, CHUNK:2 * CHUNK]])

@@ -89,29 +89,36 @@ def tile_list_redshift_gaussian_bumps_kernel(tc, tab, offs, w1, centre, gain, w2
             gains = consts[:, GROUPS:, :]
             size = keep.tile([P, GROUPS, PACK], F32, name="size")
             nc.scalar.activation(out=size[:], in_=gains, func=ACT.Abs)
-            factors = keep.tile([P, GROUPS, PACK + 2], F32, name="factors")
+            factors = keep.tile([P, GROUPS, PACK + 1], F32, name="factors")
             low, high = 2.0 ** -LN_RANGE, 2.0 ** LN_RANGE
-            nc.gpsimd.tensor_scalar(out=factors[:, :, 0:PACK], in0=size[:], scalar1=low, scalar2=high,
-                                    op0=ALU.max, op1=ALU.min)
-            below = keep.tile([P, GROUPS, 1], F32, name="below")
-            nc.gpsimd.tensor_scalar(out=below[:], in0=size[:, :, LAST:], scalar1=low, scalar2=high,
+            below = keep.tile([P, GROUPS], F32, name="below")
+            above = keep.tile([P, GROUPS], F32, name="above")
+            doubled = keep.tile([P, GROUPS], F32, name="doubled")
+            last_sign = keep.tile([P, GROUPS, 1], F32, name="last_sign")
+            nc.vector.tensor_scalar(out=doubled[:], in0=gains[:, :, LAST], scalar1=0.0, scalar2=2.0,
+                                    op0=ALU.is_ge, op1=ALU.mult)
+            nc.vector.tensor_scalar(out=below[:], in0=size[:, :, LAST], scalar1=low, scalar2=high,
                                     op0=ALU.min, op1=ALU.mult)
-            nc.gpsimd.tensor_scalar(out=factors[:, :, PACK:PACK + 1], in0=size[:, :, LAST:], scalar1=high, scalar2=low,
+            nc.vector.tensor_scalar(out=above[:], in0=size[:, :, LAST], scalar1=high, scalar2=low,
                                     op0=ALU.max, op1=ALU.mult)
-            nc.gpsimd.tensor_scalar(out=factors[:, :, PACK + 1:], in0=below[:], scalar1=low, scalar2=None, op0=ALU.max)
-            logs = keep.tile([P, GROUPS, PACK + 2], F32, name="logs")
+            nc.vector.tensor_scalar(out=factors[:, :, 0:PACK], in0=size[:], scalar1=low, scalar2=high,
+                                    op0=ALU.max, op1=ALU.min)
+            nc.vector.tensor_scalar(out=last_sign[:, :, 0], in0=doubled[:], scalar1=1.0, scalar2=None, op0=ALU.subtract)
+            nc.vector.scalar_tensor_tensor(out=factors[:, :, PACK], in0=below[:], scalar=low, in1=above[:],
+                                           op0=ALU.max, op1=ALU.mult)
+            turned_gains = keep.tile([P, GROUPS, LAST], F32, name="turned_gains")
+            nc.vector.tensor_tensor(out=turned_gains[:], in0=gains[:, :, 0:LAST],
+                                    in1=last_sign[:].to_broadcast([P, GROUPS, LAST]), op=ALU.mult)
+            logs = keep.tile([P, GROUPS, PACK + 1], F32, name="logs")
             nc.scalar.activation(out=logs[:], in_=factors[:], func=ACT.Ln)
             inverse = keep.tile([P, GROUPS, LAST], F32, name="inverse")
             nc.scalar.activation(out=inverse[:], in_=logs[:, :, 0:LAST], func=ACT.Exp, scale=-1.0)
-            rests = keep.tile([P, GROUPS, LAST], F32, name="rests")
-            nc.gpsimd.tensor_tensor(out=rests[:], in0=gains[:, :, 0:LAST], in1=inverse[:], op=ALU.mult)
             last_log = keep.tile([P, GROUPS, 1], F32, name="last_log")
-            nc.vector.tensor_reduce(out=last_log[:], in_=logs[:, :, LAST:], axis=mybir.AxisListType.X, op=ALU.add)
-            doubled = keep.tile([P, GROUPS, 1], F32, name="doubled")
-            nc.gpsimd.tensor_scalar(out=doubled[:], in0=gains[:, :, LAST:], scalar1=0.0, scalar2=2.0,
-                                    op0=ALU.is_ge, op1=ALU.mult)
-            last_sign = keep.tile([P, GROUPS, 1], F32, name="last_sign")
-            nc.gpsimd.tensor_scalar(out=last_sign[:], in0=doubled[:], scalar1=1.0, scalar2=None, op0=ALU.subtract)
+            for b in range(GROUPS):
+                nc.scalar.activation(out=last_log[:, b, :], in_=logs[:, b, LAST:PACK], func=ACT.Identity,
+                                     bias=logs[:, b, PACK:])
+            rests = keep.tile([P, GROUPS, LAST], F32, name="rests")
+            nc.gpsimd.tensor_tensor(out=rests[:], in0=turned_gains[:], in1=inverse[:], op=ALU.mult)
             nc.vector.tensor_copy(picked_scales[:], tab_scales[:].indirect(offsets[:]))
         for q in (0, 2, 1, 3):
             source = 32 + BLOCKS * q
@@ -223,7 +230,7 @@ def tile_list_redshift_gaussian_bumps_kernel(tc, tab, offs, w1, centre, gain, w2
 
         def sign(b, unit, t):
             nc.vector.tensor_scalar(out=signed[b, unit][:, t, :], in0=planes[b, unit][:, t, :],
-                                    scalar1=rests[:, b, t:t + 1], scalar2=last_sign[:, b, :], op0=ALU.mult, op1=ALU.mult)
+                                    scalar1=rests[:, b, t:t + 1], scalar2=None, op0=ALU.mult)
 
         def weave(b, unit, woven, c0, width):
             nc.vector.tensor_scalar(

@@ -29,6 +29,7 @@ GROUPS = H // PASS
 ALIGN = 64
 LAST = PACK - 1
 LN_RANGE = 64
+HALF = P // 2
 PIECE = 4 * PACK * PASS
 SLOT = 2 * PASS
 
@@ -65,7 +66,8 @@ def tile_list_redshift_gaussian_bumps_kernel(tc, tab, offs, w1, centre, gain, w2
         with tc.tile_pool(name="window", bufs=1) as window:
             tab_scales = window.tile([P, T], U8, name="tab_scales")
             rows = keep.tile([P, PASS], F32, name="rows")
-            nc.vector.memset(rows[:], 0.0)
+            for first in (0, HALF):
+                nc.vector.memset(rows[first:first + HALF - GROUPS, :], 0.0)
             for unused in (0, 96):
                 nc.vector.memset(tab_scales[unused:unused + 32, :].bitcast(I32), 0)
             nc.vector.memset(v_scales[:].rearrange("p a j -> p (a j)").bitcast(I32), 0)
@@ -75,8 +77,8 @@ def tile_list_redshift_gaussian_bumps_kernel(tc, tab, offs, w1, centre, gain, w2
                     out=tab_scales[32 + a:96:K_PASSES, :].bitcast(I32),
                     in_=tab[pair, PASS * T:].rearrange("(s g x) -> s g x", s=2, g=BLOCKS)[side].bitcast(I32))
             load_words(keep, 0)
-            nc.sync.dma_start(out=rows[0:GROUPS, :], in_=centre.rearrange("(b c) -> b c", b=GROUPS))
-            nc.sync.dma_start(out=rows[GROUPS:2 * GROUPS, :], in_=gain.rearrange("(b c) -> b c", b=GROUPS))
+            nc.sync.dma_start(out=rows[HALF - GROUPS:HALF, :], in_=centre.rearrange("(b c) -> b c", b=GROUPS))
+            nc.sync.dma_start(out=rows[P - GROUPS:, :], in_=gain.rearrange("(b c) -> b c", b=GROUPS))
             load_words(early, 1, 0)
             identity = keep.tile([P, P], F32, name="identity")
             make_identity(nc, identity[:])
@@ -84,8 +86,9 @@ def tile_list_redshift_gaussian_bumps_kernel(tc, tab, offs, w1, centre, gain, w2
             for t in range(PACK):
                 nc.tensor.transpose(turned[:, t * P:(t + 1) * P], rows[:, t::PACK], identity[:])
             consts = keep.tile([P, 2 * GROUPS, PACK], F32, name="consts")
-            nc.scalar.activation(out=consts[:], in_=turned[:].rearrange("p (t c) -> p c t", t=PACK)[:, 0:2 * GROUPS, :],
-                                 func=ACT.Copy)
+            nc.scalar.activation(
+                out=consts[:].rearrange("p (h b) t -> p h b t", h=2),
+                in_=turned[:].rearrange("p (t h c) -> p h c t", t=PACK, h=2)[:, :, HALF - GROUPS:, :], func=ACT.Copy)
             gains = consts[:, GROUPS:, :]
             size = keep.tile([P, GROUPS, PACK], F32, name="size")
             nc.scalar.activation(out=size[:], in_=gains, func=ACT.Abs)
@@ -348,11 +351,15 @@ def tile_list_redshift_gaussian_bumps_kernel(tc, tab, offs, w1, centre, gain, w2
             sign(0, 1, t)
         quantise_h(0, 0, BANK, slots(2, 4))
         woven0 = keep.tile([P, PACK * BANK], BF16, name="woven0", align_bytes=ALIGN)
-        for c0 in (0, CHUNK):
-            weave(0, 1, woven0[:], c0, CHUNK)
+        third = keep.tile([P, PACK, CHUNK], F32, name="sq_third")
+        distance = slots(2, 1).bitcast(F32)
+        weave(0, 1, woven0[:], 0, CHUNK)
+        nc.vector.tensor_scalar(out=distance, in0=banks[1, 1, 0][:, 0:CHUNK], scalar1=consts[:, 1, 0:1],
+                                scalar2=None, op0=ALU.subtract)
+        weave(0, 1, woven0[:], CHUNK, CHUNK)
+        nc.vector.tensor_tensor(out=third[:, 0, :], in0=distance, in1=distance, op=ALU.mult)
 
         fourth = late.tile([P, PACK, CHUNK], F32, name="sq_fourth", offset=2 * PIECE)
-        third = keep.tile([P, PACK, CHUNK], F32, name="sq_third")
         for unit in (1, 2):
             planes[1, unit] = keep.tile([P, LAST, CHUNK], BF16, name="planes1%d" % unit)
             signed[1, unit] = keep.tile([P, PACK, CHUNK], BF16, name="signed1%d" % unit)
@@ -364,8 +371,8 @@ def tile_list_redshift_gaussian_bumps_kernel(tc, tab, offs, w1, centre, gain, w2
         bell_plane(1, 0, LAST, plane_sq[LAST])
         steps = [(unit, t, sq[:, t, :]) for unit, sq in ((1, third), (2, fourth)) for t in range(PACK)]
         for i, (unit, t, sq) in enumerate(steps):
-            square(1, BANK + (unit - 1) * CHUNK, CHUNK, t, sq)
             if i > 0:
+                square(1, BANK + (unit - 1) * CHUNK, CHUNK, t, sq)
                 bell_plane(1, *steps[i - 1])
         for c0 in (0, P):
             bell_plane(1, 2, LAST, fourth[:, LAST, :], slice(c0, c0 + P))

@@ -241,6 +241,16 @@ def tile_list_redshift_gaussian_bumps_kernel(tc, tab, offs, w1, centre, gain, w2
                 in0=signed[b, unit][:, :, c0:c0 + width].rearrange("p t (c i) -> p c t i", i=PACK),
                 scalar1=last_sign[:, b, :], scalar2=None, op0=ALU.mult)
 
+        def bell_plain(sq, bell):
+            nc.scalar.activation(out=bell, in_=sq, func=ACT.Exp, scale=-1.0)
+
+        def weave_gain(b, bell, width, woven):
+            nc.vector.tensor_tensor(
+                out=woven.rearrange("p (c i t) -> p c t i", i=2, t=PACK),
+                in0=bell.rearrange("p t (c i) -> p c t i", i=2),
+                in1=consts[:, GROUPS + b, :].unsqueeze(1).unsqueeze(3).to_broadcast([P, width // 2, PACK, 2]),
+                op=ALU.mult)
+
         h_mx = {}
 
         def quantise_h(b, j0, width, woven):
@@ -352,30 +362,42 @@ def tile_list_redshift_gaussian_bumps_kernel(tc, tab, offs, w1, centre, gain, w2
         quantise_h(0, 0, BANK, slots(2, 4))
         woven0 = keep.tile([P, PACK * BANK], BF16, name="woven0", align_bytes=ALIGN)
         third = keep.tile([P, PACK, CHUNK], F32, name="sq_third")
-        distance = slots(2, 1).bitcast(F32)
+        distance = slots(2, 1).bitcast(F32)[:, 0:P]
         weave(0, 1, woven0[:], 0, CHUNK)
-        nc.vector.tensor_scalar(out=distance, in0=banks[1, 1, 0][:, 0:CHUNK], scalar1=consts[:, 1, 0:1],
+        nc.vector.tensor_scalar(out=distance, in0=banks[1, 1, 0][:, 0:P], scalar1=consts[:, 1, 0:1],
                                 scalar2=None, op0=ALU.subtract)
         weave(0, 1, woven0[:], CHUNK, CHUNK)
-        nc.vector.tensor_tensor(out=third[:, 0, :], in0=distance, in1=distance, op=ALU.mult)
+        nc.vector.tensor_tensor(out=third[:, 0, 0:P], in0=distance, in1=distance, op=ALU.mult)
 
         fourth = late.tile([P, PACK, CHUNK], F32, name="sq_fourth", offset=2 * PIECE)
-        for unit in (1, 2):
-            planes[1, unit] = keep.tile([P, LAST, CHUNK], BF16, name="planes1%d" % unit)
-            signed[1, unit] = keep.tile([P, PACK, CHUNK], BF16, name="signed1%d" % unit)
+        third_parts = ((0, P), (P, P // 2), (P + P // 2, P // 2))
+        bell_third = [keep.tile([P, PACK, width], F32, name="bell_third%d" % c0) for c0, width in third_parts]
+
+        def bell_third_part(i):
+            c0, width = third_parts[i]
+            bell_plain(third[:, :, c0:c0 + width], bell_third[i][:])
+
+        bell_seventh = keep.tile([P, 2, PACK, P // 2], F32, name="bell_seventh")
+        bell_eighth = keep.tile([P, 2, PACK, P // 2], F32, name="bell_eighth")
         for t in range(PACK):
             plane_sq[t] = plane_squares()
             square(1, 0, BANK, t, plane_sq[t])
             if t > 0:
                 bell_plane(1, 0, t - 1, plane_sq[t - 1])
-        bell_plane(1, 0, LAST, plane_sq[LAST])
-        steps = [(unit, t, sq[:, t, :]) for unit, sq in ((1, third), (2, fourth)) for t in range(PACK)]
-        for i, (unit, t, sq) in enumerate(steps):
-            if i > 0:
-                square(1, BANK + (unit - 1) * CHUNK, CHUNK, t, sq)
-                bell_plane(1, *steps[i - 1])
-        for c0 in (0, P):
-            bell_plane(1, 2, LAST, fourth[:, LAST, :], slice(c0, c0 + P))
+        bell_plane(1, 0, PACK - 1, plane_sq[PACK - 1])
+        square(1, BANK + P, P, 0, third[:, 0, P:])
+        for t in range(1, PACK):
+            square(1, BANK, CHUNK, t, third[:, t, :])
+        square(1, S - CHUNK, CHUNK, 0, fourth[:, 0, :])
+        bell_third_part(0)
+        bell_third_part(1)
+        for t in range(1, PACK):
+            square(1, S - CHUNK, CHUNK, t, fourth[:, t, :])
+        bell_third_part(2)
+        for i in range(2):
+            bell_plain(fourth[:, :, i * P // 2:(i + 1) * P // 2], bell_seventh[:, i])
+        for i in range(2):
+            bell_plain(fourth[:, :, P + i * P // 2:P + (i + 1) * P // 2], bell_eighth[:, i])
 
         woven1 = keep.tile([P, PACK * S], BF16, name="woven1", align_bytes=ALIGN)
 
@@ -390,17 +412,15 @@ def tile_list_redshift_gaussian_bumps_kernel(tc, tab, offs, w1, centre, gain, w2
             weave(1, 0, columns(0, BANK), c0, CHUNK)
         for j0 in (0, CHUNK):
             quantise_h(1, j0, CHUNK, columns(j0, CHUNK))
-        for t in range(LAST):
-            sign(1, 1, t)
-        weave(1, 1, columns(BANK, CHUNK), 0, CHUNK)
-        sign(1, 2, 0)
+        for i, (c0, width) in enumerate(third_parts):
+            weave_gain(1, bell_third[i][:], width, columns(BANK + c0, width))
+        weave_gain(1, bell_seventh[:, 0], P // 2, columns(S - CHUNK, P // 2))
         quantise_h(1, BANK, CHUNK, columns(BANK, CHUNK))
-        for t in range(1, LAST):
-            sign(1, 2, t)
-        for c0 in (0, P):
-            weave(1, 2, columns(S - CHUNK, CHUNK), c0, P)
-        for j0 in (S - CHUNK, S - P):
-            quantise_h(1, j0, P, columns(j0, P))
+        weave_gain(1, bell_seventh[:, 1], P // 2, columns(S - CHUNK + P // 2, P // 2))
+        for i in range(2):
+            weave_gain(1, bell_eighth[:, i], P // 2, columns(S - P + i * P // 2, P // 2))
+        quantise_h(1, S - CHUNK, P, columns(S - CHUNK, P))
+        quantise_h(1, S - P, P, columns(S - P, P))
 
         staged_rest = late.tile([P, 7 * CHUNK], F32, name="staged", offset=2 * PIECE)
         finish(0, CHUNK, True, [staged_rest[:, 0:CHUNK], staged_rest[:, CHUNK:2 * CHUNK]])

from contextlib import ExitStack

import concourse.mybir as mybir
from concourse.masks import make_identity

K, T, S, H, N = 2048, 4096, 1024, 1024, 256
FLOPS = 2 * K * H * S + 2 * H * N * S

F32 = mybir.dt.float32
BF16 = mybir.dt.bfloat16
I32 = mybir.dt.int32
U32 = mybir.dt.uint32
U16 = mybir.dt.uint16
U8 = mybir.dt.uint8
FP8X4 = mybir.dt.float8_e4m3fn_x4
FP4X4 = mybir.dt.float4_e2m1fn_x4
ACT = mybir.ActivationFunctionType
ALU = mybir.AluOpType

P = 128
PACK = 4
PASS = P * PACK
BANK = 512
CHUNK = 256
QUADRANTS = 4
BLOCKS = 16
K_PASSES = K // PASS
GROUPS = H // PASS
ALIGN = 64
LAST = PACK - 1
LN_RANGE = 64
HALF = P // 2
PIECE = 4 * PACK * PASS
SLOT = 2 * PASS


def tile_list_redshift_gaussian_bumps_kernel(tc, tab, offs, w1, centre, gain, w2_words, w2_scales, out):
    nc = tc.nc
    with ExitStack() as ctx:
        keep = ctx.enter_context(tc.tile_pool(name="keep", bufs=1))
        ring = ctx.enter_context(tc.tile_pool(name="ring", bufs=2))
        early = ctx.enter_context(tc.tile_pool(name="early", bufs=1))
        psum = ctx.enter_context(tc.psum_pool(name="psum", bufs=8))

        offsets = keep.tile([P, S // 16], U16, name="offsets")
        v_scales = keep.tile([P, K_PASSES, S], U8, name="v_scales", align_bytes=ALIGN)
        picked_scales = keep.tile([P, S], U8, name="picked_scales")
        tab_words = {}
        w1_raw = {}

        def load_w1(pool, b, a, offset=None, area=None):
            if area is None:
                area = pool.tile([P, PACK * PASS], F32, name="w1_raw%d%d" % (b, a), offset=offset)[:]
            w1_raw[b, a] = area.rearrange("p (j c) -> p j c", j=PACK)
            nc.sync.dma_start(
                out=w1_raw[b, a],
                in_=w1[a * PASS:(a + 1) * PASS, b * PASS:(b + 1) * PASS].rearrange("(p j) c -> p j c", j=PACK))

        def load_words(pool, pair, offset=None):
            tab_words[pair] = pool.tile([P, T], U32, name="tab_words%d" % pair, offset=offset)
            nc.sync.dma_start(
                out=tab_words[pair][:].bitcast(I32),
                in_=tab[pair, 0:PASS * T].rearrange("(p x) -> p x", p=P).bitcast(I32))

        nc.sync.dma_start(offsets[:], offs)
        with tc.tile_pool(name="window", bufs=1) as window:
            tab_scales = window.tile([P, T], U8, name="tab_scales")
            rows = keep.tile([P, PASS], F32, name="rows")
            for first in (0, HALF):
                nc.vector.memset(rows[first:first + HALF - GROUPS, :], 0.0)
            for unused in (0, 96):
                nc.vector.memset(tab_scales[unused:unused + 32, :].bitcast(I32), 0)
            nc.vector.memset(v_scales[:].rearrange("p a j -> p (a j)").bitcast(I32), 0)
            for a in range(K_PASSES):
                pair, side = divmod(a, 2)
                nc.sync.dma_start(
                    out=tab_scales[32 + a:96:K_PASSES, :].bitcast(I32),
                    in_=tab[pair, PASS * T:].rearrange("(s g x) -> s g x", s=2, g=BLOCKS)[side].bitcast(I32))
            load_words(keep, 0)
            nc.sync.dma_start(out=rows[HALF - GROUPS:HALF, :], in_=centre.rearrange("(b c) -> b c", b=GROUPS))
            nc.sync.dma_start(out=rows[P - GROUPS:, :], in_=gain.rearrange("(b c) -> b c", b=GROUPS))
            load_words(early, 1, 0)
            identity = keep.tile([P, P], F32, name="identity")
            make_identity(nc, identity[:])
            turned = psum.tile([P, BANK], F32, name="bank")
            for t in range(PACK):
                nc.tensor.transpose(turned[:, t * P:(t + 1) * P], rows[:, t::PACK], identity[:])
            consts = keep.tile([P, 2 * GROUPS, PACK], F32, name="consts")
            nc.scalar.activation(
                out=consts[:].rearrange("p (h b) t -> p h b t", h=2),
                in_=turned[:].rearrange("p (t h c) -> p h c t", t=PACK, h=2)[:, :, HALF - GROUPS:, :], func=ACT.Copy)
            gains = consts[:, GROUPS:, :]
            size = keep.tile([P, GROUPS, PACK], F32, name="size")
            nc.scalar.activation(out=size[:], in_=gains, func=ACT.Abs)
            factors = keep.tile([P, GROUPS, PACK + 1], F32, name="factors")
            low, high = 2.0 ** -LN_RANGE, 2.0 ** LN_RANGE
            below = keep.tile([P, GROUPS], F32, name="below")
            above = keep.tile([P, GROUPS], F32, name="above")
            doubled = keep.tile([P, GROUPS], F32, name="doubled")
            last_sign = keep.tile([P, GROUPS, 1], F32, name="last_sign")
            nc.vector.tensor_scalar(out=doubled[:], in0=gains[:, :, LAST], scalar1=0.0, scalar2=2.0,
                                    op0=ALU.is_ge, op1=ALU.mult)
            nc.vector.tensor_scalar(out=below[:], in0=size[:, :, LAST], scalar1=low, scalar2=high,
                                    op0=ALU.min, op1=ALU.mult)
            nc.vector.tensor_scalar(out=above[:], in0=size[:, :, LAST], scalar1=high, scalar2=low,
                                    op0=ALU.max, op1=ALU.mult)
            nc.vector.tensor_scalar(out=factors[:, :, 0:PACK], in0=size[:], scalar1=low, scalar2=high,
                                    op0=ALU.max, op1=ALU.min)
            nc.vector.tensor_scalar(out=last_sign[:, :, 0], in0=doubled[:], scalar1=1.0, scalar2=None, op0=ALU.subtract)
            nc.vector.scalar_tensor_tensor(out=factors[:, :, PACK], in0=below[:], scalar=low, in1=above[:],
                                           op0=ALU.max, op1=ALU.mult)
            turned_gains = keep.tile([P, GROUPS, LAST], F32, name="turned_gains")
            nc.vector.tensor_tensor(out=turned_gains[:], in0=gains[:, :, 0:LAST],
                                    in1=last_sign[:].to_broadcast([P, GROUPS, LAST]), op=ALU.mult)
            logs = keep.tile([P, GROUPS, PACK + 1], F32, name="logs")
            nc.scalar.activation(out=logs[:], in_=factors[:], func=ACT.Ln)
            inverse = keep.tile([P, GROUPS, LAST], F32, name="inverse")
            nc.scalar.activation(out=inverse[:], in_=logs[:, :, 0:LAST], func=ACT.Exp, scale=-1.0)
            last_log = keep.tile([P, GROUPS, 1], F32, name="last_log")
            for b in range(GROUPS):
                nc.scalar.activation(out=last_log[:, b, :], in_=logs[:, b, LAST:PACK], func=ACT.Identity,
                                     bias=logs[:, b, PACK:])
            rests = keep.tile([P, GROUPS, LAST], F32, name="rests")
            nc.gpsimd.tensor_tensor(out=rests[:], in0=turned_gains[:], in1=inverse[:], op=ALU.mult)
            nc.vector.tensor_copy(picked_scales[:], tab_scales[:].indirect(offsets[:]))
        for q in (0, 2, 1, 3):
            source = 32 + BLOCKS * q
            nc.sync.dma_start(out=v_scales[32 * q:32 * q + 4, :, :].bitcast(I32),
                              in_=picked_scales[source:source + BLOCKS, :].bitcast(I32))

        late = ctx.enter_context(tc.tile_pool(name="late", bufs=1))
        for a in range(K_PASSES):
            load_w1(late, 0, a, a * PIECE)
        border = PACK * PASS
        plane_words = BANK // 2
        starts = [a * border + (plane_words if a >= 2 else 0) for a in range(K_PASSES)]
        raw_words = starts[3] + 2 * border
        raw_end = late.tile([P, raw_words], F32, name="raw_end", offset=K_PASSES * PIECE)
        for a in range(K_PASSES):
            load_w1(late, 1, a, area=raw_end[:, starts[a]:starts[a] + border])
        w2_offset = K_PASSES * PIECE + 4 * raw_words
        w2w = late.tile([P, GROUPS, 2 * N], U8, name="w2w", align_bytes=ALIGN, offset=w2_offset)
        nc.sync.dma_start(out=w2w[:].bitcast(I32), in_=w2_words.rearrange("a p c -> p a c").bitcast(I32))
        w2s = late.tile([P, GROUPS, N], U8, name="w2s", align_bytes=ALIGN, offset=w2_offset + GROUPS * 2 * N)
        nc.vector.memset(w2s[:].rearrange("p a c -> p (a c)").bitcast(I32), 0)
        for q in range(QUADRANTS):
            nc.sync.dma_start(
                out=w2s[32 * q:32 * q + 4, :, :].bitcast(I32),
                in_=w2_scales[:, 4 * q:4 * q + 4, :].rearrange("a r c -> r a c").bitcast(I32))

        v_words = {}
        picked = keep.tile([P, S], U32, name="picked")
        nc.vector.tensor_copy(picked[:], tab_words[0][:].indirect(offsets[:]))
        parted = keep.tile([P, 2, S], U16, name="parted", align_bytes=ALIGN)
        nc.vector.tensor_copy(parted[:], picked[:].bitcast(U16).rearrange("p (j s) -> p s j", s=2))
        v_words[0], v_words[1] = parted[:, 0, :], parted[:, 1, :]
        nc.vector.tensor_copy(picked[:], tab_words[1][:].indirect(offsets[:]))

        def part_second(side, pool, offset=None):
            words = pool.tile([P, S], U16, name="parted%d" % side, align_bytes=ALIGN, offset=offset)
            nc.vector.tensor_copy(words[:], picked[:].bitcast(U16)[:, side::2])
            v_words[2 + side] = words[:]

        STAGE_SLOTS = 12
        stage = early.tile([P, STAGE_SLOTS * PASS], BF16, name="stage", align_bytes=ALIGN, offset=0)

        w1_grouped = {}
        w1_mx = {}

        def group_w1(b, a, t0, on_scalar, place, area=stage, outputs=slice(0, P)):
            both = area[:, place * PASS:(place + 2) * PASS]
            dst = both.rearrange("p (t m j) -> p m j t", t=2, j=PACK)[:, outputs]
            src = w1_raw[b, a].rearrange("p j (m t) -> p m j t", t=PACK)[:, outputs, :, t0:t0 + 2]
            if on_scalar:
                nc.scalar.activation(out=dst, in_=src, func=ACT.Copy)
            else:
                nc.vector.tensor_copy(out=dst, in_=src)
            w1_grouped[b, a, t0] = (area, place)
            w1_grouped[b, a, t0 + 1] = (area, place + 1)

        def quantise_w1(b, a, t0, count, codes=None):
            area, place = w1_grouped[b, a, t0]
            if codes is None:
                codes = keep.tile([P, count * P], U32, name="w1_codes%d%d%d" % (b, a, t0), align_bytes=ALIGN)[:]
            scales = keep.tile([P, count * P], U8, name="w1_scales%d%d%d" % (b, a, t0), align_bytes=ALIGN)
            nc.vector.quantize_mx(out=codes.bitcast(FP8X4), scales=scales[:],
                                  in_=area[:, place * PASS:(place + count) * PASS])
            for i in range(count):
                cols = slice(i * P, (i + 1) * P)
                w1_mx[b, a, t0 + i] = (codes[:, cols], scales[:, cols])

        banks = {}

        def project(b, half, order):
            cols = slice(half * BANK, (half + 1) * BANK)
            done = [0] * PACK
            for a, t in order:
                if done[t] == 0:
                    banks[b, half, t] = psum.tile([P, BANK], F32, name="bank")
                codes, scales = w1_mx[b, a, t]
                nc.tensor.matmul_mx(
                    out=banks[b, half, t][:],
                    lhsT=codes.bitcast(FP8X4), lhsT_scale=scales,
                    rhs=v_words[a][:, cols].bitcast(FP4X4), rhs_scale=v_scales[:, a, cols],
                    start=(done[t] == 0), stop=(done[t] == K_PASSES - 1))
                done[t] = done[t] + 1

        def as_loaded(passes):
            return [(a, t) for a in passes for t in range(PACK)]

        def by_tile(passes):
            return [(a, t) for t in range(PACK) for a in passes]

        def project_group(b):
            project(b, 0, as_loaded(range(K_PASSES)))
            project(b, 1, as_loaded([0]) + by_tile([3, 1, 2]))

        planes = {}

        def square(b, j0, width, t, sq):
            half, c0 = divmod(j0, BANK)
            nc.scalar.activation(out=sq, in_=banks[b, half, t][:, c0:c0 + width],
                                 func=ACT.Square, bias=consts[:, b, t:t + 1], scale=-1.0)

        def as_planes(area):
            return area.rearrange("p (t j) -> p t j", t=PACK)

        signed = {}

        def bell_plane(b, unit, t, sq, cols=slice(None)):
            target, bias = (signed, last_log[:, b, :]) if t == LAST else (planes, logs[:, b, t:t + 1])
            nc.scalar.activation(out=target[b, unit][:, t, cols], in_=sq[:, cols], func=ACT.Exp, scale=-1.0, bias=bias)

        def sign(b, unit, t):
            nc.vector.tensor_scalar(out=signed[b, unit][:, t, :], in0=planes[b, unit][:, t, :],
                                    scalar1=rests[:, b, t:t + 1], scalar2=None, op0=ALU.mult)

        def weave(b, unit, woven, c0, width):
            nc.vector.tensor_scalar(
                out=woven[:, PACK * c0:PACK * (c0 + width)].rearrange("p (c i t) -> p c t i", i=PACK, t=PACK),
                in0=signed[b, unit][:, :, c0:c0 + width].rearrange("p t (c i) -> p c t i", i=PACK),
                scalar1=last_sign[:, b, :], scalar2=None, op0=ALU.mult)

        def bell_plain(sq, bell):
            nc.scalar.activation(out=bell, in_=sq, func=ACT.Exp, scale=-1.0)

        def weave_gain(b, bell, width, woven):
            nc.vector.tensor_tensor(
                out=woven.rearrange("p (c i t) -> p c t i", i=2, t=PACK),
                in0=bell.rearrange("p t (c i) -> p c t i", i=2),
                in1=consts[:, GROUPS + b, :].unsqueeze(1).unsqueeze(3).to_broadcast([P, width // 2, PACK, 2]),
                op=ALU.mult)

        h_mx = {}

        def quantise_h(b, j0, width, woven):
            codes = keep.tile([P, width], U32, name="h_codes%d_%d" % (b, j0), align_bytes=ALIGN)
            scales = keep.tile([P, width], U8, name="h_scales%d_%d" % (b, j0), align_bytes=ALIGN)
            nc.vector.quantize_mx(out=codes[:].bitcast(FP8X4), scales=scales[:], in_=woven)
            for c in range(0, width, P):
                h_mx[b, j0 + c] = (codes, scales, c)

        out_rows = out.rearrange("(u p) j -> p u j", p=P)

        def finish(j0, width, on_scalar, staged):
            acc = psum.tile([P, BANK], F32, name="bank")
            for b in range(GROUPS):
                for u in range(N // P):
                    codes, scales, c = h_mx[b, j0]
                    nc.tensor.matmul_mx(
                        out=acc[:, u * width:(u + 1) * width],
                        lhsT=w2w[:, b, 2 * P * u:2 * P * (u + 1)].bitcast(FP4X4),
                        lhsT_scale=w2s[:, b, P * u:P * (u + 1)],
                        rhs=codes[:, c:c + width].bitcast(FP8X4), rhs_scale=scales[:, c:c + width],
                        start=(b == 0 and u == 0), stop=(b == GROUPS - 1 and u == N // P - 1))
            share = N // P // len(staged)
            for i, part in enumerate(staged):
                result = acc[:, i * share * width:(i + 1) * share * width]
                if on_scalar:
                    nc.scalar.copy(out=part, in_=result)
                else:
                    nc.vector.tensor_copy(out=part, in_=result)
                nc.sync.dma_start(out=out_rows[:, i * share:(i + 1) * share, j0:j0 + width],
                                  in_=part.rearrange("p (u j) -> p u j", u=share))

        opening_offset = (STAGE_SLOTS + 2) * SLOT
        opening = early.tile([P, 2 * PASS], BF16, name="opening", align_bytes=ALIGN, offset=opening_offset)
        group_w1(0, 0, 0, False, 0, opening)
        group_w1(0, 0, 2, True, 4)
        part_second(0, keep)
        quantise_w1(0, 0, 0, 2)
        quantise_w1(0, 0, 2, 2)
        part_second(1, early, opening_offset)
        for a, vector_place, scalar_place in ((1, 4, 0), (2, 0, 4)):
            group_w1(0, a, 0, False, vector_place)
            group_w1(0, a, 2, True, scalar_place)
            quantise_w1(0, a, 0, 2)
            quantise_w1(0, a, 2, 2)
        leading = early.tile([P, 2 * PASS], BF16, name="leading", align_bytes=ALIGN, offset=STAGE_SLOTS * SLOT)
        group_w1(0, 3, 0, False, 0, leading)
        group_w1(0, 3, 2, True, 0)
        quantise_w1(0, 3, 0, 1)
        quantise_w1(0, 3, 1, 1)
        second_codes = early.tile([P, 2 * P], U32, name="second_codes", align_bytes=ALIGN, offset=STAGE_SLOTS * SLOT)
        quantise_w1(0, 3, 2, 2, second_codes[:])
        project_group(0)
        for b, half in ((0, 0), (0, 1), (1, 0)):
            planes[b, half] = keep.tile([P, LAST, BANK], BF16, name="planes%d%d_wide" % (b, half))

        def laid(first, pitch):
            area = raw_end[:, first:first + PACK * pitch].bitcast(BF16)
            return as_planes(area)[:, :, 0:BANK]

        signed[0, 0] = laid(2 * border - LAST * plane_words, plane_words)
        signed[0, 1] = laid(starts[3] - border // 2, border // 2)
        signed[1, 0] = laid(starts[3] - border // 2, border // 2 + 96)

        def slots(place, count):
            return stage[:, place * PASS:(place + count) * PASS]

        def plane_squares():
            return ring.tile([P, BANK], F32, name="sq", bufs=3)[:]

        for a in range(2):
            group_w1(1, a, 0, False, 4)
            group_w1(1, a, 2, False, 0)
            quantise_w1(1, a, 0, 2)
            quantise_w1(1, a, 2, 2)

        sq_open = keep.tile([P, PACK, BANK], F32, name="sq_open")
        for t in range(PACK):
            square(0, 0, BANK, t, sq_open[:, t, :])
        bell_plane(0, 0, 0, sq_open[:, 0, :])
        bell_plane(0, 0, 1, sq_open[:, 1, :])
        plane_sq = {}
        between = ((0, 2), (1, 0), (0, LAST), (1, 1))
        for t, (half, plane) in enumerate(between):
            plane_sq[t] = plane_squares()
            square(0, BANK, BANK, t, plane_sq[t])
            bell_plane(0, half, plane, plane_sq[plane] if half else sq_open[:, plane, :])
        for t in range(2, PACK):
            bell_plane(0, 1, t, plane_sq[t])

        for t in range(3):
            sign(0, 0, t)
        group_w1(1, 2, 0, False, 0)
        group_w1(1, 2, 2, False, 3)
        quantise_w1(1, 2, 0, 2)
        quantise_w1(1, 2, 2, 2)
        sign(0, 1, 0)
        group_w1(1, 3, 0, False, 3)
        group_w1(1, 3, 2, False, 1, outputs=slice(0, P // 2))
        quantise_w1(1, 3, 0, 1)
        quantise_w1(1, 3, 1, 1)
        group_w1(1, 3, 2, True, 1, outputs=slice(P // 2, P))
        weave(0, 0, slots(2, 4), CHUNK, CHUNK)
        quantise_w1(1, 3, 2, 2)
        project_group(1)
        weave(0, 0, slots(2, 4), 0, CHUNK)
        for t in range(1, LAST):
            sign(0, 1, t)
        quantise_h(0, 0, BANK, slots(2, 4))
        woven0 = keep.tile([P, PACK * BANK], BF16, name="woven0", align_bytes=ALIGN)
        third = keep.tile([P, PACK, CHUNK], F32, name="sq_third")
        distance = slots(2, 1).bitcast(F32)[:, 0:P]
        weave(0, 1, woven0[:], 0, CHUNK)
        nc.vector.tensor_scalar(out=distance, in0=banks[1, 1, 0][:, 0:P], scalar1=consts[:, 1, 0:1],
                                scalar2=None, op0=ALU.subtract)
        weave(0, 1, woven0[:], CHUNK, CHUNK)
        nc.vector.tensor_tensor(out=third[:, 0, 0:P], in0=distance, in1=distance, op=ALU.mult)

        fourth = late.tile([P, PACK, CHUNK], F32, name="sq_fourth", offset=2 * PIECE)
        third_parts = ((0, P), (P, P // 2), (P + P // 2, P // 2))
        bell_third = [keep.tile([P, PACK, width], F32, name="bell_third%d" % c0) for c0, width in third_parts]

        def bell_third_part(i):
            c0, width = third_parts[i]
            bell_plain(third[:, :, c0:c0 + width], bell_third[i][:])

        bell_seventh = keep.tile([P, 2, PACK, P // 2], F32, name="bell_seventh")
        bell_eighth = keep.tile([P, 2, PACK, P // 2], F32, name="bell_eighth")
        for t in range(PACK):
            plane_sq[t] = plane_squares()
            square(1, 0, BANK, t, plane_sq[t])
            if t > 0:
                bell_plane(1, 0, t - 1, plane_sq[t - 1])
        bell_plane(1, 0, PACK - 1, plane_sq[PACK - 1])
        square(1, BANK + P, P, 0, third[:, 0, P:])
        for t in range(1, PACK):
            square(1, BANK, CHUNK, t, third[:, t, :])
        square(1, S - CHUNK, CHUNK, 0, fourth[:, 0, :])
        bell_third_part(0)
        bell_third_part(1)
        for t in range(1, PACK):
            square(1, S - CHUNK, CHUNK, t, fourth[:, t, :])
        bell_third_part(2)
        for i in range(2):
            bell_plain(fourth[:, :, i * P // 2:(i + 1) * P // 2], bell_seventh[:, i])
        for i in range(2):
            bell_plain(fourth[:, :, P + i * P // 2:P + (i + 1) * P // 2], bell_eighth[:, i])

        woven1 = keep.tile([P, PACK * S], BF16, name="woven1", align_bytes=ALIGN)

        def columns(j0, width):
            return woven1[:, PACK * j0:PACK * (j0 + width)]

        for c in range(BANK // CHUNK):
            for t in range(2 * c, min(2 * c + 2, LAST)):
                sign(1, 0, t)
            quantise_h(0, BANK + c * CHUNK, CHUNK, woven0[:, c * PACK * CHUNK:(c + 1) * PACK * CHUNK])
        for c0 in (0, CHUNK):
            weave(1, 0, columns(0, BANK), c0, CHUNK)
        for j0 in (0, CHUNK):
            quantise_h(1, j0, CHUNK, columns(j0, CHUNK))
        for i, (c0, width) in enumerate(third_parts):
            weave_gain(1, bell_third[i][:], width, columns(BANK + c0, width))
        weave_gain(1, bell_seventh[:, 0], P // 2, columns(S - CHUNK, P // 2))
        quantise_h(1, BANK, CHUNK, columns(BANK, CHUNK))
        weave_gain(1, bell_seventh[:, 1], P // 2, columns(S - CHUNK + P // 2, P // 2))
        for i in range(2):
            weave_gain(1, bell_eighth[:, i], P // 2, columns(S - P + i * P // 2, P // 2))
        quantise_h(1, S - CHUNK, P, columns(S - CHUNK, P))
        quantise_h(1, S - P, P, columns(S - P, P))

        staged_rest = late.tile([P, 7 * CHUNK], F32, name="staged", offset=2 * PIECE)
        finish(0, CHUNK, True, [staged_rest[:, 0:CHUNK], staged_rest[:, CHUNK:2 * CHUNK]])
        finish(CHUNK, CHUNK, True, [staged_rest[:, 2 * CHUNK:4 * CHUNK]])
        finish(BANK, CHUNK, True, [staged_rest[:, 4 * CHUNK:6 * CHUNK]])
        finish(S - CHUNK, P, True, [staged_rest[:, 6 * CHUNK:]])
        staged_last = keep.tile([P, CHUNK], F32, name="staged_last")
        finish(S - P, P, False, [staged_last[:]])
